import numpy as np, ml_dtypes
CORES = [40,41,42,43,44,45,46,47]
N = 8
BF = ml_dtypes.bfloat16
def gentries(a):
    return np.ascontiguousarray(a.reshape(8, 16, -1).transpose(0, 2, 1)).reshape(8, -1)
def gtable(e):
    e = np.asarray(e); return np.ascontiguousarray(e.reshape(8, -1, 16).transpose(0, 2, 1)).reshape(128, -1).astype(np.int32)
W, L, M, B, TS, CAP = 8192, 512, 2, 4, 4, 128
R = M * B
KAPPA = (3, 29)
def run(x, z, v):
    tr = []
    for b in range(B):
        u = np.add.reduce(z, axis=2)
        c = np.concatenate([((u * u >> 4) + k * u + v) & (W - 1) for k in KAPPA], axis=2)
        y = np.take_along_axis(x, c[:, :, None, :], 3).reshape(N, 8, 16, M, L)
        z = np.abs(np.maximum.reduce(y, axis=3) - z)
        tr.append(c)
    return z, np.concatenate(tr, axis=2)
def starts(z, h, fr):
    halt = (~fr) & (np.add.reduce((z >= h[..., None]).astype(np.int64), axis=2) >= 9)
    slot = np.add.accumulate(halt.astype(np.int64), axis=2) - halt
    return halt & (slot < CAP)
def parts(rng):
    return rng.integers(0, 256, (N, 8, 16, W)), rng.integers(0, 256, (N, 8, 16, L)), rng.integers(0, W, (N, 8, L))
def levels(rng, x, s, v, share):
    j = rng.integers(-24, 25, (N, 8, 16, TS)); z = run(x, s, v)[0]; th = np.zeros((N, 8, 16, TS), np.int64)
    for t in range(TS):
        k = np.sort(np.sort(z - j[..., t:t + 1], axis=2)[:, :, 7], axis=2)
        n = np.minimum(np.maximum((share[..., t] * L).astype(np.int64), 1), L)
        th[..., t] = np.take_along_axis(k, (L - n)[..., None], 2) + j[..., t]
    return np.minimum(np.maximum(th, 0), 255)
def pack(x, s, v, th):
    return {"x": x.reshape(N, 128, W).astype(np.float32).astype(BF), "sd": s.reshape(N, 128, L).astype(np.float32).astype(BF),
            "v0": np.stack([gtable(a) for a in v]), "th": np.ascontiguousarray(th.reshape(N, 128, TS)).astype(np.int32)}
def shares(rng):
    return rng.choice(np.array([0.1, 0.25, 0.4, 0.6]), (N, 8, TS))
def setup_inputs(rng):
    x, s, v = parts(rng)
    return pack(x, s, v, levels(rng, x, s, v, shares(rng)))
def setup_inputs_claims(rng):
    x, s, v = parts(rng); share = rng.choice(np.array([0.2, 0.35, 0.45]), (N, 8, TS)); th = levels(rng, x, s, v, share)
    z, c = run(x, s, v); go = starts(z, th[..., 0], np.zeros((N, 8, L), bool))
    for r in range(0, N, 2):
        for g in range(8):
            j = np.nonzero(go[r + 1, g])[0]
            if len(j) == 0: j = np.arange(L)
            e = rng.choice(np.array([0, R - 1, -1]), L); e = np.where(e < 0, rng.integers(0, R, L), e)
            v[r, g] = np.where(rng.random(L) < 0.6, c[r + 1, g, e * L + rng.choice(j, L)], v[r, g])
    th[0::2] = levels(rng, x, s, v, share)[0::2]
    th[1, :, :, 1] = 255; th[:, 5, :, 2] = 255; th[2, :, :, TS - 1] = 255
    return pack(x, s, v, th)
def setup_inputs_corners(rng):
    x, s, v = parts(rng); v = np.ascontiguousarray(np.argsort(rng.random((N, 8, W)), axis=-1)[..., :L])
    pm = np.ones((N, 8), bool); pm[2:, 6:] = False
    x = np.where(pm[:, :, None, None], 255, x)
    n = rng.choice(np.array([0, 1, CAP - 1, CAP, CAP + 1, L]), (N, 8)); n[0] = 0
    n[1] = np.array([CAP, CAP + 1, L, CAP, L, CAP + 1, CAP, L]); n[2] = np.array([CAP, CAP + 1, L, CAP - 1, 1, 0, CAP, CAP])
    hot = np.argsort(np.argsort(rng.random((N, 8, L)), axis=2), axis=2) < n[:, :, None]
    k = np.where(hot, np.where(rng.random((N, 8, L)) < 0.5, 9, rng.integers(9, 17, (N, 8, L))), np.where(rng.random((N, 8, L)) < 0.5, 8, rng.integers(0, 9, (N, 8, L))))
    up = np.argsort(np.argsort(rng.random((N, 8, 16, L)), axis=2), axis=2) < k[:, :, None, :]
    tb = rng.integers(1, 256, (N, 8, 16)); tb[:, 1] = 1; tb[:, 3] = 255; tb[:, 5] = rng.choice(np.array([1, 255]), (N, 16))
    b = tb[..., None]; near = rng.random(s.shape) < 0.5
    hi = np.where(near, b, b + ((256 - b) * rng.random(s.shape)).astype(np.int64)); lo = np.where(near, b - 1, (b * rng.random(s.shape)).astype(np.int64))
    s = np.where(pm[:, :, None, None], np.where(up, hi, lo), s)
    th = levels(rng, x, s, v, shares(rng)); th[..., 0] = np.where(pm[:, :, None], tb, th[..., 0])
    return pack(x, s, v, th)
def setup_inputs_ends(rng):
    x, s, v = parts(rng); one = 1.0
    for i in range(M.bit_length() - 1): one = one * 0.5
    a = rng.random((N, 8, 1, W)); x = np.where(a < 0.4 * one, 255, np.where(a < 1.2 * one, 255 * rng.integers(0, 2, x.shape), 0))
    a = rng.random((N, 8, 1, L)); s = np.where(a < 0.35, 255, np.where(a < 0.6, 0, 255 * rng.integers(0, 2, s.shape)))
    v = np.where(rng.random(v.shape) < 0.72, (W - 1) * rng.integers(0, 2, v.shape), v)
    x[:, 1::2, :, W - 1] = 255; x[:, 0::2, :, W - 1] = 0; x[:, :, :, 0] = 255 - x[:, :, :, W - 1]
    s[:, 1::2, :, L - 1] = 255; s[:, 0::2, :, L - 1] = 0; s[:, :, :, 0] = 255 - s[:, :, :, L - 1]; s[:, 1::2, :, 5] = 255; s[:, 1::2, :, L - 4] = 255
    v[:, :, L - 1] = W - 1; v[:, :, L - 4] = W - 1; v[:, :, 5] = W - 1; v[:, :, 0] = 0
    k = rng.choice(np.array([16, 16, 12, 10, 9, 8, 8, 7, 0]), (N, 8, 1, TS)); k[:, 7, :, 0] = 12; k[:, 6, :, 0] = 0; k[:, 0, :, TS - 1] = 9; k[:, 7, :, TS - 1] = 16
    th = np.where(np.argsort(np.argsort(rng.random((N, 8, 16, TS)), axis=2), axis=2) < k, 255, 0)
    return pack(x, s, v, th)
def setup_inputs_spread(rng):
    x, s, v = parts(rng)
    x = np.minimum((np.exp2(1 + 7 * rng.random((N, 8, 1, W))) * rng.random(x.shape)).astype(np.int64), 255)
    s = np.minimum((np.exp2(1 + 7 * rng.random((N, 8, 1, L))) * rng.random(s.shape)).astype(np.int64), 255)
    v = np.minimum((W * rng.random(v.shape) ** 3).astype(np.int64), W - 1)
    return pack(x, s, v, levels(rng, x, s, v, shares(rng)))
def setup_inputs_ties(rng):
    x, s, v = parts(rng); pool = rng.integers(0, W, (8, 12)); pool[:, 0] = 0; pool[:, 1] = W - 1; h = L // 2; q = L // 4
    v = np.stack([pool[g][rng.integers(0, 12, (N, L))] for g in range(8)], axis=1)
    s[..., h:] = s[..., :h]; v[..., h:] = np.where(rng.random((N, 8, h)) < 0.5, v[..., :h], v[..., h:])
    pl = [2, 4, 7]; x[:, 2] = 255; x[:, 4] = 0; x[:, 7] = 0
    s[:, pl] = rng.integers(0, 100, (N, 3, 16, L))
    for a in range(0, N, 2):
        b = a + 1
        k = int(rng.integers(1, 4)); p = int(v[b, 2, 0])
        s[b, 2, :, k * q:(k + 1) * q] = 255; v[b, 2, k * q:(k + 1) * q] = p
        s[a, 2, :, (k - 1) * q:k * q] = rng.integers(201, 256, (16, q))
        v[a, 2, (k - 1) * q:k * q] = np.where(rng.random(q) < 0.8, p, v[a, 2, (k - 1) * q:k * q]); v[a, 2, (k - 1) * q] = p
        ln = np.append(q + rng.permutation(3 * q - 1)[:3], L - 1); e = rng.integers(201, 252, 4); pv = 16 * rng.permutation(W // 16)[:4] + 1; u = 16 * e
        s[b, 4][:, ln] = e; v[b, 4][ln] = pv
        wr = rng.permutation(q)[:4 * M]; s[a, 4][:, wr] = rng.integers(201, 252, 4 * M); s[a, 4][5, wr] += 4
        v[a, 4][wr] = np.concatenate([((u * u >> 4) + m * u + pv) & (W - 1) for m in KAPPA])
        p = W - 2 if a == 0 else int(rng.integers(W // 2, W - 1))
        for l, c in ((0, p + 1), (h, p)):
            s[b, 7, :, l] = rng.integers(201, 256, 16); u = int(np.sum(s[b, 7, :, l])); v[b, 7, l] = (c - (u * u >> 4) - KAPPA[0] * u) & (W - 1)
        for l, c in ((3, p + 1), (L - 1, p)):
            s[a, 7, :, l] = rng.integers(201, 256, 16); v[a, 7, l] = c
    th = levels(rng, x, s, v, shares(rng)); th[..., 0][:, pl] = rng.integers(100, 201, (N, 3, 16))
    return pack(x, s, v, th)
def check_inputs(d):
    bad = []
    for k, lo, hi in (("x", 0, 255), ("sd", 0, 255), ("v0", 0, W - 1), ("th", 0, 255)):
        a = np.asarray(d[k]).astype(np.float64)
        if not (np.min(a) >= lo and np.max(a) <= hi): bad.append("range of " + k)
        elif np.any(np.floor(a) != a): bad.append("whole numbers in " + k)
    return bad
def reference(x, sd, v0, th):
    X = x.astype(np.float32).astype(np.int64).reshape(N, 8, 16, W); S = sd.astype(np.float32).astype(np.int64).reshape(N, 8, 16, L)
    H = th.astype(np.int64).reshape(N, 8, 16, TS); v = np.stack([gentries(a) for a in v0]).astype(np.int64)
    fr = np.zeros((N, 8, L), bool); tr = np.zeros((N, 8, R * L), np.int64); cl = np.arange(L) * 4 // L
    for t in range(TS):
        z, c = run(X, S, v)
        tr = np.where(np.tile(fr, (1, 1, R)), tr, c)
        go = starts(z, H[..., t], fr); fr = fr | go
        back = np.zeros((N, 8, L), bool); hurt = np.zeros((N, 8, L), bool); done = np.zeros((N, 1, 1), np.int64)
        for q in range(N):
            p = q ^ (1 + t % (N - 1))
            for g in range(8):
                ln = np.nonzero(go[p, g])[0]; w = v[p, g, ln]
                mark = np.full(W, 9); np.minimum.at(mark, tr[q, g], np.where(np.tile(fr[q, g], R), np.tile(cl, R), 9))
                ok = np.nonzero(mark[w] > cl[ln])[0]
                win = np.zeros(len(ln), bool); win[ok[np.unique(w[ok], return_index=True)[1]]] = True
                back[p, g, ln[~win]] = True; done[q, 0, 0] += np.count_nonzero(win)
                if t < TS - 1: X[q, g][:, w[win]] = z[p, g][:, ln[win]]
                hit = np.zeros(W, bool); hit[w[win]] = True
                hurt[q, g] = fr[q, g] & np.any(hit[tr[q, g]].reshape(R, L), axis=0)
        fr = fr & (~back) & (~hurt)
        v = np.where(fr, v, (((v & 4095) ** 2 >> 3) + 37 * v + done) & (W - 1))
    ys = np.concatenate([v, fr.astype(np.int64)], axis=2)
    return {"yt": np.stack([gtable(a) for a in tr]).astype(np.float32), "ys": np.stack([gtable(a) for a in ys]).astype(np.float32)}

@@ -1,0 +1,624 @@
+from concourse.mybir import AluOpType as ALU, AxisListType, ActivationFunctionType as AF
+
+W, L, TS = 8192, 512, 4
+KS = (3, 29)
+NM = 16384 + 256
+
+SCRATCH = {
+    "X": ("sbuf", [128, NM], "bfloat16"), "MAP": ("sbuf", [128, NM], "bfloat16"),
+    "SEL": ("sbuf", [128, 2048], "bfloat16"), "EI": ("sbuf", [128, 2048], "bfloat16"),
+    "SD": ("sbuf", [128, 512], "bfloat16"), "V0": ("sbuf", [128, 32], "int32"), "THI": ("sbuf", [128, 4], "int32"),
+    "KL": ("sbuf", [128, 512], "float32"), "KWS": ("sbuf", [128, 32], "float32"), "KWL": ("sbuf", [128, 32], "float32"),
+    "ZS": ("sbuf", [128, 384], "bfloat16"), "ZL": ("sbuf", [128, 384], "bfloat16"),
+    "NDS": ("sbuf", [128, 512], "bfloat16"), "NDL": ("sbuf", [128, 512], "bfloat16"),
+    "MVS": ("sbuf", [128, 512], "bfloat16"), "MVL": ("sbuf", [128, 512], "bfloat16"),
+    "G": ("sbuf", [128, 4096], "bfloat16"), "HG": ("sbuf", [128, 4096], "bfloat16"),
+    "LO": ("sbuf", [128, 4096], "bfloat16"), "HI": ("sbuf", [128, 2048], "bfloat16"),
+    "KX": ("sbuf", [128, 512], "float32"), "KEYR": ("sbuf", [128, 512], "float32"),
+    "YT": ("sbuf", [128, 256], "float32"), "YS": ("sbuf", [128, 64], "float32"),
+    "PF": ("sbuf", [128, 6000], "float32"), "PI": ("sbuf", [128, 3000], "int32"),
+    "PU": ("sbuf", [128, 1000], "uint16"), "PB": ("sbuf", [128, 12000], "bfloat16"),
+}
+for _t in range(TS): SCRATCH["KSD%d" % _t] = ("sbuf", [128, 1536], "float32")
+PSUM = ("U0", "D0", "D1", "D2", "TPA", "TPB", "HP", "BD")
+for _b in PSUM: SCRATCH[_b] = ("psum", [128, 512], "float32")
+QUEUES = ("pe", "dve", "act", "gp")
+SEMAPHORES = (["c_" + q for q in QUEUES] + ["ld_x", "ld_sd", "ld_v", "ld_th", "st_t", "st_s", "lsem"]
+              + ["%s%d" % (k, t) for k in ("rk", "rw", "rm", "rz", "rb") for t in range(TS)])
+
+CYC, PEC, HOP = 0.001, 0.00086, 0.16
+ORDER = {}
+CFG = {"map": ((1, 2), (1, 2, 4, 6), (2, 4, 5, 6, 8), (3, 5, 6, 7, 11, 13)),
+       "hg": ((0, 1, 2, 3), (2, 3, 4, 5), (0, 3, 8, 9, 11), (0, 3, 4, 7, 8, 11, 13, 14)),
+       "cut": ((0, 8), (8, 16), (16, 24), (24, 32)), "dcut": ((0, 16), (16, 24), (24, 32)),
+       "kw": 3, "kx": 8, "lg": 0, "span": [0.0]}
+
+
+def dv(n, c=1.0):
+    return max(64, n * c) * CYC
+
+
+def gat(n):
+    return 0.066 + 1.56 * n * CYC
+
+
+def sca(n):
+    return 0.06 + 3.8 * n * CYC
+
+
+def rank_program(g, core, T, topo):
+    rank = T.rank_of(core)
+    if rank is None:
+        return
+    ops = []
+    acc = {}
+    pool = {"PF": [0], "PI": [0], "PU": [0], "PB": [0]}
+
+    def op(eng, fn, reads, writes, dur, event=None, after=(), lat=0.0, early=False):
+        n = len(ops)
+        deps = {}
+
+        def need(m, wait):
+            deps[m] = deps.get(m, False) or wait
+        for (b, lo, hi) in reads:
+            ex = b in PSUM
+            for (l2, h2, m, wr) in acc.get(b, []):
+                over = l2 < hi and lo < h2
+                if over or ex:
+                    same = ops[m]["eng"] == eng
+                    if wr: need(m, over if same else True)
+                    elif ex: need(m, not same)
+        for (b, lo, hi) in writes:
+            ex = b in PSUM
+            for (l2, h2, m, wr) in acc.get(b, []):
+                if l2 < hi and lo < h2 or ex:
+                    need(m, ops[m]["eng"] != eng or eng in ("sp", "net") or not (wr or ex))
+        for m in after: need(m, False)
+        ops.append({"eng": eng, "fn": fn, "deps": deps, "dur": dur, "event": event, "lat": lat, "early": early})
+        for (b, lo, hi) in reads:
+            acc.setdefault(b, []).append((lo, hi, n, False))
+        for (b, lo, hi) in writes:
+            if b in PSUM: keep = [a for a in acc.get(b, []) if ops[a[2]]["eng"] == eng and a[3]][-40:]
+            else: keep = [a for a in acc.get(b, []) if not (lo <= a[0] and a[1] <= hi)]
+            acc[b] = keep + [(lo, hi, n, True)]
+        return n
+
+    def al(p, n):
+        a = pool[p][0]
+        pool[p][0] = a + (n + 15) // 16 * 16
+        assert pool[p][0] <= SCRATCH[p][1][1], p
+        return (p, a, a + n)
+
+    def two(p, n):
+        return (al(p, n), al(p, n))
+
+    def ap(r):
+        return T[r[0]][:, r[1]:r[2]] if len(r) == 3 else T[r[0]][:, r[1]:r[2]:r[3]]
+
+    def rg(r):
+        return (r[0], r[1], r[2])
+
+    def sub(r, lo, hi, st=None):
+        return (r[0], r[1] + lo, r[1] + hi) if st is None else (r[0], r[1] + lo, r[1] + hi, st)
+
+    def wd(r):
+        return r[2] - r[1] if len(r) == 3 else (r[2] - r[1] + r[3] - 1) // r[3]
+
+    def fastc(*rs):
+        return 0.5 if all(SCRATCH[r[0]][2] in ("bfloat16", "uint16") and r[0] not in PSUM for r in rs) else 1.0
+
+    def copy(o, i):
+        op("dve", lambda: g.vector.tensor_copy(out=ap(o), in_=ap(i)), [rg(i)], [rg(o)], dv(wd(o), fastc(o, i)))
+
+    def tt(o, a, b, f):
+        c = 1.0 if (a[0] in PSUM or b[0] in PSUM) else 2.0
+        op("dve", lambda: g.vector.tensor_tensor(out=ap(o), in0=ap(a), in1=ap(b), op=f), [rg(a), rg(b)], [rg(o)], dv(wd(o), c))
+
+    def ts(o, a, s1, f1, s2=None, f2=None):
+        rd = [rg(a)] + [rg(s) for s in (s1, s2) if isinstance(s, tuple)]
+
+        def fn():
+            x1 = ap(s1) if isinstance(s1, tuple) else s1
+            x2 = ap(s2) if isinstance(s2, tuple) else s2
+            if f2 is None:
+                return g.vector.tensor_scalar(out=ap(o), in0=ap(a), scalar1=x1, scalar2=None, op0=f1)
+            return g.vector.tensor_scalar(out=ap(o), in0=ap(a), scalar1=x1, scalar2=x2, op0=f1, op1=f2)
+        op("dve", fn, rd, [rg(o)], dv(wd(o), fastc(o, a)))
+
+    def fill(o, v):
+        op("dve", lambda: g.vector.memset(ap(o), v), [], [rg(o)], dv(wd(o), fastc(o)), early=128 < wd(o))
+
+    def red(o, a, f):
+        op("dve", lambda: g.vector.tensor_reduce(out=ap(o), in_=ap(a), axis=AxisListType.X, op=f), [rg(a)], [rg(o)], dv(wd(a)))
+
+    def ind(win, off):
+        return T[win[0]][:, win[1]:win[2]].indirect(ap(off))
+
+    def scatter(win, off, src):
+        op("dve", lambda: g.vector.tensor_copy(out=ind(win, off), in_=ap(src)), [rg(off), rg(src)], [rg(win)], sca(wd(src)))
+
+    def gather(eng, o, win, off):
+        if eng == "act": fn = lambda: g.scalar.activation(out=ap(o), in_=ind(win, off), func=AF.Copy)
+        else: fn = lambda: g.vector.tensor_copy(out=ap(o), in_=ind(win, off))
+        op(eng, fn, [rg(win), rg(off)], [rg(o)], gat(wd(o)))
+
+    def act(o, a, f, bias=None, scale=None, acc_o=None):
+        rd = [rg(a)] + [rg(r) for r in (bias, scale) if r is not None]
+
+        def fn():
+            kw = {}
+            if bias is not None: kw["bias"] = ap(bias)
+            if scale is not None: kw["scale"] = ap(scale)
+            if acc_o is not None: kw["accum_out"] = ap(acc_o)
+            return g.scalar.activation(out=ap(o), in_=ap(a), func=f, **kw)
+        op("act", fn, rd, [rg(o)] + ([rg(acc_o)] if acc_o is not None else []), dv(wd(o)) + (0.02 if acc_o is not None else 0.0))
+
+    def mm(lst, f32=False, p8=False):
+        rd, wr = [], []
+        d = 0.0
+        for (o, a, b, s0, s1) in lst:
+            for r in (a, b):
+                if rg(r) not in rd: rd.append(rg(r))
+            if rg(o) not in wr: wr.append(rg(o))
+            d += max(min(64, wd(a)), wd(b)) * PEC * (4 if f32 else 1)
+
+        def fn():
+            x = None
+            for (o, a, b, s0, s1) in lst:
+                x = g.tensor.matmul(T[o[0]][0:8, o[1]:o[2]] if p8 else ap(o), ap(a), ap(b), s0, s1)
+            return x
+        op("pe", fn, rd, wr, d)
+
+    def iota(o, pat, base, cm):
+        op("gp", lambda: g.iota(ap(o), pat, base, cm, allow_small_or_imprecise_dtypes=True), [], [rg(o)], 0.15 + 2 * wd(o) * CYC)
+
+    def asel(o, a, pat, cmp, base, cm):
+        op("gp", lambda: g.affine_select(ap(o), ap(a), pat, cmp, 0.0, base, cm), [rg(a)], [rg(o)], 0.2 + 2 * wd(o) * CYC)
+
+    used = [0]
+
+    def send(dst, o, i, sem, lat):
+        rid, pid, _ = topo.addr(dst)
+        en = topo.engines(core, dst)[::2]
+        m = sum(1 << e for e in en)
+        used[0] += len(en)
+
+        def fn():
+            g.remote_dma(ap(o), ap(i), T.sem[sem], T.sem.lsem, pid, rid, m)
+        s = op("gp", fn, [rg(i)], [], 0.1)
+        op("net", None, [], [rg(o)], 0.0, event=(sem, len(en)), after=(s,), lat=lat)
+
+    def dma(o_ap, i_ap, rd, wr, sem, lat, eng="sp"):
+        op(eng, lambda: (g.sync if eng == "sp" else g.scalar).dma_start(o_ap, i_ap).then_inc(T.sem[sem], 16), rd, wr, 0.1, event=(sem, 16), lat=lat)
+
+    V0, THI, SD, XW = ("V0", 0, 32), ("THI", 0, 4), ("SD", 0, 512), ("X", 0, W)
+    dma(T.V0[:], T.v0[:], [], [V0], "ld_v", 2.0, "act")
+    dma(T.THI[:], T.th[:], [], [THI], "ld_th", 3.0, "act")
+    dma(T.SD[:], T.sd[:], [], [SD], "ld_sd", 2.5)
+    dma(T.X[:, 0:W], T.x[:], [], [XW], "ld_x", 10.0)
+
+    ONE, BO, t0, ID = al("PB", 128), al("PB", 128), al("PB", 128), al("PB", 128)
+    fill(ONE, 1.0)
+    asel(t0, ONE, [[-16, 8], [0, 16]], ALU.is_ge, 0, 1)
+    asel(BO, t0, [[16, 8], [0, 16]], ALU.is_ge, 15, -1)
+    asel(ID, ONE, [[-1, 128]], ALU.is_equal, 0, 1)
+    fill(("SEL", 0, 2048), 0.0)
+    for i in range(16): copy(("SEL", i * 128 + i, (i + 1) * 128, 16), sub(BO, i, 128, 16))
+
+    def sel(i):
+        return ("SEL", i * 128, (i + 1) * 128)
+    NID, NID16 = al("PB", 128), al("PB", 128)
+    ts(NID, ID, -1.0, ALU.mult)
+    ts(NID16, ID, -16.0, ALU.mult)
+    BIAS = (al("PF", 1), al("PF", 1))
+    for m in range(2): fill(BIAS[m], 8.0 * KS[m])
+    h1, h2, M16 = al("PF", 64), al("PF", 32), al("PF", 16)
+    tt(h1, sub(ID, 0, 64), sub(ID, 64, 128), ALU.add)
+    tt(h2, sub(h1, 0, 32), sub(h1, 32, 64), ALU.add)
+    tt(M16, sub(h2, 0, 16), sub(h2, 16, 32), ALU.add)
+
+    def m16(i):
+        return sub(M16, i, i + 1)
+    i16, x16, IC = al("PF", 16), al("PF", 16), al("PF", 1)
+    iota(i16, [[1, 16]], 0, 0)
+    tt(x16, M16, i16, ALU.mult)
+    red(IC, x16, ALU.add)
+    INI, iq, LANE, TL, P16N = al("PF", 1), al("PF", 32), al("PF", 32), al("PF", 32), al("PF", 32)
+    ts(INI, IC, 512.0 - 16.0, ALU.add)
+    iota(iq, [[16, 32]], 0, 0)
+    ts(LANE, iq, IC, ALU.add)
+    ts(TL, LANE, 512.0, ALU.add)
+    fill(P16N, 16.0)
+    V16 = al("PF", 64)
+
+    def v16ops(dst, src):
+        for m in range(2): ts(sub(dst, m * 32, m * 32 + 32), src, 16.0, ALU.mult, -64.0 * KS[m] ** 2, ALU.add)
+    v16ops(V16, V0)
+
+    def sums(zr, extra=None):
+        o = ("U0", 0, 32)
+        lst = [(o, NID16, extra, True, False)] if extra is not None else []
+        for i in range(16): lst.append((o, sel(i), sub(zr, i, 512, 16), extra is None and i == 0, i == 15))
+        mm(lst)
+        return o
+    SQ0 = al("PF", 64)
+    o = sums(SD)
+    for m in range(2): act(sub(SQ0, m * 32, m * 32 + 32), o, AF.Square, BIAS[m])
+
+    MAP, MAPW = ("MAP", 0, NM), ("MAP", 0, W)
+    fill(MAPW, 0.0)
+    TH = al("PF", 4)
+    copy(TH, THI)
+    NEG = al("PF", 1)
+    fill(NEG, -1.0)
+    TRI, nbo, BOF = al("PB", 128), al("PB", 128), al("PF", 128)
+    ts(nbo, BO, -1.0, ALU.mult)
+    asel(TRI, nbo, [[-1, 128]], ALU.is_ge, 0, 1)
+    copy(BOF, BO)
+    for i in range(16): ts(("EI", i * 128, i * 128 + 128), BO, m16(i), ALU.mult)
+    RHE, RK = al("PB", 64), al("PB", 24)
+    for k in range(8): ts(sub(RHE, k * 8, k * 8 + 8), sub(BO, 0, 128, 16), m16(0), ALU.mult)
+    for k in range(3): ts(sub(RK, k, 24, 3), sub(BO, 0, 128, 16), m16(k), ALU.mult)
+    ex0, EXP, KT = al("PB", 128), al("PB", 128), al("PB", 512)
+    asel(ex0, ONE, [[1, 128]], ALU.is_ge, 0, -16)
+    asel(EXP, ex0, [[-1, 128]], ALU.is_ge, 15, 16)
+    DM, dm1, dm2 = al("PF", 128), al("PF", 16), al("PF", 16)
+    ts(dm1, M16, 33554432.0, ALU.mult, -17.0, ALU.add)
+    ts(sub(dm2, 1, 16), sub(M16, 0, 15), -1.0, ALU.mult)
+    ts(sub(dm2, 0, 1), m16(15), -1.0, ALU.mult)
+    for k in range(8): tt(sub(DM, k * 16, k * 16 + 16), dm1, dm2, ALU.add)
+    pc, c8, c9, g8, g9, dl = (al("PF", 1) for _ in range(6))
+    DL = al("PU", 1)
+    iota(pc, [[0, 1]], 0, 1)
+    tt(g8, pc, IC, ALU.subtract)
+    ts(c8, IC, 7.5, ALU.is_ge, -8.0, ALU.mult)
+    tt(c9, c8, IC, ALU.add)
+    ts(g9, g8, 0.5, ALU.mult)
+    tt(dl, g9, c9, ALU.add)
+    copy(DL, dl)
+    i8, TRW, SROW = al("PF", 8), al("PF", 8), al("PF", 128)
+    iota(i8, [[16, 8]], 2 * W + 128, 0)
+    ts(TRW, i8, IC, ALU.add)
+    iota(SROW, [[1024, 128]], W * 1024 + 896, 0)
+    for t in range(TS): copy(("KSD%d" % t, 0, 128), SROW)
+    hir, lor, hm2, lm2, SC = al("PF", 128), al("PF", 128), al("PF", 128), al("PF", 128), al("PB", 128)
+    iota(hir, [[1, 8], [0, 16]], 1, 0)
+    iota(lor, [[0, 8], [1, 16]], 1, 0)
+    ts(hm2, hir, m16(0), ALU.mult)
+    ts(lm2, lor, m16(1), ALU.mult)
+    tt(SC, hm2, lm2, ALU.add)
+    KRP, P16, N16, ZERO = al("PB", 512), al("PB", 128), al("PB", 128), al("PB", 128)
+    fill(KRP, 0.0)
+    fill(P16, 16.0)
+    fill(N16, -16.0)
+    fill(ZERO, 0.0)
+
+    SQ, SI, C16, Y1, HB = two("PF", 64), two("PI", 64), two("PU", 64), two("PB", 512), two("PB", 512)
+    ZH, ZF, GE = al("PB", 1536), al("PB", 512), al("PB", 512)
+    CN, TM = two("PI", 256), two("PF", 256)
+    tda, tdb = al("PF", 256), al("PF", 256)
+    OFF, CLX = al("PU", 256), al("PF", 256)
+    ZG, SQS, VSE, SIS, CS, VSW = al("PB", 512), al("PF", 64), al("PF", 64), al("PI", 64), al("PI", 64), al("PI", 8)
+    KSI, KSC, CLB, MK = al("PI", 128), al("PI", 128), al("PB", 128), al("PB", 128)
+    LRF, lr1, lr2, lr3, LRU = two("PF", 32), al("PF", 32), al("PF", 32), al("PF", 32), two("PU", 32)
+    KB, LG, WO = al("PB", 256), al("PB", 512), two("PF", 32)
+    HALT, GO, FRA, FR = al("PB", 32), al("PB", 32), al("PB", 32), two("PB", 32)
+    scn, HT, wy, SOFF = al("PF", 32), al("PF", 32), al("PF", 32), al("PU", 32)
+    vm, vq, vs, v37, vsum, vbp = (al("PI", 32) for _ in range(6))
+    SV0, SIN = al("PF", 64), al("PI", 64)
+    VB16, VBL, VN, VNs, VC = al("PF", 64), al("PF", 32), two("PI", 32), al("PI", 32), two("PF", 32)
+    vd, vd2, KW, kw1 = al("PF", 32), al("PF", 32), al("PF", 32), al("PF", 32)
+    KJ, KM, MN, UQ = al("PF", 128), al("PF", 128), al("PF", 8), al("PF", 16)
+    fill(UQ, 0.0)
+    AB = [al("PF", 16 * q + 16) for q in range(8)]
+    KI, VW, VT = al("PI", 8), al("PI", 8), al("PF", 8)
+    mt, mo, to1, to2 = al("PF", 8), al("PF", 8), al("PF", 16), al("PF", 8)
+    MOFF, TOFF = two("PU", 8), two("PU", 8)
+    MG = al("PB", 128)
+    ZI, ZJ, ZO, DNR = al("PI", 8), al("PI", 8), al("PU", 8), al("PB", 128)
+    HS, LS = two("PB", 128), two("PB", 128)
+    HPS, DNB, SENT, A16 = al("PF", 64), al("PB", 16), al("PB", 8), al("PF", 1)
+
+    def vbase(src):
+        copy(vs, src)
+        ts(vm, vs, 4095, ALU.bitwise_and)
+        tt(vq, vm, vm, ALU.mult)
+        ts(vsum, vq, 3, ALU.arith_shift_right)
+        ts(v37, vs, 37.0, ALU.mult)
+        tt(vsum, vsum, v37, ALU.add)
+        ts(vbp, vsum, 8191, ALU.bitwise_and)
+        ts(VBL, vbp, 16.0, ALU.mult)
+        v16ops(VB16, vbp)
+        tt(SV0, SQ0, VB16, ALU.add)
+
+    def keys(v):
+        ts(kw1, v, 1024.0, ALU.mult)
+        tt(KW, kw1, LANE, ALU.add)
+        for i in range(16):
+            if i < CFG["kx"]: act(("KX", i, 512, 16), KW, AF.Copy, scale=m16(i))
+            else: ts(("KX", i, 512, 16), KW, m16(i), ALU.mult)
+        for k in range(4): mm([(("TPA", k * 128, k * 128 + 128), BOF, ("KX", k * 128, k * 128 + 128), True, True)], f32=True)
+        act(("KEYR", 0, 512), ("TPA", 0, 512), AF.Copy)
+
+    copy(VC[0], V0)
+    keys(V0)
+    vbase(VC[0])
+
+    for t in range(TS):
+        pr, nx, last = t % 2, (t + 1) % 2, t == TS - 1
+        partner = T.cores[rank ^ (1 + t % 7)]
+        cn, fr, vc = CN[pr], FR[pr], VC[pr]
+        zc = SD
+        for b in range(4):
+            p = b % 2
+            if b == 0: sq = SQ0
+            else:
+                sq = SQ[p]
+                o = sums(zc)
+                for m in (1, 0): act(sub(sq, m * 32, m * 32 + 32), o, AF.Square, BIAS[m])
+            c16 = C16[p]
+            for m in (1, 0):
+                k0, k1 = m * 32, m * 32 + 32
+                if b or not t: tt(sub(SI[p], k0, k1), sub(sq, k0, k1), sub(V16, k0, k1), ALU.add)
+                c = sub(cn, b * 64 + k0, b * 64 + k1)
+                ts(c, sub(SI[p] if b or not t else SIN, k0, k1), 4, ALU.arith_shift_right, 8191, ALU.bitwise_and)
+                copy(sub(c16, k0, k1), c)
+            zn = sub(ZH, b * 512, b * 512 + 512) if b < 3 else ZF
+            for c0, c1 in CFG["cut"]:
+                yy, hu = sub(Y1[p], c0 * 16, c1 * 16), sub(HB[p], c0 * 16, c1 * 16)
+                gather("act", yy, XW, sub(c16, 32 + c0, 32 + c1))
+                o16 = sub(c16, c0, c1)
+                op("dve", lambda o16=o16, yy=yy, hu=hu: g.vector.tensor_tensor(out=ap(hu), in0=ind(XW, o16), in1=ap(yy), op=ALU.max),
+                   [XW, o16, yy], [hu], gat(c1 * 16 - c0 * 16))
+            for h, (c0, c1) in enumerate(CFG["dcut"]):
+                r0, r1 = c0 * 16, c1 * 16
+                dps = ("D%d" % h, 0, r1 - r0)
+                mm([(dps, NID, sub(zc, r0, r1), True, False)])
+                mm([(dps, ID, sub(HB[p], r0, r1), False, True)])
+                act(sub(zn, r0, r1), dps, AF.Abs)
+            zc = zn
+        if t:
+            mm([(("TPB", k * 32, k * 32 + 32), ID, fr, True, True) for k in range(8)])
+            tt(tda, TM[nx] if t > 1 else CN[0], cn, ALU.subtract)
+            tt(tdb, ("TPB", 0, 256), tda, ALU.mult)
+            tt(("YT", 0, 256) if last else TM[pr], tdb, cn, ALU.add)
+        for c0, c1 in CFG["dcut"]: ts(sub(GE, c0 * 16, c1 * 16), sub(zc, c0 * 16, c1 * 16), sub(TH, t, t + 1), ALU.is_ge)
+        o = sums(GE, fr if t else None)
+        ts(HALT, o, 8.5, ALU.is_ge)
+        p2, p12 = ("HP", 0, 32), ("HP", 32, 64)
+        mm([(p2, BO, HALT, True, True), (p12, TRI, HALT, True, True)])
+        tt(HT, HALT, TL, ALU.mult)
+        op("dve", lambda p2=p2: g.vector.tensor_tensor_scan(out=ap(scn), data0=ap(P16N), data1=ap(p2), initial=ap(INI), op0=ALU.add, op1=ALU.add),
+           [P16N, p2, INI], [scn], dv(32))
+        tt(wy, p12, HT, ALU.subtract)
+        tt(WO[pr], wy, scn, ALU.add)
+        copy(SOFF, WO[pr])
+        scatter(("KSD%d" % t, 0, 1536), SOFF, ("KEYR", 0, 512))
+        ks = ("KSD%d" % t, 0, 128)
+        send(partner, ("KL", t * 128, t * 128 + 128), ks, "rk%d" % t, 2.4)
+        kws = ("KWS", t * 8, t * 8 + 8)
+        tt(KM, ks, DM, ALU.min)
+        for q in range(8):
+            if q < CFG["kw"]: act(sub(KJ, q * 16, q * 16 + 16), sub(KM, q * 16, q * 16 + 16), AF.Copy, acc_o=sub(kws, q, q + 1))
+            else: red(sub(kws, q, q + 1), sub(KM, q * 16, q * 16 + 16), ALU.add)
+        send(partner, ("KWL", t * 8, t * 8 + 8), kws, "rw%d" % t, 1.8)
+        copy(KSI, ks)
+        ts(KSC, KSI, 7, ALU.arith_shift_right, 7, ALU.bitwise_and)
+        mvs = ("MVS", t * 128, t * 128 + 128)
+        ts(MG, KSC, 1.0, ALU.add, m16(2), ALU.mult)
+        tt(mvs, MG, SC, ALU.add)
+        send(partner, ("MVL", t * 128, t * 128 + 128), mvs, "rm%d" % t, 2.2)
+        ts(GO, WO[pr], 127.5, ALU.is_lt)
+        if t:
+            tt(FRA, fr, GO, ALU.add)
+            tt(lr1, WO[pr], LRF[nx], ALU.subtract)
+            ts(lr2, lr1, 128.0 * t, ALU.add)
+            tt(lr3, lr2, GO, ALU.mult)
+            tt(LRF[pr], LRF[nx], lr3, ALU.add)
+        else:
+            copy(FRA, GO)
+            tt(LRF[pr], WO[pr], GO, ALU.mult)
+        copy(LRU[pr], LRF[pr])
+        ts(ZI, kws, 256.0, ALU.add)
+        ts(ZJ, ZI, 511, ALU.bitwise_and)
+        copy(ZO, ZJ)
+        for b in range(4):
+            gather("act", sub(ZG, b * 128, b * 128 + 128), SD if b == 0 else sub(ZH, b * 512 - 512, b * 512), ZO)
+        us = ("BD", 0, 32)
+        mm([(us, sel(i), sub(ZG, i, 512, 16), i == 0, i == 15) for i in range(16)])
+        for m in range(2): act(sub(SQS, m * 32, m * 32 + 32), us, AF.Square, BIAS[m])
+        ts(VSW, ZI, 10, ALU.arith_shift_right, 8191, ALU.bitwise_and)
+        ts(sub(VSE, 0, 8), VSW, 16.0, ALU.mult, -64.0 * KS[0] ** 2, ALU.add)
+        copy(sub(VSE, 8, 16), sub(VSE, 0, 8))
+        copy(sub(VSE, 16, 32), sub(VSE, 0, 16))
+        ts(sub(VSE, 32, 64), sub(VSE, 0, 32), 64.0 * (KS[0] ** 2 - KS[1] ** 2), ALU.add)
+        tt(SIS, SQS, VSE, ALU.add)
+        ts(CS, SIS, 4, ALU.arith_shift_right, 8191, ALU.bitwise_and)
+        copy(sub(OFF, t * 64, t * 64 + 64), CS)
+        ts(CLB, KSC, 1.0, ALU.add)
+        mm([(("BD", 64, 128), CLB, RHE, True, True)])
+        copy(sub(CLX, t * 64, t * 64 + 64), ("BD", 64, 128))
+        if not last:
+            gather("act", ("ZS", t * 128, t * 128 + 128), ZF, ZO)
+            send(partner, ("ZL", t * 128, t * 128 + 128), ("ZS", t * 128, t * 128 + 128), "rz%d" % t, 2.2)
+        kl, kwl = ("KL", t * 128, t * 128 + 128), ("KWL", t * 8, t * 8 + 8)
+        for q in range(8): act(AB[q], sub(kl, 0, 16 * q + 16), AF.Abs, sub(kwl, q, q + 1), NEG)
+        ts(KI, kwl, 256.0, ALU.add)
+        ts(VW, KI, 10, ALU.arith_shift_right)
+        tt(VT, VW, TRW, ALU.subtract)
+        ts(SENT, kwl, float(W * 1024), ALU.is_ge)
+        for q in range(8): red(sub(MN, q, q + 1), AB[q], ALU.min)
+        uq = sub(UQ, 0, 8)
+        ts(uq, MN, 255.5, ALU.is_ge)
+        tt(mt, uq, VT, ALU.mult)
+        tt(mo, mt, TRW, ALU.add)
+        copy(MOFF[pr], mo)
+        scatter(MAP, MOFF[pr], ("MVL", t * 128, t * 128 + 128))
+        tiles = 8 * (t + 1)
+        for k in range((t + 2) // 2):
+            bank = ("TPA", "TPB")[k]
+            nt = min(16, tiles - 16 * k)
+            for j in range(nt // 2):
+                jj = k * 8 + j
+                gather("dve" if jj in CFG["map"][t] else "act", ("G", jj * 256, jj * 256 + 256), MAPW, sub(OFF, jj * 16, jj * 16 + 16))
+                mm([((bank, (2 * j + w) * 24, (2 * j + w) * 24 + 24), ("G", jj * 256 + w * 128, jj * 256 + w * 128 + 128), RK, True, True) for w in range(2)])
+            nc = nt * 8
+            hs, ls, mk = sub(HS[k], 0, nc), sub(LS[k], 0, nc), sub(MK, 0, nc)
+            copy(ls, (bank, 1, nt * 24, 3))
+            tt(mk, (bank, 2, nt * 24, 3), sub(CLX, k * 128, k * 128 + nc), ALU.is_ge)
+            for d in range(16):
+                ts(("LO", k * 2048 + d, k * 2048 + nc * 16, 16), ls, float(d + 1), ALU.is_equal)
+            tt(hs, (bank, 0, nt * 24, 3), mk, ALU.mult)
+            for d in range(8):
+                ts(("HI", k * 1024 + d, k * 1024 + nc * 8, 8), hs, float(d + 1), ALU.is_equal)
+            mm([(("HP", 0, 64), ("LO", k * 2048 + u * 128, k * 2048 + u * 128 + 128), ("HI", k * 1024 + u * 64, k * 1024 + u * 64 + 64),
+                 k == 0 and u == 0, 16 * k + u == tiles - 1) for u in range(nt)])
+        copy(HPS, ("HP", 0, 64))
+        op("dve", lambda: g.vector.tensor_tensor(out=ap(DNB), in0=ind(HPS, DL), in1=ap(UQ), op=ALU.is_lt), [HPS, DL, UQ], [DNB], gat(16))
+        aps = ("HP", 0, 8)
+        mm([(aps, N16, SENT, True, False), (aps, P16, sub(DNB, 0, 8), False, True)])
+        red(A16, aps, ALU.add)
+        if not last:
+            for m in (1, 0): ts(sub(SIN, m * 32, m * 32 + 32), sub(SV0, m * 32, m * 32 + 32), A16, ALU.add)
+            ts(V16, VB16, A16, ALU.add)
+        op("dve", lambda: g.vector.tensor_scalar(out=ap(to1), in0=ind(HPS, DL), scalar1=0.5, scalar2=float(W + 128), op0=ALU.is_ge, op1=ALU.mult),
+           [HPS, DL], [to1], gat(16))
+        tt(to2, sub(to1, 0, 8), mo, ALU.add)
+        copy(TOFF[pr], to2)
+        if not last: scatter(("X", 0, NM), TOFF[pr], ("ZL", t * 128, t * 128 + 128))
+        mm([(("BD", i, 128, 16), ("EI", i * 128, i * 128 + 128), sub(DNB, 0, 8), True, True) for i in range(16)])
+        copy(DNR, ("BD", 0, 128))
+        nds = ("NDS", t * 128, t * 128 + 128)
+        ts(nds, ("BD", 0, 128), -1.0, ALU.mult, 1.0, ALU.add)
+        scatter(MAP, MOFF[pr], DNR)
+        ndl = ("NDL", t * 128, t * 128 + 128)
+        send(partner, ndl, nds, "rb%d" % t, 2.0)
+        vn = VN[pr]
+        ts(VNs, VBL, A16, ALU.add)
+        ts(vn, VNs, 4, ALU.arith_shift_right, 8191, ALU.bitwise_and)
+        if not last: keys(vn)
+        krep = []
+        for b in range(t + 1):
+            for j in range(b * 4, b * 4 + 4):
+                gather("dve" if j in CFG["hg"][t] else "act", ("HG", j * 256, j * 256 + 256), MAPW, sub(OFF, j * 16, j * 16 + 16))
+            tl = [("HG", b * 1024 + k * 128, b * 1024 + k * 128 + 128) for k in range(8)] + ([ndl] if b == t else [])
+            kp, kb = ("BD", b * 64, b * 64 + 64), sub(KB, b * 64, b * 64 + 64)
+            mm([(kp, x, RHE, n == 0, n == len(tl) - 1) for n, x in enumerate(tl)])
+            ts(kb, kp, 0.5, ALU.is_gt, 8.0, ALU.mult)
+            if not last: tt(sub(CLX, b * 64, b * 64 + 64), sub(CLX, b * 64, b * 64 + 64), kb, ALU.max)
+            krep.append((("D0" if last and b > 1 else "TPB", b * 128, b * 128 + 128), sub(kb, 0, 8), ID, True, True))
+        if not last: scatter(MAP, MOFF[pr], ZERO)
+        mm(krep, p8=True)
+        e = 128 * t + 128
+        f = e // 2 if last else e
+        op("act", lambda f=f: g.scalar.activation(out=T.PB[0:8, KT[1]:KT[1] + f], in_=T.TPB[0:8, 0:f], func=AF.Copy), [("TPB", 0, f)], [sub(KT, 0, f)], dv(f))
+        if last:
+            op("dve", lambda f=f, e=e: g.vector.tensor_copy(out=T.PB[0:8, KT[1] + f:KT[1] + e], in_=T.D0[0:8, f:e]), [("D0", f, e)], [sub(KT, f, e)], dv(e - f))
+        for bank, lo, hi in ((("TPB", 0, f), ("D0", f, e)) if last else (("TPB", 0, e),)):
+            op("pe", lambda bank=bank, lo=lo, hi=hi: g.tensor.matmul(T[bank][:, lo:hi], T.PB[0:8, EXP[1]:EXP[2]], T.PB[0:8, KT[1] + lo:KT[1] + hi], True, True),
+               [EXP, sub(KT, lo, hi)], [(bank, lo, hi)], (hi - lo) * PEC)
+        act(sub(KRP, 0, f), ("TPB", 0, f), AF.Copy)
+        if last: copy(sub(KRP, f, e), ("D0", f, e))
+        for h in range(2): gather("dve" if CFG["lg"] == h else "act", sub(LG, h * 256, h * 256 + 256), KRP, sub(LRU[pr], h * 16, h * 16 + 16))
+        bw = ("BD", 384, 416)
+        mm([(bw, sel(i), sub(LG, i, 512, 16), i == 0, i == 15) for i in range(16)])
+        frn = FR[nx]
+        tt(frn, FRA, bw, ALU.is_gt)
+        vcn = ("YS", 0, 32) if last else VC[nx]
+        tt(vd, vc, vn, ALU.subtract)
+        tt(vd2, vd, frn, ALU.mult)
+        tt(vcn, vd2, vn, ALU.add)
+        if not last: vbase(vcn)
+
+    dma(T.yt[:], T.YT[:], [("YT", 0, 256)], [], "st_t", 2.0)
+    copy(("YS", 32, 64), FR[TS % 2])
+    dma(T.ys[:], T.YS[:], [("YS", 0, 64)], [], "st_s", 2.0)
+
+    n = len(ops)
+    if n not in ORDER:
+        users = [[] for _ in range(n)]
+        for i, o in enumerate(ops):
+            for d in o["deps"]: users[d].append(i)
+        pri = [0.0] * n
+        for i in range(n - 1, -1, -1):
+            best = 0.0
+            for u in users[i]: best = max(best, pri[u] + (HOP if ops[u]["deps"][i] else 0.0))
+            pri[i] = best + ops[i]["dur"] + ops[i]["lat"]
+            if ops[i]["early"]: pri[i] = 400.0 + pri[i] * 0.01
+        busy = {}
+        start = [0.0] * n
+        left = [len(o["deps"]) for o in ops]
+        ready = [i for i in range(n) if left[i] == 0]
+        while ready:
+            i = max(ready, key=lambda j: (pri[j], -j))
+            ready.remove(i)
+            o = ops[i]
+            at = 0.0
+            for d, w in o["deps"].items():
+                e = start[d] + ops[d]["dur"]
+                at = max(at, e + ops[d]["lat"] + HOP if w else e)
+            if o["eng"] != "net":
+                sl = busy.setdefault(o["eng"], [])
+                k = len(sl)
+                while k > 0 and sl[k - 1][1] > at: k -= 1
+                while k < len(sl) and sl[k][0] < at + o["dur"] - 1e-9:
+                    at = max(at, sl[k][1])
+                    k += 1
+                sl.insert(k, (at, at + o["dur"]))
+            start[i] = at
+            CFG["span"][0] = max(CFG["span"][0], at + o["dur"] + o["lat"])
+            for u in users[i]:
+                left[u] -= 1
+                if left[u] == 0: ready.append(u)
+        ORDER[n] = sorted(range(n), key=lambda i: (start[i], i))
+    order = ORDER[n]
+
+    pos, cnt = {}, {}
+    for i in order:
+        q = ops[i]["eng"]
+        cnt[q] = cnt.get(q, 0) + 1
+        pos[i] = cnt[q]
+    known, vcs, waits, needed, final = {}, {}, {}, set(), {}
+    for i in order:
+        o = ops[i]
+        q = o["eng"]
+        final[q] = i
+        if q == "net":
+            vcs[i] = {("ev", i): 1}
+            continue
+        kn = known.setdefault(q, {})
+        mine = []
+        for d in sorted((d for d, w in o["deps"].items() if w), key=lambda d: -pos[d]):
+            key, val = (("ev", d), 1) if ops[d]["event"] else (ops[d]["eng"], pos[d])
+            if kn.get(key, 0) >= val: continue
+            mine.append(d)
+            needed.add(d)
+            for k2, x2 in vcs[d].items():
+                if kn.get(k2, 0) < x2: kn[k2] = x2
+        waits[i] = mine
+        v = dict(kn)
+        v[("ev", i) if o["event"] else q] = 1 if o["event"] else pos[i]
+        vcs[i] = v
+    for q in ("pe", "dve", "act"): needed.add(final[q])
+
+    eng = {"pe": g.tensor, "dve": g.vector, "act": g.scalar, "gp": g, "sp": g.sync}
+    num, tot = {}, {}
+    for i in order:
+        q = ops[i]["eng"]
+        if i in needed and not ops[i]["event"]:
+            tot[q] = tot.get(q, 0) + 1
+            num[i] = tot[q]
+    for i in order:
+        o = ops[i]
+        q = o["eng"]
+        if q == "net": continue
+        best = {}
+        for d in waits[i]:
+            s, v = ops[d]["event"] if ops[d]["event"] else ("c_" + ops[d]["eng"], num[d])
+            best[s] = max(best.get(s, 0), v)
+        for s in best: eng[q].wait_ge(T.sem[s], best[s])
+        x = o["fn"]()
+        if i in num: x.then_inc(T.sem["c_" + q], 1)
+    for q in tot: g.sync.wait_ge(T.sem["c_" + q], tot[q])
+    g.sync.wait_ge(T.sem.lsem, used[0])
+    for s in ("st_t", "st_s"): g.sync.wait_ge(T.sem[s], 16)

@@ -1,87 +1,94 @@
+import numpy as np
 from concourse.mybir import AluOpType as ALU, AxisListType, ActivationFunctionType as AF
 
 W, L, TS = 8192, 512, 4
 KS = (3, 29)
-NM = 16384 + 256
+NMAP = 8464
+NX = W + NMAP
+KB, KK = 65536.0, 16777216.0
 
 SCRATCH = {
-    "X": ("sbuf", [128, NM], "bfloat16"), "MAP": ("sbuf", [128, NM], "bfloat16"),
+    "X": ("sbuf", [128, NX], "bfloat16"), "MAP": ("sbuf", [128, NMAP], "bfloat16"),
     "SEL": ("sbuf", [128, 2048], "bfloat16"), "EI": ("sbuf", [128, 2048], "bfloat16"),
-    "SD": ("sbuf", [128, 512], "bfloat16"), "V0": ("sbuf", [128, 32], "int32"), "THI": ("sbuf", [128, 4], "int32"),
-    "KL": ("sbuf", [128, 512], "float32"), "KWS": ("sbuf", [128, 32], "float32"), "KWL": ("sbuf", [128, 32], "float32"),
+    "SD": ("sbuf", [128, 1024], "bfloat16"), "V0": ("sbuf", [128, 32], "int32"), "THI": ("sbuf", [128, 4], "int32"),
     "ZS": ("sbuf", [128, 384], "bfloat16"), "ZL": ("sbuf", [128, 384], "bfloat16"),
-    "NDS": ("sbuf", [128, 512], "bfloat16"), "NDL": ("sbuf", [128, 512], "bfloat16"),
+    "NDS": ("sbuf", [128, 32], "bfloat16"), "NDL": ("sbuf", [128, 32], "bfloat16"),
     "MVS": ("sbuf", [128, 512], "bfloat16"), "MVL": ("sbuf", [128, 512], "bfloat16"),
-    "G": ("sbuf", [128, 4096], "bfloat16"), "HG": ("sbuf", [128, 4096], "bfloat16"),
-    "LO": ("sbuf", [128, 4096], "bfloat16"), "HI": ("sbuf", [128, 2048], "bfloat16"),
-    "KX": ("sbuf", [128, 512], "float32"), "KEYR": ("sbuf", [128, 512], "float32"),
+    "MOS": ("sbuf", [128, 32], "uint16"), "MOL": ("sbuf", [128, 32], "uint16"),
+    "G": ("sbuf", [128, 4096], "bfloat16"), "LO": ("sbuf", [128, 4096], "bfloat16"), "HI": ("sbuf", [128, 2048], "bfloat16"),
+    "KEYR": ("sbuf", [128, 512], "float32"),
     "YT": ("sbuf", [128, 256], "float32"), "YS": ("sbuf", [128, 64], "float32"),
     "PF": ("sbuf", [128, 6000], "float32"), "PI": ("sbuf", [128, 3000], "int32"),
-    "PU": ("sbuf", [128, 1000], "uint16"), "PB": ("sbuf", [128, 12000], "bfloat16"),
+    "PU": ("sbuf", [128, 1000], "uint16"), "PB": ("sbuf", [128, 14000], "bfloat16"),
 }
 for _t in range(TS): SCRATCH["KSD%d" % _t] = ("sbuf", [128, 1536], "float32")
-PSUM = ("U0", "D0", "D1", "D2", "TPA", "TPB", "HP", "BD")
-for _b in PSUM: SCRATCH[_b] = ("psum", [128, 512], "float32")
+PSUM = ("P0", "Q0", "P1", "Q1", "HP", "BD", "TA", "TB")
+for _b in PSUM[:6]: SCRATCH[_b] = ("psum", [128, 512], "float32")
+for _b in PSUM[6:]: SCRATCH[_b] = ("psum", [128, 1024], "bfloat16")
 QUEUES = ("pe", "dve", "act", "gp")
 SEMAPHORES = (["c_" + q for q in QUEUES] + ["ld_x", "ld_sd", "ld_v", "ld_th", "st_t", "st_s", "lsem"]
-              + ["%s%d" % (k, t) for k in ("rk", "rw", "rm", "rz", "rb") for t in range(TS)])
+              + ["%s%d" % (k, t) for k in ("ro", "rm", "rz", "rb") for t in range(TS)])
 
-CYC, PEC, HOP = 0.001, 0.00086, 0.16
-ORDER = {}
-CFG = {"map": ((1, 2), (1, 2, 4, 6), (2, 4, 5, 6, 8), (3, 5, 6, 7, 11, 13)),
-       "hg": ((0, 1, 2, 3), (2, 3, 4, 5), (0, 3, 8, 9, 11), (0, 3, 4, 7, 8, 11, 13, 14)),
-       "cut": ((0, 8), (8, 16), (16, 24), (24, 32)), "dcut": ((0, 16), (16, 24), (24, 32)),
-       "kw": 3, "kx": 8, "lg": 0, "span": [0.0]}
+CYC, PEC, HOP = 0.00095, 0.00055, 0.14
+PLAN = {}
+CFG = {"cut": ((0, 8), (8, 16)), "batch": ((8,), (16,), (16, 8), (16, 16)), "ldx": 12.0, "net": 2.4, "span": [],
+       "banks": ("TA", "TB"), "turn": 2, "passes": 2, "r1": 100, "r2": 30, "shake": 0.3}
 
 
 def dv(n, c=1.0):
     return max(64, n * c) * CYC
 
 
-def gat(n):
-    return 0.066 + 1.56 * n * CYC
+def gat(n, eng="dve"):
+    return (0.05 if eng == "dve" else 0.065) + 1.56 * n * CYC
 
 
 def sca(n):
-    return 0.06 + 3.8 * n * CYC
+    return 0.05 + 3.8 * n * CYC
 
 
-def rank_program(g, core, T, topo):
-    rank = T.rank_of(core)
-    if rank is None:
-        return
+def build(g, core, rank, T, topo, choice):
     ops = []
     acc = {}
     pool = {"PF": [0], "PI": [0], "PU": [0], "PB": [0]}
 
-    def op(eng, fn, reads, writes, dur, event=None, after=(), lat=0.0, early=False):
+    def op(eng, fn, reads, writes, dur, event=None, after=(), lat=0.0, alts=None):
         n = len(ops)
         deps = {}
 
         def need(m, wait):
             deps[m] = deps.get(m, False) or wait
-        for (b, lo, hi) in reads:
-            ex = b in PSUM
-            for (l2, h2, m, wr) in acc.get(b, []):
-                over = l2 < hi and lo < h2
-                if over or ex:
-                    same = ops[m]["eng"] == eng
-                    if wr: need(m, over if same else True)
-                    elif ex: need(m, not same)
-        for (b, lo, hi) in writes:
-            ex = b in PSUM
-            for (l2, h2, m, wr) in acc.get(b, []):
-                if l2 < hi and lo < h2 or ex:
-                    need(m, ops[m]["eng"] != eng or eng in ("sp", "net") or not (wr or ex))
+        reads, writes = [rg(r) for r in reads], [rg(r) for r in writes]
+        for r in reads:
+            ex = r[0] in PSUM
+            for (r2, m, wr) in acc.get(r[0], []):
+                if ex: need(m, ops[m]["eng"] != eng)
+                elif wr and meet(r, r2): need(m, True)
+        for r in writes:
+            ex = r[0] in PSUM
+            for (r2, m, wr) in acc.get(r[0], []):
+                if ex: need(m, ops[m]["eng"] != eng)
+                elif meet(r, r2): need(m, True)
         for m in after: need(m, False)
-        ops.append({"eng": eng, "fn": fn, "deps": deps, "dur": dur, "event": event, "lat": lat, "early": early})
-        for (b, lo, hi) in reads:
-            acc.setdefault(b, []).append((lo, hi, n, False))
-        for (b, lo, hi) in writes:
-            if b in PSUM: keep = [a for a in acc.get(b, []) if ops[a[2]]["eng"] == eng and a[3]][-40:]
-            else: keep = [a for a in acc.get(b, []) if not (lo <= a[0] and a[1] <= hi)]
-            acc[b] = keep + [(lo, hi, n, True)]
+        ops.append({"eng": eng, "fn": fn, "deps": deps, "dur": dur, "event": event, "lat": lat, "alts": alts})
+        for r in reads:
+            acc.setdefault(r[0], []).append((r, n, False))
+        for r in writes:
+            if r[0] in PSUM: keep = []
+            else: keep = [a for a in acc.get(r[0], []) if not (a[0] == r or r[3] == 1 and r[1] <= a[0][1] and a[0][2] <= r[2])]
+            acc[r[0]] = keep + [(r, n, True)]
         return n
+
+    def meet(a, b):
+        if a[1] >= b[2] or b[1] >= a[2]: return False
+        if a[3] == b[3]: return (a[1] - b[1]) % a[3] == 0
+        if a[3] < b[3]: a, b = b, a
+        return any(b[1] <= x < b[2] and (x - b[1]) % b[3] == 0 for x in range(a[1], a[2], a[3]))
+
+    def either(alts, reads, writes):
+        n = len(ops)
+        if n in choice: return op(choice[n], alts[choice[n]][0], reads, writes, alts[choice[n]][1])
+        return op("open%d" % n, None, reads, writes, min(a[1] for a in alts.values()), alts={e: alts[e][1] for e in alts})
 
     def al(p, n):
         a = pool[p][0]
@@ -96,7 +103,7 @@ def rank_program(g, core, T, topo):
         return T[r[0]][:, r[1]:r[2]] if len(r) == 3 else T[r[0]][:, r[1]:r[2]:r[3]]
 
     def rg(r):
-        return (r[0], r[1], r[2])
+        return r if len(r) == 4 else (r[0], r[1], r[2], 1)
 
     def sub(r, lo, hi, st=None):
         return (r[0], r[1] + lo, r[1] + hi) if st is None else (r[0], r[1] + lo, r[1] + hi, st)
@@ -105,7 +112,7 @@ def rank_program(g, core, T, topo):
         return r[2] - r[1] if len(r) == 3 else (r[2] - r[1] + r[3] - 1) // r[3]
 
     def fastc(*rs):
-        return 0.5 if all(SCRATCH[r[0]][2] in ("bfloat16", "uint16") and r[0] not in PSUM for r in rs) else 1.0
+        return 0.5 if all(SCRATCH[r[0]][2] in ("bfloat16", "uint16") for r in rs) else 1.0
 
     def copy(o, i):
         op("dve", lambda: g.vector.tensor_copy(out=ap(o), in_=ap(i)), [rg(i)], [rg(o)], dv(wd(o), fastc(o, i)))
@@ -114,22 +121,24 @@ def rank_program(g, core, T, topo):
         c = 1.0 if (a[0] in PSUM or b[0] in PSUM) else 2.0
         op("dve", lambda: g.vector.tensor_tensor(out=ap(o), in0=ap(a), in1=ap(b), op=f), [rg(a), rg(b)], [rg(o)], dv(wd(o), c))
 
-    def ts(o, a, s1, f1, s2=None, f2=None):
-        rd = [rg(a)] + [rg(s) for s in (s1, s2) if isinstance(s, tuple)]
-
+    def ts_call(o, a, s1, f1, s2=None, f2=None):
         def fn():
             x1 = ap(s1) if isinstance(s1, tuple) else s1
             x2 = ap(s2) if isinstance(s2, tuple) else s2
             if f2 is None:
                 return g.vector.tensor_scalar(out=ap(o), in0=ap(a), scalar1=x1, scalar2=None, op0=f1)
             return g.vector.tensor_scalar(out=ap(o), in0=ap(a), scalar1=x1, scalar2=x2, op0=f1, op1=f2)
-        op("dve", fn, rd, [rg(o)], dv(wd(o), fastc(o, a)))
+        return fn
+
+    def ts(o, a, s1, f1, s2=None, f2=None):
+        rd = [rg(a)] + [rg(s) for s in (s1, s2) if isinstance(s, tuple)]
+        op("dve", ts_call(o, a, s1, f1, s2, f2), rd, [rg(o)], dv(wd(o), fastc(o, a)))
 
     def fill(o, v):
-        op("dve", lambda: g.vector.memset(ap(o), v), [], [rg(o)], dv(wd(o), fastc(o)), early=128 < wd(o))
+        op("dve", lambda: g.vector.memset(ap(o), v), [], [rg(o)], dv(wd(o), fastc(o)))
 
-    def red(o, a, f):
-        op("dve", lambda: g.vector.tensor_reduce(out=ap(o), in_=ap(a), axis=AxisListType.X, op=f), [rg(a)], [rg(o)], dv(wd(a)))
+    def red(o, a, f, neg=False):
+        op("dve", lambda: g.vector.tensor_reduce(out=ap(o), in_=ap(a), axis=AxisListType.X, op=f, negate=neg), [rg(a)], [rg(o)], dv(wd(a)))
 
     def ind(win, off):
         return T[win[0]][:, win[1]:win[2]].indirect(ap(off))
@@ -138,22 +147,32 @@ def rank_program(g, core, T, topo):
         op("dve", lambda: g.vector.tensor_copy(out=ind(win, off), in_=ap(src)), [rg(off), rg(src)], [rg(win)], sca(wd(src)))
 
     def gather(eng, o, win, off):
-        if eng == "act": fn = lambda: g.scalar.activation(out=ap(o), in_=ind(win, off), func=AF.Copy)
-        else: fn = lambda: g.vector.tensor_copy(out=ap(o), in_=ind(win, off))
-        op(eng, fn, [rg(win), rg(off)], [rg(o)], gat(wd(o)))
+        alts = {"act": (lambda: g.scalar.activation(out=ap(o), in_=ind(win, off), func=AF.Copy), gat(wd(o), "act")),
+                "dve": (lambda: g.vector.tensor_copy(out=ap(o), in_=ind(win, off)), gat(wd(o)))}
+        if eng: op(eng, alts[eng][0], [rg(win), rg(off)], [rg(o)], alts[eng][1])
+        else: either(alts, [rg(win), rg(off)], [rg(o)])
 
-    def act(o, a, f, bias=None, scale=None, acc_o=None):
-        rd = [rg(a)] + [rg(r) for r in (bias, scale) if r is not None]
-
+    def act_call(o, a, f, bias=None, scale=None, acc_o=None):
         def fn():
             kw = {}
             if bias is not None: kw["bias"] = ap(bias)
-            if scale is not None: kw["scale"] = ap(scale)
+            if scale is not None: kw["scale"] = ap(scale) if isinstance(scale, tuple) else scale
             if acc_o is not None: kw["accum_out"] = ap(acc_o)
             return g.scalar.activation(out=ap(o), in_=ap(a), func=f, **kw)
-        op("act", fn, rd, [rg(o)] + ([rg(acc_o)] if acc_o is not None else []), dv(wd(o)) + (0.02 if acc_o is not None else 0.0))
+        return fn
 
-    def mm(lst, f32=False, p8=False):
+    def act(o, a, f, bias=None, scale=None, acc_o=None):
+        rd = [rg(a)] + [rg(r) for r in (bias, scale) if isinstance(r, tuple)]
+        op("act", act_call(o, a, f, bias, scale, acc_o), rd, [rg(o)] + ([rg(acc_o)] if acc_o is not None else []),
+           dv(wd(o)) + (0.02 if acc_o is not None else 0.0))
+
+    def move(o, a, relu=False, scale=None):
+        if relu: d, s = ts_call(o, a, 0.0, ALU.max), act_call(o, a, AF.Relu)
+        elif scale: d, s = ts_call(o, a, scale, ALU.mult), act_call(o, a, AF.Copy, scale=scale)
+        else: d, s = (lambda: g.vector.tensor_copy(out=ap(o), in_=ap(a))), act_call(o, a, AF.Copy)
+        either({"dve": (d, dv(wd(o), fastc(o, a))), "act": (s, dv(wd(o)))}, [rg(a)], [rg(o)])
+
+    def mm(lst, f32=False):
         rd, wr = [], []
         d = 0.0
         for (o, a, b, s0, s1) in lst:
@@ -164,10 +183,12 @@ def rank_program(g, core, T, topo):
 
         def fn():
             x = None
-            for (o, a, b, s0, s1) in lst:
-                x = g.tensor.matmul(T[o[0]][0:8, o[1]:o[2]] if p8 else ap(o), ap(a), ap(b), s0, s1)
+            for (o, a, b, s0, s1) in lst: x = g.tensor.matmul(ap(o), ap(a), ap(b), s0, s1)
             return x
         op("pe", fn, rd, wr, d)
+
+    def mms(lst, k):
+        for j in range(0, len(lst), k): mm(lst[j:j + k])
 
     def iota(o, pat, base, cm):
         op("gp", lambda: g.iota(ap(o), pat, base, cm, allow_small_or_imprecise_dtypes=True), [], [rg(o)], 0.15 + 2 * wd(o) * CYC)
@@ -177,7 +198,7 @@ def rank_program(g, core, T, topo):
 
     used = [0]
 
-    def send(dst, o, i, sem, lat):
+    def send(dst, o, i, sem):
         rid, pid, _ = topo.addr(dst)
         en = topo.engines(core, dst)[::2]
         m = sum(1 << e for e in en)
@@ -186,30 +207,42 @@ def rank_program(g, core, T, topo):
         def fn():
             g.remote_dma(ap(o), ap(i), T.sem[sem], T.sem.lsem, pid, rid, m)
         s = op("gp", fn, [rg(i)], [], 0.1)
-        op("net", None, [], [rg(o)], 0.0, event=(sem, len(en)), after=(s,), lat=lat)
+        op("net", None, [], [rg(o)], 0.0, event=(sem, len(en)), after=(s,), lat=CFG["net"])
 
-    def dma(o_ap, i_ap, rd, wr, sem, lat, eng="sp"):
-        op(eng, lambda: (g.sync if eng == "sp" else g.scalar).dma_start(o_ap, i_ap).then_inc(T.sem[sem], 16), rd, wr, 0.1, event=(sem, 16), lat=lat)
+    def dma(o_ap, i_ap, rd, wr, sem, lat, eng="sp", after=()):
+        return op(eng, lambda: (g.sync if eng == "sp" else g.scalar).dma_start(o_ap, i_ap).then_inc(T.sem[sem], 16), rd, wr, 0.1,
+                  event=(sem, 16), lat=lat, after=after)
 
     V0, THI, SD, XW = ("V0", 0, 32), ("THI", 0, 4), ("SD", 0, 512), ("X", 0, W)
     dma(T.V0[:], T.v0[:], [], [V0], "ld_v", 2.0, "act")
-    dma(T.THI[:], T.th[:], [], [THI], "ld_th", 3.0, "act")
-    dma(T.SD[:], T.sd[:], [], [SD], "ld_sd", 2.5)
-    dma(T.X[:, 0:W], T.x[:], [], [XW], "ld_x", 10.0)
+    d0 = dma(T.SD[:, 0:512], T.sd[:], [], [SD], "ld_sd", 3.0)
+    d1 = dma(T.X[:, 0:W], T.x[:], [], [XW], "ld_x", CFG["ldx"], after=(d0,))
+    dma(T.THI[:], T.th[:], [], [THI], "ld_th", CFG["ldx"] + 0.5, after=(d1,))
 
     ONE, BO, t0, ID = al("PB", 128), al("PB", 128), al("PB", 128), al("PB", 128)
     fill(ONE, 1.0)
     asel(t0, ONE, [[-16, 8], [0, 16]], ALU.is_ge, 0, 1)
     asel(BO, t0, [[16, 8], [0, 16]], ALU.is_ge, 15, -1)
     asel(ID, ONE, [[-1, 128]], ALU.is_equal, 0, 1)
+    BO8 = sub(BO, 0, 128, 16)
     fill(("SEL", 0, 2048), 0.0)
     for i in range(16): copy(("SEL", i * 128 + i, (i + 1) * 128, 16), sub(BO, i, 128, 16))
 
     def sel(i):
         return ("SEL", i * 128, (i + 1) * 128)
-    NID, NID16 = al("PB", 128), al("PB", 128)
-    ts(NID, ID, -1.0, ALU.mult)
-    ts(NID16, ID, -16.0, ALU.mult)
+
+    def ei(i):
+        return ("EI", i * 128, (i + 1) * 128)
+
+    def scaled(src, c, p="PB"):
+        r = al(p, wd(src))
+        move(r, src, scale=c)
+        return r
+    NID, NID16, ID4K, IDF, N8F = scaled(ID, -1.0), scaled(ID, -16.0), scaled(ID, 4096.0), scaled(ID, 1.0, "PF"), scaled(ONE, -8.0, "PF")
+    ID2 = [scaled(ID, -2.0 ** q) for q in range(8)]
+    IDG = [al("PB", 128) for _ in range(8)]
+    for k in range(8): ts(IDG[k], ID, sub(BO, 16 * k, 16 * k + 1), ALU.mult, -2.0 ** -8, ALU.mult)
+    RX = scaled(BO8, -0.25)
     BIAS = (al("PF", 1), al("PF", 1))
     for m in range(2): fill(BIAS[m], 8.0 * KS[m])
     h1, h2, M16 = al("PF", 64), al("PF", 32), al("PF", 16)
@@ -223,191 +256,192 @@ def rank_program(g, core, T, topo):
     iota(i16, [[1, 16]], 0, 0)
     tt(x16, M16, i16, ALU.mult)
     red(IC, x16, ALU.add)
-    INI, iq, LANE, TL, P16N = al("PF", 1), al("PF", 32), al("PF", 32), al("PF", 32), al("PF", 32)
+    INI, iq, TL, C16B, BASE = al("PF", 1), al("PF", 32), al("PF", 32), al("PB", 16), al("PB", 64)
     ts(INI, IC, 512.0 - 16.0, ALU.add)
-    iota(iq, [[16, 32]], 0, 0)
-    ts(LANE, iq, IC, ALU.add)
-    ts(TL, LANE, 512.0, ALU.add)
-    fill(P16N, 16.0)
+    iota(iq, [[16, 32]], 512, 0)
+    ts(TL, iq, IC, ALU.add)
+    fill(C16B, 16.0)
+    fill(BASE, 2.0 ** -9)
     V16 = al("PF", 64)
 
     def v16ops(dst, src):
-        for m in range(2): ts(sub(dst, m * 32, m * 32 + 32), src, 16.0, ALU.mult, -64.0 * KS[m] ** 2, ALU.add)
+        for c in range(2):
+            for m in range(2): ts(sub(dst, c * 32 + m * 16, c * 32 + m * 16 + 16), sub(src, c * 16, c * 16 + 16), 16.0, ALU.mult, -64.0 * KS[m] ** 2, ALU.add)
     v16ops(V16, V0)
 
-    def sums(zr, extra=None):
-        o = ("U0", 0, 32)
+    def sums(o, zr, extra=None):
         lst = [(o, NID16, extra, True, False)] if extra is not None else []
-        for i in range(16): lst.append((o, sel(i), sub(zr, i, 512, 16), extra is None and i == 0, i == 15))
-        mm(lst)
-        return o
-    SQ0 = al("PF", 64)
-    o = sums(SD)
-    for m in range(2): act(sub(SQ0, m * 32, m * 32 + 32), o, AF.Square, BIAS[m])
+        for i in range(16): lst.append((o, sel(i), sub(zr, i, wd(zr), 16), extra is None and i == 0, i == 15))
+        mms(lst, 4)
+    SQ0, SQ1 = al("PF", 64), al("PF", 64)
+    sums(("P0", 0, 32), SD)
+    for c in range(2):
+        for m in range(2): act(sub(SQ0, c * 32 + m * 16, c * 32 + m * 16 + 16), ("P0", c * 16, c * 16 + 16), AF.Square, BIAS[m])
+    ts(SQ1, SQ0, 65536.0, ALU.add)
 
-    MAP, MAPW = ("MAP", 0, NM), ("MAP", 0, W)
-    fill(MAPW, 0.0)
+    MAP, MAPW = ("MAP", 0, NMAP), ("MAP", 0, W)
+    for k in range(4): fill(("MAP", k * 2048, k * 2048 + 2048), 0.0)
     TH = al("PF", 4)
     copy(TH, THI)
-    NEG = al("PF", 1)
-    fill(NEG, -1.0)
-    TRI, nbo, BOF = al("PB", 128), al("PB", 128), al("PF", 128)
-    ts(nbo, BO, -1.0, ALU.mult)
-    asel(TRI, nbo, [[-1, 128]], ALU.is_ge, 0, 1)
-    copy(BOF, BO)
-    for i in range(16): ts(("EI", i * 128, i * 128 + 128), BO, m16(i), ALU.mult)
-    RHE, RK = al("PB", 64), al("PB", 24)
-    for k in range(8): ts(sub(RHE, k * 8, k * 8 + 8), sub(BO, 0, 128, 16), m16(0), ALU.mult)
-    for k in range(3): ts(sub(RK, k, 24, 3), sub(BO, 0, 128, 16), m16(k), ALU.mult)
-    ex0, EXP, KT = al("PB", 128), al("PB", 128), al("PB", 512)
-    asel(ex0, ONE, [[1, 128]], ALU.is_ge, 0, -16)
-    asel(EXP, ex0, [[-1, 128]], ALU.is_ge, 15, 16)
-    DM, dm1, dm2 = al("PF", 128), al("PF", 16), al("PF", 16)
-    ts(dm1, M16, 33554432.0, ALU.mult, -17.0, ALU.add)
-    ts(sub(dm2, 1, 16), sub(M16, 0, 15), -1.0, ALU.mult)
-    ts(sub(dm2, 0, 1), m16(15), -1.0, ALU.mult)
-    for k in range(8): tt(sub(DM, k * 16, k * 16 + 16), dm1, dm2, ALU.add)
-    pc, c8, c9, g8, g9, dl = (al("PF", 1) for _ in range(6))
-    DL = al("PU", 1)
+    UT, LT = al("PB", 128), al("PB", 128)
+    asel(UT, BO, [[-1, 128]], ALU.is_ge, 0, 1)
+    asel(LT, BO, [[1, 128]], ALU.is_gt, 0, -1)
+    for i in range(16): ts(ei(i), BO, m16(i), ALU.mult)
+    EH, EL, LH, LL = scaled(ei(0), 2.0 ** -6), scaled(ei(0), 2.0 ** -10), al("PB", 512), al("PB", 512)
+    iota(LH, [[1, 32], [0, 16]], 0, 0)
+    iota(LL, [[0, 32], [1, 16]], 0, 0)
+    RHE = al("PB", 64)
+    for k in range(8): ts(sub(RHE, k * 8, k * 8 + 8), BO8, m16(0), ALU.mult)
+    DM, dm1, dm2 = al("PF", 32), al("PF", 16), al("PF", 16)
+    ts(dm1, M16, 33554432.0 * KB, ALU.mult, -17.0 * KB, ALU.add)
+    ts(sub(dm2, 1, 16), sub(M16, 0, 15), -KB, ALU.mult)
+    ts(sub(dm2, 0, 1), m16(15), -KB, ALU.mult)
+    for k in range(2): tt(sub(DM, k * 16, k * 16 + 16), dm1, dm2, ALU.add)
+    pc, g8, CQ4 = al("PF", 1), al("PF", 1), al("PF", 1)
     iota(pc, [[0, 1]], 0, 1)
     tt(g8, pc, IC, ALU.subtract)
-    ts(c8, IC, 7.5, ALU.is_ge, -8.0, ALU.mult)
-    tt(c9, c8, IC, ALU.add)
-    ts(g9, g8, 0.5, ALU.mult)
-    tt(dl, g9, c9, ALU.add)
-    copy(DL, dl)
+    ts(CQ4, g8, 0.25, ALU.mult, 129.6875, ALU.add)
     i8, TRW, SROW = al("PF", 8), al("PF", 8), al("PF", 128)
-    iota(i8, [[16, 8]], 2 * W + 128, 0)
-    ts(TRW, i8, IC, ALU.add)
+    iota(i8, [[16, 8]], W + 129, 0)
+    ts(TRW, i8, IC, ALU.add, -KK, ALU.add)
     iota(SROW, [[1024, 128]], W * 1024 + 896, 0)
-    for t in range(TS): copy(("KSD%d" % t, 0, 128), SROW)
-    hir, lor, hm2, lm2, SC = al("PF", 128), al("PF", 128), al("PF", 128), al("PF", 128), al("PB", 128)
-    iota(hir, [[1, 8], [0, 16]], 1, 0)
-    iota(lor, [[0, 8], [1, 16]], 1, 0)
-    ts(hm2, hir, m16(0), ALU.mult)
-    ts(lm2, lor, m16(1), ALU.mult)
-    tt(SC, hm2, lm2, ALU.add)
-    KRP, P16, N16, ZERO = al("PB", 512), al("PB", 128), al("PB", 128), al("PB", 128)
+    for t in range(TS): move(("KSD%d" % t, 0, 128), SROW, scale=KB)
+    CQ, C2, dd, dr = al("PF", 128), al("PB", 128), al("PF", 16), al("PF", 16)
+    iota(CQ, [[-16, 8], [0, 16]], -8, 0)
+    ts(sub(dr, 0, 8), sub(M16, 8, 16), -2.0 ** 20, ALU.mult)
+    ts(sub(dr, 8, 16), sub(M16, 0, 8), -2.0 ** 20, ALU.mult)
+    tt(dd, dr, M16, ALU.add)
+    for q in range(8): move(sub(C2, q * 16, q * 16 + 16), dd, scale=2.0 ** (-q - 1))
+    KRP, KBZ, ZERO = al("PB", 512), al("PB", 512), al("PB", 128)
     fill(KRP, 0.0)
-    fill(P16, 16.0)
-    fill(N16, -16.0)
+    fill(KBZ, 0.0)
     fill(ZERO, 0.0)
 
     SQ, SI, C16, Y1, HB = two("PF", 64), two("PI", 64), two("PU", 64), two("PB", 512), two("PB", 512)
     ZH, ZF, GE = al("PB", 1536), al("PB", 512), al("PB", 512)
     CN, TM = two("PI", 256), two("PF", 256)
     tda, tdb = al("PF", 256), al("PF", 256)
-    OFF, CLX = al("PU", 256), al("PF", 256)
-    ZG, SQS, VSE, SIS, CS, VSW = al("PB", 512), al("PF", 64), al("PF", 64), al("PI", 64), al("PI", 64), al("PI", 8)
-    KSI, KSC, CLB, MK = al("PI", 128), al("PI", 128), al("PB", 128), al("PB", 128)
+    OFF, CR, crk = al("PU", 256), al("PF", 256), al("PF", 256)
+    ZG, SQS, VSE, SIS, CS = al("PB", 512), al("PF", 64), al("PF", 64), al("PI", 64), al("PI", 64)
+    AQ, CLT, KKC = al("PB", 128), al("PB", 1024), al("PF", 1)
+    iota(CLT, [[-1, 8], [0, 128]], 0, 0)
+    fill(("SD", 512, 1024), 0.0)
+    fill(KKC, KK)
     LRF, lr1, lr2, lr3, LRU = two("PF", 32), al("PF", 32), al("PF", 32), al("PF", 32), two("PU", 32)
-    KB, LG, WO = al("PB", 256), al("PB", 512), two("PF", 32)
-    HALT, GO, FRA, FR = al("PB", 32), al("PB", 32), al("PB", 32), two("PB", 32)
-    scn, HT, wy, SOFF = al("PF", 32), al("PF", 32), al("PF", 32), al("PU", 32)
-    vm, vq, vs, v37, vsum, vbp = (al("PI", 32) for _ in range(6))
+    LG, WO = al("PB", 512), two("PF", 32)
+    HAL, HTT, GO, FRA, FR = al("PB", 48), al("PF", 48), al("PB", 32), al("PB", 32), two("PB", 32)
+    fill(HAL, 0.0)
+    fill(HTT, 0.0)
+    HALT, HT = sub(HAL, 16, 48), sub(HTT, 16, 48)
+    dht, SOFF = al("PF", 32), al("PU", 32)
+    vm, vw, vq, vr, VB = (al("PI", 32) for _ in range(5))
     SV0, SIN = al("PF", 64), al("PI", 64)
-    VB16, VBL, VN, VNs, VC = al("PF", 64), al("PF", 32), two("PI", 32), al("PI", 32), two("PF", 32)
-    vd, vd2, KW, kw1 = al("PF", 32), al("PF", 32), al("PF", 32), al("PF", 32)
-    KJ, KM, MN, UQ = al("PF", 128), al("PF", 128), al("PF", 8), al("PF", 16)
-    fill(UQ, 0.0)
-    AB = [al("PF", 16 * q + 16) for q in range(8)]
-    KI, VW, VT = al("PI", 8), al("PI", 8), al("PF", 8)
-    mt, mo, to1, to2 = al("PF", 8), al("PF", 8), al("PF", 16), al("PF", 8)
-    MOFF, TOFF = two("PU", 8), two("PU", 8)
-    MG = al("PB", 128)
-    ZI, ZJ, ZO, DNR = al("PI", 8), al("PI", 8), al("PU", 8), al("PB", 128)
-    HS, LS = two("PB", 128), two("PB", 128)
-    HPS, DNB, SENT, A16 = al("PF", 64), al("PB", 16), al("PB", 8), al("PF", 1)
+    VB16, VN, VNs, VC = al("PF", 64), two("PI", 32), al("PI", 32), two("PI", 32)
+    vd, vd2, VD, VDB = al("PF", 32), al("PF", 32), al("PI", 64), al("PB", 64)
+    KJ, KM, KW, MN, MO = al("PF", 128), al("PF", 128), al("PF", 8), al("PF", 8), al("PF", 8)
+    AB = al("PF", 8 * 144)
+    EXT = sub(AB, 0, 8 * 144, 144)
+    OK, MOF, TOFF = al("PB", 8), al("PF", 8), two("PU", 8)
+    ZI, ZJ, ZO = al("PI", 8), al("PI", 8), al("PU", 8)
+    YQ = two("PB", 128)
+    SG, ACC, A16, DMS = al("PB", 64), al("PF", 1), al("PF", 1), al("PB", 8)
+    hb1, hb2, hb3, hb4 = al("PI", 256), al("PI", 256), al("PI", 128), al("PI", 64)
 
-    def vbase(src):
-        copy(vs, src)
-        ts(vm, vs, 4095, ALU.bitwise_and)
-        tt(vq, vm, vm, ALU.mult)
-        ts(vsum, vq, 3, ALU.arith_shift_right)
-        ts(v37, vs, 37.0, ALU.mult)
-        tt(vsum, vsum, v37, ALU.add)
-        ts(vbp, vsum, 8191, ALU.bitwise_and)
-        ts(VBL, vbp, 16.0, ALU.mult)
-        v16ops(VB16, vbp)
-        tt(SV0, SQ0, VB16, ALU.add)
+    def vbase(v):
+        ts(vm, v, 4095, ALU.bitwise_and)
+        ts(vw, vm, 288.0, ALU.add)
+        tt(vq, vm, vw, ALU.mult)
+        ts(vr, vq, 3, ALU.arith_shift_right, 8191, ALU.bitwise_and)
+        tt(VB, vr, v, ALU.add)
+        v16ops(VB16, VB)
+        tt(SV0, SQ1, VB16, ALU.add)
 
     def keys(v):
-        ts(kw1, v, 1024.0, ALU.mult)
-        tt(KW, kw1, LANE, ALU.add)
-        for i in range(16):
-            if i < CFG["kx"]: act(("KX", i, 512, 16), KW, AF.Copy, scale=m16(i))
-            else: ts(("KX", i, 512, 16), KW, m16(i), ALU.mult)
-        for k in range(4): mm([(("TPA", k * 128, k * 128 + 128), BOF, ("KX", k * 128, k * 128 + 128), True, True)], f32=True)
-        act(("KEYR", 0, 512), ("TPA", 0, 512), AF.Copy)
+        ts(sub(VD, 0, 32), v, 8064, ALU.bitwise_and)
+        ts(sub(VD, 32, 64), v, 127, ALU.bitwise_and)
+        copy(VDB, VD)
+        mm([(("BD", 0, 512), EH, LH, True, False)])
+        mm([(("BD", 0, 512), EL, LL, False, False)])
+        mms([(("BD", i, 512, 16), ei(i), sub(VDB, d * 32, d * 32 + 32), False, i == 15 and d == 1) for i in range(16) for d in range(2)], 4)
+        for h in range(2): move(("KEYR", h * 256, h * 256 + 256), ("BD", h * 256, h * 256 + 256), scale=1024.0 * KB)
 
-    copy(VC[0], V0)
     keys(V0)
-    vbase(VC[0])
+    vbase(V0)
 
     for t in range(TS):
         pr, nx, last = t % 2, (t + 1) % 2, t == TS - 1
         partner = T.cores[rank ^ (1 + t % 7)]
-        cn, fr, vc = CN[pr], FR[pr], VC[pr]
-        zc = SD
+        cn, fr, vc = CN[pr], FR[pr], VC[pr] if t else V0
+        ksd = "KSD%d" % t
         for b in range(4):
             p = b % 2
-            if b == 0: sq = SQ0
-            else:
-                sq = SQ[p]
-                o = sums(zc)
-                for m in (1, 0): act(sub(sq, m * 32, m * 32 + 32), o, AF.Square, BIAS[m])
-            c16 = C16[p]
-            for m in (1, 0):
-                k0, k1 = m * 32, m * 32 + 32
-                if b or not t: tt(sub(SI[p], k0, k1), sub(sq, k0, k1), sub(V16, k0, k1), ALU.add)
-                c = sub(cn, b * 64 + k0, b * 64 + k1)
-                ts(c, sub(SI[p] if b or not t else SIN, k0, k1), 4, ALU.arith_shift_right, 8191, ALU.bitwise_and)
-                copy(sub(c16, k0, k1), c)
+            zc = SD if b == 0 else sub(ZH, b * 512 - 512, b * 512)
             zn = sub(ZH, b * 512, b * 512 + 512) if b < 3 else ZF
-            for c0, c1 in CFG["cut"]:
-                yy, hu = sub(Y1[p], c0 * 16, c1 * 16), sub(HB[p], c0 * 16, c1 * 16)
-                gather("act", yy, XW, sub(c16, 32 + c0, 32 + c1))
-                o16 = sub(c16, c0, c1)
-                op("dve", lambda o16=o16, yy=yy, hu=hu: g.vector.tensor_tensor(out=ap(hu), in0=ind(XW, o16), in1=ap(yy), op=ALU.max),
-                   [XW, o16, yy], [hu], gat(c1 * 16 - c0 * 16))
-            for h, (c0, c1) in enumerate(CFG["dcut"]):
-                r0, r1 = c0 * 16, c1 * 16
-                dps = ("D%d" % h, 0, r1 - r0)
-                mm([(dps, NID, sub(zc, r0, r1), True, False)])
-                mm([(dps, ID, sub(HB[p], r0, r1), False, True)])
-                act(sub(zn, r0, r1), dps, AF.Abs)
-            zc = zn
-        if t:
-            mm([(("TPB", k * 32, k * 32 + 32), ID, fr, True, True) for k in range(8)])
-            tt(tda, TM[nx] if t > 1 else CN[0], cn, ALU.subtract)
-            tt(tdb, ("TPB", 0, 256), tda, ALU.mult)
-            tt(("YT", 0, 256) if last else TM[pr], tdb, cn, ALU.add)
-        for c0, c1 in CFG["dcut"]: ts(sub(GE, c0 * 16, c1 * 16), sub(zc, c0 * 16, c1 * 16), sub(TH, t, t + 1), ALU.is_ge)
-        o = sums(GE, fr if t else None)
-        ts(HALT, o, 8.5, ALU.is_ge)
-        p2, p12 = ("HP", 0, 32), ("HP", 32, 64)
-        mm([(p2, BO, HALT, True, True), (p12, TRI, HALT, True, True)])
-        tt(HT, HALT, TL, ALU.mult)
-        op("dve", lambda p2=p2: g.vector.tensor_tensor_scan(out=ap(scn), data0=ap(P16N), data1=ap(p2), initial=ap(INI), op0=ALU.add, op1=ALU.add),
-           [P16N, p2, INI], [scn], dv(32))
-        tt(wy, p12, HT, ALU.subtract)
-        tt(WO[pr], wy, scn, ALU.add)
-        copy(SOFF, WO[pr])
-        scatter(("KSD%d" % t, 0, 1536), SOFF, ("KEYR", 0, 512))
-        ks = ("KSD%d" % t, 0, 128)
-        send(partner, ("KL", t * 128, t * 128 + 128), ks, "rk%d" % t, 2.4)
-        kws = ("KWS", t * 8, t * 8 + 8)
-        tt(KM, ks, DM, ALU.min)
-        for q in range(8):
-            if q < CFG["kw"]: act(sub(KJ, q * 16, q * 16 + 16), sub(KM, q * 16, q * 16 + 16), AF.Copy, acc_o=sub(kws, q, q + 1))
-            else: red(sub(kws, q, q + 1), sub(KM, q * 16, q * 16 + 16), ALU.add)
-        send(partner, ("KWL", t * 8, t * 8 + 8), kws, "rw%d" % t, 1.8)
-        copy(KSI, ks)
-        ts(KSC, KSI, 7, ALU.arith_shift_right, 7, ALU.bitwise_and)
-        mvs = ("MVS", t * 128, t * 128 + 128)
-        ts(MG, KSC, 1.0, ALU.add, m16(2), ALU.mult)
-        tt(mvs, MG, SC, ALU.add)
-        send(partner, ("MVL", t * 128, t * 128 + 128), mvs, "rm%d" % t, 2.2)
+            for c in range(2):
+                banks = ("P%d" % c, "Q%d" % c)
+                k0, z0 = c * 32, c * 256
+                si = sub(SI[p], k0, k0 + 32)
+                if b:
+                    o = (banks[0], 256, 272)
+                    sums(o, sub(zc, z0, z0 + 256))
+                    for m in (1, 0): act(sub(SQ[p], k0 + m * 16, k0 + m * 16 + 16), o, AF.Square, BIAS[m])
+                    tt(si, sub(SQ[p], k0, k0 + 32), sub(V16, k0, k0 + 32), ALU.add)
+                elif t: si = sub(SIN, k0, k0 + 32)
+                else: tt(si, sub(SQ0, k0, k0 + 32), sub(V16, k0, k0 + 32), ALU.add)
+                cc = sub(cn, c * 128 + b * 32, c * 128 + b * 32 + 32)
+                ts(cc, si, 4, ALU.arith_shift_right, 8191, ALU.bitwise_and)
+                c16 = sub(C16[p], k0, k0 + 32)
+                copy(c16, cc)
+                for h, (c0, c1) in enumerate(CFG["cut"]):
+                    r0, r1 = z0 + c0 * 16, z0 + c1 * 16
+                    yy, hu, o16 = sub(Y1[p], r0, r1), sub(HB[p], r0, r1), sub(c16, c0, c1)
+                    gather("act", yy, XW, sub(c16, 16 + c0, 16 + c1))
+                    op("dve", lambda o16=o16, yy=yy, hu=hu: g.vector.tensor_tensor(out=ap(hu), in0=ind(XW, o16), in1=ap(yy), op=ALU.max),
+                       [XW, o16, yy], [hu], gat(r1 - r0))
+                    dps = (banks[h], 0, r1 - r0)
+                    mm([(dps, NID, sub(zc, r0, r1), True, False)])
+                    mm([(dps, ID, hu, False, True)])
+                    act(sub(zn, r0, r1), dps, AF.Abs)
+                    if b == 3: ts(sub(GE, r0, r1), sub(zn, r0, r1), sub(TH, t, t + 1), ALU.is_ge)
+        for c in range(2):
+            q0, q1 = c * 16, c * 16 + 16
+            o, dl = ("P%d" % c, 256, 272), ("Q%d" % c, 256, 272)
+            sums(o, sub(GE, c * 256, c * 256 + 256), sub(fr, q0, q1) if t else None)
+            ts(sub(HALT, q0, q1), o, 8.5, ALU.is_ge)
+            mm([(dl, ID, C16B, True, False)])
+            mm([(dl, UT, sub(HALT, q0 - 1, q1 - 1), False, False), (dl, LT, sub(HALT, q0, q1), False, True)])
+            tt(sub(HT, q0, q1), sub(HALT, q0, q1), sub(TL, q0, q1), ALU.mult)
+            tt(sub(dht, q0, q1), sub(HT, q0 - 1, q1 - 1), sub(HT, q0, q1), ALU.subtract)
+            ini, wo, da = sub(WO[pr], 15, 16) if c else INI, sub(WO[pr], q0, q1), sub(dht, q0, q1)
+            op("dve", lambda ini=ini, wo=wo, da=da, dl=dl: g.vector.tensor_tensor_scan(out=ap(wo), data0=ap(da), data1=ap(dl), initial=ap(ini), op0=ALU.add, op1=ALU.add),
+               [da, dl, ini], [wo], dv(16))
+            copy(sub(SOFF, q0, q1), wo)
+            scatter((ksd, 0, 1536), sub(SOFF, q0, q1), ("KEYR", c * 256, c * 256 + 256))
+        ks = (ksd, 0, 128)
+        for k in (3, 2, 1, 0): tt(sub(KM, k * 32, k * 32 + 32), sub(ks, k * 32, k * 32 + 32), DM, ALU.min)
+        for q in range(7, -1, -1):
+            km, kw = sub(KM, q * 16, q * 16 + 16), sub(KW, q, q + 1)
+            either({"act": (act_call(sub(KJ, q * 16, q * 16 + 16), km, AF.Copy, acc_o=kw), dv(16) + 0.02),
+                    "dve": (lambda km=km, kw=kw: g.vector.tensor_reduce(out=ap(kw), in_=ap(km), axis=AxisListType.X, op=ALU.add), dv(16))},
+                   [km], [kw, sub(KJ, q * 16, q * 16 + 16)])
+        for h in (1, 0):
+            ex, kw = sub(AB, h * 576, h * 576 + 576, 144), sub(KW, h * 4, h * 4 + 4)
+            either({"act": (act_call(ex, kw, AF.Identity, KKC, -1.0 / (1024.0 * KB)), dv(4)),
+                    "dve": (ts_call(ex, kw, -1.0 / (1024.0 * KB), ALU.mult, KK, ALU.add), dv(4))}, [kw, KKC], [ex])
+        for q in range(7, -1, -1):
+            act(sub(AB, q * 144 + 1, q * 144 + 16 * q + 17), sub(ks, 0, 16 * q + 16), AF.Abs, sub(KW, q, q + 1), -1.0)
+            red(sub(MN, q, q + 1), sub(AB, q * 144, q * 144 + 16 * q + 17), ALU.min, True)
+        tt(MO, MN, TRW, ALU.min)
+        mos, mol = ("MOS", t * 8, t * 8 + 8), ("MOL", t * 8, t * 8 + 8)
+        ts(mos, MO, KK, ALU.add)
+        ts(ZI, KW, 1.0 / KB, ALU.mult, 256.0, ALU.add)
+        ts(ZJ, ZI, 1023, ALU.bitwise_and)
+        copy(ZO, ZJ)
+        op("dve", lambda: g.vector.tensor_tensor(out=ap(AQ), in0=ind(CLT, ZO), in1=ap(CQ), op=ALU.add), [CLT, ZO, CQ], [AQ], gat(128))
+        mvs, mvl = ("MVS", t * 128, t * 128 + 128), ("MVL", t * 128, t * 128 + 128)
+        tt(mvs, AQ, C2, ALU.max)
+        send(partner, mvl, mvs, "rm%d" % t)
+        send(partner, mol, mos, "ro%d" % t)
         ts(GO, WO[pr], 127.5, ALU.is_lt)
         if t:
             tt(FRA, fr, GO, ALU.add)
@@ -419,110 +453,110 @@ def rank_program(g, core, T, topo):
             copy(FRA, GO)
             tt(LRF[pr], WO[pr], GO, ALU.mult)
         copy(LRU[pr], LRF[pr])
-        ts(ZI, kws, 256.0, ALU.add)
-        ts(ZJ, ZI, 511, ALU.bitwise_and)
-        copy(ZO, ZJ)
         for b in range(4):
-            gather("act", sub(ZG, b * 128, b * 128 + 128), SD if b == 0 else sub(ZH, b * 512 - 512, b * 512), ZO)
+            gather(None, sub(ZG, b * 128, b * 128 + 128), ("SD", 0, 1024) if b == 0 else sub(ZH, b * 512 - 512, b * 512 + 512), ZO)
         us = ("BD", 0, 32)
-        mm([(us, sel(i), sub(ZG, i, 512, 16), i == 0, i == 15) for i in range(16)])
+        sums(us, ZG)
         for m in range(2): act(sub(SQS, m * 32, m * 32 + 32), us, AF.Square, BIAS[m])
-        ts(VSW, ZI, 10, ALU.arith_shift_right, 8191, ALU.bitwise_and)
-        ts(sub(VSE, 0, 8), VSW, 16.0, ALU.mult, -64.0 * KS[0] ** 2, ALU.add)
+        ts(sub(VSE, 0, 8), EXT, -16.0, ALU.mult, 16.0 * KK - 64.0 * KS[0] ** 2, ALU.add)
         copy(sub(VSE, 8, 16), sub(VSE, 0, 8))
         copy(sub(VSE, 16, 32), sub(VSE, 0, 16))
         ts(sub(VSE, 32, 64), sub(VSE, 0, 32), 64.0 * (KS[0] ** 2 - KS[1] ** 2), ALU.add)
         tt(SIS, SQS, VSE, ALU.add)
         ts(CS, SIS, 4, ALU.arith_shift_right, 8191, ALU.bitwise_and)
         copy(sub(OFF, t * 64, t * 64 + 64), CS)
-        ts(CLB, KSC, 1.0, ALU.add)
-        mm([(("BD", 64, 128), CLB, RHE, True, True)])
-        copy(sub(CLX, t * 64, t * 64 + 64), ("BD", 64, 128))
+        mm([(("BD", 64, 128), AQ, RHE, True, True)])
+        ts(sub(CR, t * 64, t * 64 + 64), ("BD", 64, 128), 0.25, ALU.mult, CQ4, ALU.add)
         if not last:
-            gather("act", ("ZS", t * 128, t * 128 + 128), ZF, ZO)
-            send(partner, ("ZL", t * 128, t * 128 + 128), ("ZS", t * 128, t * 128 + 128), "rz%d" % t, 2.2)
-        kl, kwl = ("KL", t * 128, t * 128 + 128), ("KWL", t * 8, t * 8 + 8)
-        for q in range(8): act(AB[q], sub(kl, 0, 16 * q + 16), AF.Abs, sub(kwl, q, q + 1), NEG)
-        ts(KI, kwl, 256.0, ALU.add)
-        ts(VW, KI, 10, ALU.arith_shift_right)
-        tt(VT, VW, TRW, ALU.subtract)
-        ts(SENT, kwl, float(W * 1024), ALU.is_ge)
-        for q in range(8): red(sub(MN, q, q + 1), AB[q], ALU.min)
-        uq = sub(UQ, 0, 8)
-        ts(uq, MN, 255.5, ALU.is_ge)
-        tt(mt, uq, VT, ALU.mult)
-        tt(mo, mt, TRW, ALU.add)
-        copy(MOFF[pr], mo)
-        scatter(MAP, MOFF[pr], ("MVL", t * 128, t * 128 + 128))
-        tiles = 8 * (t + 1)
-        for k in range((t + 2) // 2):
-            bank = ("TPA", "TPB")[k]
-            nt = min(16, tiles - 16 * k)
-            for j in range(nt // 2):
-                jj = k * 8 + j
-                gather("dve" if jj in CFG["map"][t] else "act", ("G", jj * 256, jj * 256 + 256), MAPW, sub(OFF, jj * 16, jj * 16 + 16))
-                mm([((bank, (2 * j + w) * 24, (2 * j + w) * 24 + 24), ("G", jj * 256 + w * 128, jj * 256 + w * 128 + 128), RK, True, True) for w in range(2)])
-            nc = nt * 8
-            hs, ls, mk = sub(HS[k], 0, nc), sub(LS[k], 0, nc), sub(MK, 0, nc)
-            copy(ls, (bank, 1, nt * 24, 3))
-            tt(mk, (bank, 2, nt * 24, 3), sub(CLX, k * 128, k * 128 + nc), ALU.is_ge)
-            for d in range(16):
-                ts(("LO", k * 2048 + d, k * 2048 + nc * 16, 16), ls, float(d + 1), ALU.is_equal)
-            tt(hs, (bank, 0, nt * 24, 3), mk, ALU.mult)
-            for d in range(8):
-                ts(("HI", k * 1024 + d, k * 1024 + nc * 8, 8), hs, float(d + 1), ALU.is_equal)
-            mm([(("HP", 0, 64), ("LO", k * 2048 + u * 128, k * 2048 + u * 128 + 128), ("HI", k * 1024 + u * 64, k * 1024 + u * 64 + 64),
-                 k == 0 and u == 0, 16 * k + u == tiles - 1) for u in range(nt)])
-        copy(HPS, ("HP", 0, 64))
-        op("dve", lambda: g.vector.tensor_tensor(out=ap(DNB), in0=ind(HPS, DL), in1=ap(UQ), op=ALU.is_lt), [HPS, DL, UQ], [DNB], gat(16))
-        aps = ("HP", 0, 8)
-        mm([(aps, N16, SENT, True, False), (aps, P16, sub(DNB, 0, 8), False, True)])
-        red(A16, aps, ALU.add)
+            gather(None, ("ZS", t * 128, t * 128 + 128), sub(ZF, 0, 1024), ZO)
+            send(partner, ("ZL", t * 128, t * 128 + 128), ("ZS", t * 128, t * 128 + 128), "rz%d" % t)
+        if t:
+            mms([(("HP", c * 128 + k * 16, c * 128 + k * 16 + 16), ID, sub(fr, c * 16, c * 16 + 16), True, True) for c in range(2) for k in range(8)], 4)
+            tt(tda, TM[nx] if t > 1 else CN[0], cn, ALU.subtract)
+            tt(tdb, ("HP", 0, 256), tda, ALU.mult)
+            tt(TM[pr], tdb, cn, ALU.add)
+            if last:
+                for c in range(2):
+                    for e in range(8): move(("YT", e * 32 + c * 16, e * 32 + c * 16 + 16), sub(TM[pr], c * 128 + e * 16, c * 128 + e * 16 + 16))
+                dma(T.yt[:], T.YT[:], [("YT", 0, 256)], [], "st_t", 2.4)
+        scatter(MAP, mol, mvl)
+        ts(OK, mol, W - 0.5, ALU.is_lt)
+        ts(MOF, mol, -6.0 * 4096, ALU.add)
+        hp, tp, ap16 = ("HP", 0, 64), ("P1", 0, 8), ("P0", 0, 1)
+        mm([(hp, ID, BASE, True, False)] + [(sub(hp, k * 8, k * 8 + 8), IDG[k], OK, False, False) for k in range(8)])
+        mm([(tp, IDF, MOF, True, False)], f32=True)
+        u0 = 0
+        for k, nt in enumerate(CFG["batch"][t]):
+            xs = ("Q%d" % (k % 2), 0, nt * 8)
+            for j in range(u0 // 2, (u0 + nt) // 2):
+                gather(None, ("G", j * 256, j * 256 + 256), MAPW, sub(OFF, j * 16, j * 16 + 16))
+                tn = CFG["turn"]
+                bank, c0 = CFG["banks"][j // tn % len(CFG["banks"])], j % tn * 256
+                tiles = [("G", u * 128, u * 128 + 128) for u in (2 * j, 2 * j + 1)]
+                mm([(sub(xs, (2 * j + w - u0) * 8, (2 * j + w - u0) * 8 + 8), tiles[w], RX, True, True) for w in range(2)])
+
+                def turn(tiles=tiles, bank=bank, c0=c0):
+                    g.tensor.transpose(T[bank][:, c0:c0 + 128], ap(tiles[0]), ap(ID))
+                    return g.tensor.transpose(T[bank][:, c0 + 128:c0 + 256], ap(tiles[1]), ap(ID))
+                if bank[0] == "T": op("pe", turn, tiles + [ID], [(bank, c0, c0 + 256)], 256 * PEC)
+                else: mm([((bank, c0 + w * 128, c0 + w * 128 + 128), tiles[w], ID, True, True) for w in range(2)])
+                if j % tn == tn - 1: move(("LO", j * 256 - c0, j * 256 + 256), (bank, 0, c0 + 256), relu=True)
+            yq = sub(YQ[k % 2], 0, nt * 8)
+            tt(yq, xs, sub(CR, u0 * 8, (u0 + nt) * 8), ALU.add)
+            for d in range(8): ts(("HI", u0 * 64 + d, (u0 + nt) * 64, 8), yq, 130.0 + 4 * d, ALU.is_equal)
+            mms([(hp, ("LO", u * 128, u * 128 + 128), ("HI", u * 64, u * 64 + 64), False, u == 8 * t + 7) for u in range(u0, u0 + nt)], 8)
+            u0 += nt
+        act(SG, hp, AF.Sign, acc_o=ACC)
+        mm([(ap16, N8F, ACC, True, True)], f32=True)
+        mm([(tp, ID4K, sub(SG, k * 8, k * 8 + 8), False, k == 7) for k in range(8)])
         if not last:
-            for m in (1, 0): ts(sub(SIN, m * 32, m * 32 + 32), sub(SV0, m * 32, m * 32 + 32), A16, ALU.add)
-            ts(V16, VB16, A16, ALU.add)
-        op("dve", lambda: g.vector.tensor_scalar(out=ap(to1), in0=ind(HPS, DL), scalar1=0.5, scalar2=float(W + 128), op0=ALU.is_ge, op1=ALU.mult),
-           [HPS, DL], [to1], gat(16))
-        tt(to2, sub(to1, 0, 8), mo, ALU.add)
-        copy(TOFF[pr], to2)
-        if not last: scatter(("X", 0, NM), TOFF[pr], ("ZL", t * 128, t * 128 + 128))
-        mm([(("BD", i, 128, 16), ("EI", i * 128, i * 128 + 128), sub(DNB, 0, 8), True, True) for i in range(16)])
-        copy(DNR, ("BD", 0, 128))
-        nds = ("NDS", t * 128, t * 128 + 128)
-        ts(nds, ("BD", 0, 128), -1.0, ALU.mult, 1.0, ALU.add)
-        scatter(MAP, MOFF[pr], DNR)
-        ndl = ("NDL", t * 128, t * 128 + 128)
-        send(partner, ndl, nds, "rb%d" % t, 2.0)
+            for c in range(2): ts(sub(SIN, c * 32, c * 32 + 32), sub(SV0, c * 32, c * 32 + 32), ap16, ALU.add)
+            copy(TOFF[pr], tp)
+            scatter(("X", 0, NX), TOFF[pr], ("ZL", t * 128, t * 128 + 128))
+        ts(A16, ap16, 65536.0, ALU.add)
+        nds, ndl = ("NDS", t * 8, t * 8 + 8), ("NDL", t * 8, t * 8 + 8)
+        ts(nds, tp, W - 0.5, ALU.is_ge)
+        send(partner, ndl, nds, "rb%d" % t)
+        if not last: ts(V16, VB16, A16, ALU.add)
         vn = VN[pr]
-        ts(VNs, VBL, A16, ALU.add)
+        ts(VNs, VB, 16.0, ALU.mult, A16, ALU.add)
         ts(vn, VNs, 4, ALU.arith_shift_right, 8191, ALU.bitwise_and)
-        if not last: keys(vn)
-        krep = []
-        for b in range(t + 1):
-            for j in range(b * 4, b * 4 + 4):
-                gather("dve" if j in CFG["hg"][t] else "act", ("HG", j * 256, j * 256 + 256), MAPW, sub(OFF, j * 16, j * 16 + 16))
-            tl = [("HG", b * 1024 + k * 128, b * 1024 + k * 128 + 128) for k in range(8)] + ([ndl] if b == t else [])
-            kp, kb = ("BD", b * 64, b * 64 + 64), sub(KB, b * 64, b * 64 + 64)
-            mm([(kp, x, RHE, n == 0, n == len(tl) - 1) for n, x in enumerate(tl)])
-            ts(kb, kp, 0.5, ALU.is_gt, 8.0, ALU.mult)
-            if not last: tt(sub(CLX, b * 64, b * 64 + 64), sub(CLX, b * 64, b * 64 + 64), kb, ALU.max)
-            krep.append((("D0" if last and b > 1 else "TPB", b * 128, b * 128 + 128), sub(kb, 0, 8), ID, True, True))
-        if not last: scatter(MAP, MOFF[pr], ZERO)
-        mm(krep, p8=True)
-        e = 128 * t + 128
-        f = e // 2 if last else e
-        op("act", lambda f=f: g.scalar.activation(out=T.PB[0:8, KT[1]:KT[1] + f], in_=T.TPB[0:8, 0:f], func=AF.Copy), [("TPB", 0, f)], [sub(KT, 0, f)], dv(f))
+        if not last:
+            keys(vn)
+            scatter(MAP, mol, ZERO)
+        dp, w = ("HP", 256, 264), 8 * t + 8
+        mm([(dp, ID2[q], sub(SG, q, 64, 8), q == 0, q == 7) for q in range(8)])
+        ts(DMS, dp, 255.0, ALU.add)
+        for e0 in (0, 4):
+            hq = ("HP" if e0 == 0 or not last else "Q1", e0 * w, e0 * w + 4 * w)
+            mms([(sub(hq, (e - e0) * w + b * 8, (e - e0) * w + b * 8 + 8), ("G", (b * 8 + e) * 128, (b * 8 + e) * 128 + 128), DMS, True, True)
+                 for e in range(e0, e0 + 4) for b in range(t + 1)], 4)
+            ts(sub(hb1, e0 * w, e0 * w + 4 * w), hq, -0.5 + 2.0 ** -8, ALU.add)
+            ts(sub(hb2, e0 * w, e0 * w + 4 * w), sub(hb1, e0 * w, e0 * w + 4 * w), 1, ALU.bitwise_and)
+            tt(sub(hb3, e0 * w // 2, e0 * w // 2 + 2 * w), sub(hb2, e0 * w, e0 * w + 2 * w), sub(hb2, e0 * w + 2 * w, e0 * w + 4 * w), ALU.max)
+        tt(sub(hb4, 0, 2 * w), sub(hb3, 0, 2 * w), sub(hb3, 2 * w, 4 * w), ALU.max)
+        tt(sub(KBZ, 0, 16 * w, 16), sub(hb4, 0, w), sub(hb4, w, 2 * w), ALU.max)
+        vt = ("Q0" if last else "BD", t * 128, t * 128 + 128)
         if last:
-            op("dve", lambda f=f, e=e: g.vector.tensor_copy(out=T.PB[0:8, KT[1] + f:KT[1] + e], in_=T.D0[0:8, f:e]), [("D0", f, e)], [sub(KT, f, e)], dv(e - f))
-        for bank, lo, hi in ((("TPB", 0, f), ("D0", f, e)) if last else (("TPB", 0, e),)):
-            op("pe", lambda bank=bank, lo=lo, hi=hi: g.tensor.matmul(T[bank][:, lo:hi], T.PB[0:8, EXP[1]:EXP[2]], T.PB[0:8, KT[1] + lo:KT[1] + hi], True, True),
-               [EXP, sub(KT, lo, hi)], [(bank, lo, hi)], (hi - lo) * PEC)
-        act(sub(KRP, 0, f), ("TPB", 0, f), AF.Copy)
-        if last: copy(sub(KRP, f, e), ("D0", f, e))
-        for h in range(2): gather("dve" if CFG["lg"] == h else "act", sub(LG, h * 256, h * 256 + 256), KRP, sub(LRU[pr], h * 16, h * 16 + 16))
-        bw = ("BD", 384, 416)
-        mm([(bw, sel(i), sub(LG, i, 512, 16), i == 0, i == 15) for i in range(16)])
-        frn = FR[nx]
+            mm([(("Q0", 256, 512), ZERO, sub(LH, 0, 256), True, False)])
+            mms([(sub(vt, i, 128, 16), ei(i), ndl, False, False) for i in range(16)], 4)
+        for b in range(t + 1):
+            kp = ("Q0" if last and b > 1 else "BD", b * 128, b * 128 + 128)
+            mm([(kp, sub(KBZ, b * 128, b * 128 + 128), ID, not (last and b > 1), b == 3 if last and b > 1 else b < t)])
+        if not last: mms([(sub(vt, i, 128, 16), ei(i), ndl, False, i == 15) for i in range(16)], 4)
+        e = 128 * t + 128
+        if last:
+            move(sub(KRP, 0, 256), ("BD", 0, 256))
+            move(sub(KRP, 256, 512), ("Q0", 256, 512))
+        else:
+            move(sub(KRP, 0, e), ("BD", 0, e))
+            mm([(("HP", 256 + b * 64, 320 + b * 64), sub(KRP, b * 128, b * 128 + 128), RHE, True, True) for b in range(t + 1)])
+            ts(sub(crk, 0, e // 2), ("HP", 256, 256 + e // 2), 0.5, ALU.is_lt, 200.0, ALU.mult)
+            tt(sub(CR, 0, e // 2), sub(CR, 0, e // 2), sub(crk, 0, e // 2), ALU.min)
+        for h in range(2): gather(None, sub(LG, h * 256, h * 256 + 256), KRP, sub(LRU[pr], h * 16, h * 16 + 16))
+        bw = ("HP", 0, 32)
+        sums(bw, LG)
+        frn = ("YS", 32, 64) if last else FR[nx]
         tt(frn, FRA, bw, ALU.is_gt)
         vcn = ("YS", 0, 32) if last else VC[nx]
         tt(vd, vc, vn, ALU.subtract)
@@ -530,48 +564,80 @@ def rank_program(g, core, T, topo):
         tt(vcn, vd2, vn, ALU.add)
         if not last: vbase(vcn)
 
-    dma(T.yt[:], T.YT[:], [("YT", 0, 256)], [], "st_t", 2.0)
-    copy(("YS", 32, 64), FR[TS % 2])
-    dma(T.ys[:], T.YS[:], [("YS", 0, 64)], [], "st_s", 2.0)
+    dma(T.ys[:], T.YS[:], [("YS", 0, 64)], [], "st_s", 2.4)
+    return ops, used[0]
 
+
+def place(ops, links, first, order):
     n = len(ops)
-    if n not in ORDER:
-        users = [[] for _ in range(n)]
-        for i, o in enumerate(ops):
-            for d in o["deps"]: users[d].append(i)
-        pri = [0.0] * n
-        for i in range(n - 1, -1, -1):
-            best = 0.0
-            for u in users[i]: best = max(best, pri[u] + (HOP if ops[u]["deps"][i] else 0.0))
-            pri[i] = best + ops[i]["dur"] + ops[i]["lat"]
-            if ops[i]["early"]: pri[i] = 400.0 + pri[i] * 0.01
-        busy = {}
-        start = [0.0] * n
-        left = [len(o["deps"]) for o in ops]
-        ready = [i for i in range(n) if left[i] == 0]
-        while ready:
-            i = max(ready, key=lambda j: (pri[j], -j))
-            ready.remove(i)
-            o = ops[i]
-            at = 0.0
-            for d, w in o["deps"].items():
-                e = start[d] + ops[d]["dur"]
-                at = max(at, e + ops[d]["lat"] + HOP if w else e)
-            if o["eng"] != "net":
-                sl = busy.setdefault(o["eng"], [])
-                k = len(sl)
-                while k > 0 and sl[k - 1][1] > at: k -= 1
-                while k < len(sl) and sl[k][0] < at + o["dur"] - 1e-9:
+    busy, choice = {}, {}
+    start, end = [0.0] * n, [0.0] * n
+    for i in order:
+        o = ops[i]
+        at0 = first[i]
+        for j, lag in links[i]:
+            if end[j] + lag > at0: at0 = end[j] + lag
+        best = None
+        for q, du in o["ways"]:
+            at, k = at0, 0
+            if q != "net":
+                sl = busy.setdefault(q, [])
+                k, hi = 0, len(sl)
+                while k < hi:
+                    mid = (k + hi) // 2
+                    if sl[mid][1] > at: hi = mid
+                    else: k = mid + 1
+                while k < len(sl) and sl[k][0] < at + du - 1e-9:
                     at = max(at, sl[k][1])
                     k += 1
-                sl.insert(k, (at, at + o["dur"]))
-            start[i] = at
-            CFG["span"][0] = max(CFG["span"][0], at + o["dur"] + o["lat"])
-            for u in users[i]:
-                left[u] -= 1
-                if left[u] == 0: ready.append(u)
-        ORDER[n] = sorted(range(n), key=lambda i: (start[i], i))
-    order = ORDER[n]
+            if best is None or at + du < best[0] + best[1] - 1e-9: best = (at, du, q, k)
+        at, du, q, k = best
+        if q != "net": busy[q].insert(k, (at, at + du))
+        if o["alts"]: choice[i] = q
+        start[i], end[i] = at, at + du
+    return start, end, choice
+
+
+def schedule(ops, rounds, key=None):
+    n = len(ops)
+    for o in ops: o["ways"] = sorted((o["alts"] or {o["eng"]: o["dur"]}).items())
+    fwd = [[(d, ops[d]["lat"] + HOP if w else 0.0) for d, w in o["deps"].items()] for o in ops]
+    bwd = [[] for _ in range(n)]
+    for i in range(n):
+        for d, lag in fwd[i]: bwd[d].append((i, lag))
+    if key is None:
+        key = [0.0] * n
+        for i in range(n - 1, -1, -1):
+            key[i] = min([key[u] - lag for u, lag in bwd[i]] + [-ops[i]["lat"]]) - ops[i]["dur"]
+    zero, lat = [0.0] * n, [o["lat"] for o in ops]
+    rng = np.random.RandomState(1)
+    best = None
+    for r in range(rounds):
+        if r:
+            key = [float(x) for x in np.array(best[3]) + rng.uniform(0.0, CFG["shake"], n)]
+        key = list(key)
+        for i in range(n):
+            for d, lag in fwd[i]:
+                if key[d] > key[i]: key[i] = key[d]
+        for _ in range(CFG["passes"] if r else 6):
+            start, end, choice = place(ops, fwd, zero, sorted(range(n), key=lambda i: (key[i], i)))
+            span = max(end[i] + lat[i] for i in range(n))
+            if best is None or span < best[0]: best = (span, start, choice, key)
+            back, bend, _c = place(ops, bwd, lat, sorted(range(n), key=lambda i: (-end[i], -i)))
+            key = [-x for x in bend]
+    CFG["span"].append(round(best[0], 1))
+    start = best[1]
+    return sorted(range(n), key=lambda i: (start[i], i)), best[2], best[3]
+
+
+def rank_program(g, core, T, topo):
+    rank = T.rank_of(core)
+    if rank is None:
+        return
+    if "choice" not in PLAN: PLAN["choice"], PLAN["key"] = schedule(build(g, core, rank, T, topo, {})[0], CFG["r1"])[1:]
+    ops, used = build(g, core, rank, T, topo, PLAN["choice"])
+    if "order" not in PLAN: PLAN["order"] = schedule(ops, CFG["r2"], PLAN["key"])[0]
+    order = PLAN["order"]
 
     pos, cnt = {}, {}
     for i in order:
@@ -620,5 +686,5 @@ def rank_program(g, core, T, topo):
         x = o["fn"]()
         if i in num: x.then_inc(T.sem["c_" + q], 1)
     for q in tot: g.sync.wait_ge(T.sem["c_" + q], tot[q])
-    g.sync.wait_ge(T.sem.lsem, used[0])
+    g.sync.wait_ge(T.sem.lsem, used)
     for s in ("st_t", "st_s"): g.sync.wait_ge(T.sem[s], 16)

@@ -9,17 +9,17 @@ KB, KK = 65536.0, 16777216.0
 
 SCRATCH = {
     "X": ("sbuf", [128, NX], "bfloat16"), "MAP": ("sbuf", [128, NMAP], "bfloat16"),
-    "SEL": ("sbuf", [128, 2048], "bfloat16"), "EI": ("sbuf", [128, 2048], "bfloat16"),
-    "SD": ("sbuf", [128, 1024], "bfloat16"), "V0": ("sbuf", [128, 32], "int32"), "THI": ("sbuf", [128, 4], "int32"),
+    "SEL": ("sbuf", [128, 2048], "bfloat16"),
+    "KX": ("sbuf", [128, 1024], "bfloat16"), "SD": ("sbuf", [128, 1024], "bfloat16"), "V0": ("sbuf", [128, 32], "int32"), "THI": ("sbuf", [128, 4], "int32"),
     "ZS": ("sbuf", [128, 384], "bfloat16"), "ZL": ("sbuf", [128, 384], "bfloat16"),
-    "NDS": ("sbuf", [128, 32], "bfloat16"), "NDL": ("sbuf", [128, 32], "bfloat16"),
+    "NDS": ("sbuf", [128, 32], "float32"), "NDL": ("sbuf", [128, 32], "float32"),
     "MVS": ("sbuf", [128, 512], "bfloat16"), "MVL": ("sbuf", [128, 512], "bfloat16"),
     "MOS": ("sbuf", [128, 32], "uint16"), "MOL": ("sbuf", [128, 32], "uint16"),
     "G": ("sbuf", [128, 4096], "bfloat16"), "LO": ("sbuf", [128, 4096], "bfloat16"), "HI": ("sbuf", [128, 2048], "bfloat16"),
     "KEYR": ("sbuf", [128, 512], "float32"),
     "YT": ("sbuf", [128, 256], "float32"), "YS": ("sbuf", [128, 64], "float32"),
-    "PF": ("sbuf", [128, 6000], "float32"), "PI": ("sbuf", [128, 3000], "int32"),
-    "PU": ("sbuf", [128, 1000], "uint16"), "PB": ("sbuf", [128, 14000], "bfloat16"),
+    "PF": ("sbuf", [128, 7000], "float32"), "PI": ("sbuf", [128, 3000], "int32"),
+    "PU": ("sbuf", [128, 1000], "uint16"), "PB": ("sbuf", [128, 18000], "bfloat16"),
 }
 for _t in range(TS): SCRATCH["KSD%d" % _t] = ("sbuf", [128, 1536], "float32")
 PSUM = ("P0", "Q0", "P1", "Q1", "HP", "BD", "TA", "TB")
@@ -29,14 +29,24 @@ QUEUES = ("pe", "dve", "act", "gp")
 SEMAPHORES = (["c_" + q for q in QUEUES] + ["ld_x", "ld_sd", "ld_v", "ld_th", "st_t", "st_s", "lsem"]
               + ["%s%d" % (k, t) for k in ("ro", "rm", "rz", "rb") for t in range(TS)])
 
-CYC, PEC, HOP = 0.00095, 0.00055, 0.14
+CYC, PEC, HOP = 0.00087, 0.00046, 0.14
 PLAN = {}
-CFG = {"cut": ((0, 8), (8, 16)), "batch": ((8,), (16,), (16, 8), (16, 16)), "ldx": 12.0, "net": 2.4, "span": [],
-       "banks": ("TA", "TB"), "turn": 2, "passes": 2, "r1": 100, "r2": 30, "shake": 0.3}
+CFG = {"cut": ((0, 10), (10, 16)), "batch": ((8,), (16,), (16, 8), (16, 16)), "ldx": 5.0, "net": 2.4, "iss": 0.8,
+       "keys": "pe", "dm": "dve", "veto": "pe", "mv": "ends", "toff": "dve", "span": [],
+       "every": 2, "banks": ("TA", "TB"), "turn": 2, "passes": 2, "r1": 400, "r2": 150, "shake": 0.4, "near": 3.0, "kk": 1}
+
+
+def setup():
+    if CFG["veto"] == "pe":
+        for k in ("NDS", "NDL"): SCRATCH[k] = ("sbuf", [128, 32], "bfloat16")
 
 
 def dv(n, c=1.0):
     return max(64, n * c) * CYC
+
+
+def ac(n):
+    return 0.065 + n * CYC
 
 
 def gat(n, eng="dve"):
@@ -164,13 +174,16 @@ def build(g, core, rank, T, topo, choice):
     def act(o, a, f, bias=None, scale=None, acc_o=None):
         rd = [rg(a)] + [rg(r) for r in (bias, scale) if isinstance(r, tuple)]
         op("act", act_call(o, a, f, bias, scale, acc_o), rd, [rg(o)] + ([rg(acc_o)] if acc_o is not None else []),
-           dv(wd(o)) + (0.02 if acc_o is not None else 0.0))
+           ac(wd(o)) + (0.02 if acc_o is not None else 0.0))
 
     def move(o, a, relu=False, scale=None):
         if relu: d, s = ts_call(o, a, 0.0, ALU.max), act_call(o, a, AF.Relu)
         elif scale: d, s = ts_call(o, a, scale, ALU.mult), act_call(o, a, AF.Copy, scale=scale)
         else: d, s = (lambda: g.vector.tensor_copy(out=ap(o), in_=ap(a))), act_call(o, a, AF.Copy)
-        either({"dve": (d, dv(wd(o), fastc(o, a))), "act": (s, dv(wd(o)))}, [rg(a)], [rg(o)])
+        either({"dve": (d, dv(wd(o), fastc(o, a))), "act": (s, ac(wd(o)))}, [rg(a)], [rg(o)])
+
+    def times(o, a, col):
+        either({"dve": (ts_call(o, a, col, ALU.mult), dv(wd(o), fastc(o, a))), "act": (act_call(o, a, AF.Copy, scale=col), ac(wd(o)))}, [a, col], [o])
 
     def mm(lst, f32=False):
         rd, wr = [], []
@@ -200,13 +213,13 @@ def build(g, core, rank, T, topo, choice):
 
     def send(dst, o, i, sem):
         rid, pid, _ = topo.addr(dst)
-        en = topo.engines(core, dst)[::2]
+        en = topo.engines(core, dst)[::CFG["every"]]
         m = sum(1 << e for e in en)
         used[0] += len(en)
 
         def fn():
             g.remote_dma(ap(o), ap(i), T.sem[sem], T.sem.lsem, pid, rid, m)
-        s = op("gp", fn, [rg(i)], [], 0.1)
+        s = op("gp", fn, [rg(i)], [], CFG["iss"] + (0.0 if used[0] > len(en) else 1.0))
         op("net", None, [], [rg(o)], 0.0, event=(sem, len(en)), after=(s,), lat=CFG["net"])
 
     def dma(o_ap, i_ap, rd, wr, sem, lat, eng="sp", after=()):
@@ -231,18 +244,13 @@ def build(g, core, rank, T, topo, choice):
     def sel(i):
         return ("SEL", i * 128, (i + 1) * 128)
 
-    def ei(i):
-        return ("EI", i * 128, (i + 1) * 128)
-
     def scaled(src, c, p="PB"):
         r = al(p, wd(src))
         move(r, src, scale=c)
         return r
-    NID, NID16, ID4K, IDF, N8F = scaled(ID, -1.0), scaled(ID, -16.0), scaled(ID, 4096.0), scaled(ID, 1.0, "PF"), scaled(ONE, -8.0, "PF")
-    ID2 = [scaled(ID, -2.0 ** q) for q in range(8)]
+    NID, NID16, IDH, ID2, N8F = scaled(ID, -1.0), scaled(ID, -16.0), scaled(ID, -0.125), scaled(ID, -0.5), scaled(ONE, -8.0, "PF")
     IDG = [al("PB", 128) for _ in range(8)]
-    for k in range(8): ts(IDG[k], ID, sub(BO, 16 * k, 16 * k + 1), ALU.mult, -2.0 ** -8, ALU.mult)
-    RX = scaled(BO8, -0.25)
+    for k in range(8): ts(IDG[k], ID, sub(BO, 16 * k, 16 * k + 1), ALU.mult, -2.0 ** -10, ALU.mult)
     BIAS = (al("PF", 1), al("PF", 1))
     for m in range(2): fill(BIAS[m], 8.0 * KS[m])
     h1, h2, M16 = al("PF", 64), al("PF", 32), al("PF", 16)
@@ -261,7 +269,7 @@ def build(g, core, rank, T, topo, choice):
     iota(iq, [[16, 32]], 512, 0)
     ts(TL, iq, IC, ALU.add)
     fill(C16B, 16.0)
-    fill(BASE, 2.0 ** -9)
+    fill(BASE, 2.0 ** -11)
     V16 = al("PF", 64)
 
     def v16ops(dst, src):
@@ -286,10 +294,25 @@ def build(g, core, rank, T, topo, choice):
     UT, LT = al("PB", 128), al("PB", 128)
     asel(UT, BO, [[-1, 128]], ALU.is_ge, 0, 1)
     asel(LT, BO, [[1, 128]], ALU.is_gt, 0, -1)
-    for i in range(16): ts(ei(i), BO, m16(i), ALU.mult)
-    EH, EL, LH, LL = scaled(ei(0), 2.0 ** -6), scaled(ei(0), 2.0 ** -10), al("PB", 512), al("PB", 512)
-    iota(LH, [[1, 32], [0, 16]], 0, 0)
-    iota(LL, [[0, 32], [1, 16]], 0, 0)
+    LR, lh, ll = al("PB", 512), al("PB", 512), al("PB", 512)
+    iota(lh, [[1, 32], [0, 16]], 0, 0)
+    iota(ll, [[0, 32], [1, 16]], 0, 0)
+    ts(lh, lh, m16(0), ALU.mult, 2.0 ** -6, ALU.mult)
+    ts(ll, ll, m16(1), ALU.mult, 2.0 ** -10, ALU.mult)
+    for k in range(4): tt(sub(LR, k * 128, k * 128 + 128), sub(lh, k * 128, k * 128 + 128), sub(ll, k * 128, k * 128 + 128), ALU.add)
+    W64 = al("PF", 65)
+    for q in range(8): move(sub(W64, q, 64, 8), BO8, scale=-2.0 ** (q + 2))
+    fill(sub(W64, 64, 65), 1020.0)
+    if "pe" in (CFG["keys"], CFG["veto"]):
+        EI = [al("PB", 128) for _ in range(16)]
+        for i in range(16): times(EI[i], BO, m16(i))
+    if CFG["dm"] == "pe": IDQ = [scaled(ID, -2.0 ** (q + 2)) for q in range(8)]
+    if CFG["mv"] == "list":
+        CLT, CQF = al("PB", 1024), al("PF", 128)
+        iota(CLT, [[-1, 8], [0, 128]], 0, 0)
+        ts(CLT, CLT, 0.25, ALU.mult)
+        iota(CQF, [[-4, 8], [0, 16]], -2, 0)
+        fill(("SD", 512, 1024), 0.0)
     RHE = al("PB", 64)
     for k in range(8): ts(sub(RHE, k * 8, k * 8 + 8), BO8, m16(0), ALU.mult)
     DM, dm1, dm2 = al("PF", 32), al("PF", 16), al("PF", 16)
@@ -306,12 +329,14 @@ def build(g, core, rank, T, topo, choice):
     ts(TRW, i8, IC, ALU.add, -KK, ALU.add)
     iota(SROW, [[1024, 128]], W * 1024 + 896, 0)
     for t in range(TS): move(("KSD%d" % t, 0, 128), SROW, scale=KB)
-    CQ, C2, dd, dr = al("PF", 128), al("PB", 128), al("PF", 16), al("PF", 16)
-    iota(CQ, [[-16, 8], [0, 16]], -8, 0)
-    ts(sub(dr, 0, 8), sub(M16, 8, 16), -2.0 ** 20, ALU.mult)
-    ts(sub(dr, 8, 16), sub(M16, 0, 8), -2.0 ** 20, ALU.mult)
+    CQ, C2, dd, dr, cq, SLH = al("PB", 128), al("PB", 128), al("PF", 16), al("PF", 16), al("PF", 128), al("PF", 128)
+    iota(cq, [[-32, 8], [0, 16]], -23, 0)
+    move(CQ, cq, scale=0.125)
+    ts(SLH, SROW, 1.0 / 1024, ALU.mult, -W - 0.375, ALU.add)
+    ts(sub(dr, 0, 8), sub(ONE, 0, 8), m16(8), ALU.mult, -2.0 ** 20, ALU.mult)
+    ts(sub(dr, 8, 16), sub(ONE, 0, 8), m16(0), ALU.mult, -2.0 ** 20, ALU.mult)
     tt(dd, dr, M16, ALU.add)
-    for q in range(8): move(sub(C2, q * 16, q * 16 + 16), dd, scale=2.0 ** (-q - 1))
+    for q in range(8): move(sub(C2, q * 16, q * 16 + 16), dd, scale=2.0 ** (-q - 3))
     KRP, KBZ, ZERO = al("PB", 512), al("PB", 512), al("PB", 128)
     fill(KRP, 0.0)
     fill(KBZ, 0.0)
@@ -323,9 +348,7 @@ def build(g, core, rank, T, topo, choice):
     tda, tdb = al("PF", 256), al("PF", 256)
     OFF, CR, crk = al("PU", 256), al("PF", 256), al("PF", 256)
     ZG, SQS, VSE, SIS, CS = al("PB", 512), al("PF", 64), al("PF", 64), al("PI", 64), al("PI", 64)
-    AQ, CLT, KKC = al("PB", 128), al("PB", 1024), al("PF", 1)
-    iota(CLT, [[-1, 8], [0, 128]], 0, 0)
-    fill(("SD", 512, 1024), 0.0)
+    AQ, KKC, NC, SGN = al("PB", 128), al("PF", 1), al("PF", 4), al("PB", 512)
     fill(KKC, KK)
     LRF, lr1, lr2, lr3, LRU = two("PF", 32), al("PF", 32), al("PF", 32), al("PF", 32), two("PU", 32)
     LG, WO = al("PB", 512), two("PF", 32)
@@ -341,10 +364,19 @@ def build(g, core, rank, T, topo, choice):
     KJ, KM, KW, MN, MO = al("PF", 128), al("PF", 128), al("PF", 8), al("PF", 8), al("PF", 8)
     AB = al("PF", 8 * 144)
     EXT = sub(AB, 0, 8 * 144, 144)
-    OK, MOF, TOFF = al("PB", 8), al("PF", 8), two("PU", 8)
+    OK, MOF, TP, TOFF, NDX = al("PB", 8), al("PF", 16), al("PF", 16), two("PU", 8), al("PB", 128)
+    fill(MOF, 0.0)
+    c8, c9, g9, dl0, DL = al("PF", 1), al("PF", 1), al("PF", 1), al("PF", 1), al("PU", 1)
+    ts(c8, IC, 7.5, ALU.is_ge, -8.0, ALU.mult)
+    tt(c9, c8, IC, ALU.add)
+    ts(g9, g8, 0.5, ALU.mult)
+    tt(dl0, g9, c9, ALU.add)
+    copy(DL, dl0)
     ZI, ZJ, ZO = al("PI", 8), al("PI", 8), al("PU", 8)
-    YQ = two("PB", 128)
-    SG, ACC, A16, DMS = al("PB", 64), al("PF", 1), al("PF", 1), al("PB", 8)
+    YA, YQ = al("PF", 256), al("PB", 256)
+    SG, ACC, A16, DMS, DMC, sw = al("PB", 65), al("PF", 1), al("PF", 1), al("PB", 8), al("PF", 1), al("PF", 65)
+    fill(sub(SG, 64, 65), 1.0)
+    SG = sub(SG, 0, 64)
     hb1, hb2, hb3, hb4 = al("PI", 256), al("PI", 256), al("PI", 128), al("PI", 64)
 
     def vbase(v):
@@ -360,9 +392,15 @@ def build(g, core, rank, T, topo, choice):
         ts(sub(VD, 0, 32), v, 8064, ALU.bitwise_and)
         ts(sub(VD, 32, 64), v, 127, ALU.bitwise_and)
         copy(VDB, VD)
-        mm([(("BD", 0, 512), EH, LH, True, False)])
-        mm([(("BD", 0, 512), EL, LL, False, False)])
-        mms([(("BD", i, 512, 16), ei(i), sub(VDB, d * 32, d * 32 + 32), False, i == 15 and d == 1) for i in range(16) for d in range(2)], 4)
+        if CFG["keys"] == "pe":
+            mm([(("BD", 0, 512), BO, LR, True, False)])
+            mms([(("BD", i, 512, 16), EI[i], sub(VDB, d * 32, d * 32 + 32), False, i == 15 and d == 1) for i in range(16) for d in range(2)], 4)
+        else:
+            for i in range(16): times(("KX", i, 1024, 16), VDB, m16(i))
+        for h in range(2 * (CFG["keys"] != "pe")):
+            o = ("BD", h * 256, h * 256 + 256)
+            mms([(o, BO, sub(LR, h * 256, h * 256 + 256), True, False), (o, BO, ("KX", h * 256, h * 256 + 256), False, False),
+                 (o, BO, ("KX", 512 + h * 256, 768 + h * 256), False, True)], 1)
         for h in range(2): move(("KEYR", h * 256, h * 256 + 256), ("BD", h * 256, h * 256 + 256), scale=1024.0 * KB)
 
     keys(V0)
@@ -418,15 +456,29 @@ def build(g, core, rank, T, topo, choice):
             copy(sub(SOFF, q0, q1), wo)
             scatter((ksd, 0, 1536), sub(SOFF, q0, q1), ("KEYR", c * 256, c * 256 + 256))
         ks = (ksd, 0, 128)
+        aq = ("P0", 0, 128)
+        ends = CFG["mv"] == "ends"
+        if ends: mm([(aq, ID, CQ, True, False)])
+        for c in range(2 * ends):
+            mm([(("BD", c * 16, c * 16 + 16), BO, sub(HALT, c * 16, c * 16 + 16), True, True)])
+            for k in (2 * c, 2 * c + 1):
+                act(sub(KJ, 0, 8 * k + 8), ("BD", 0, 8 * k + 8), AF.Copy, scale=-1.0, acc_o=sub(NC, k, k + 1))
+                act(sub(SGN, k * 128, k * 128 + 128), SLH, AF.Sign, sub(NC, k, k + 1))
+                mm([(aq, ID2 if k == 3 else IDH, sub(SGN, k * 128, k * 128 + 128), False, k == 3)])
+        mvs, mvl = ("MVS", t * 128, t * 128 + 128), ("MVL", t * 128, t * 128 + 128)
+        if ends:
+            tt(mvs, aq, C2, ALU.max)
+            send(partner, mvl, mvs, "rm%d" % t)
+            move(AQ, aq)
         for k in (3, 2, 1, 0): tt(sub(KM, k * 32, k * 32 + 32), sub(ks, k * 32, k * 32 + 32), DM, ALU.min)
         for q in range(7, -1, -1):
             km, kw = sub(KM, q * 16, q * 16 + 16), sub(KW, q, q + 1)
-            either({"act": (act_call(sub(KJ, q * 16, q * 16 + 16), km, AF.Copy, acc_o=kw), dv(16) + 0.02),
+            either({"act": (act_call(sub(KJ, q * 16, q * 16 + 16), km, AF.Copy, acc_o=kw), ac(16) + 0.02),
                     "dve": (lambda km=km, kw=kw: g.vector.tensor_reduce(out=ap(kw), in_=ap(km), axis=AxisListType.X, op=ALU.add), dv(16))},
                    [km], [kw, sub(KJ, q * 16, q * 16 + 16)])
         for h in (1, 0):
             ex, kw = sub(AB, h * 576, h * 576 + 576, 144), sub(KW, h * 4, h * 4 + 4)
-            either({"act": (act_call(ex, kw, AF.Identity, KKC, -1.0 / (1024.0 * KB)), dv(4)),
+            either({"act": (act_call(ex, kw, AF.Identity, KKC, -1.0 / (1024.0 * KB)), ac(4)),
                     "dve": (ts_call(ex, kw, -1.0 / (1024.0 * KB), ALU.mult, KK, ALU.add), dv(4))}, [kw, KKC], [ex])
         for q in range(7, -1, -1):
             act(sub(AB, q * 144 + 1, q * 144 + 16 * q + 17), sub(ks, 0, 16 * q + 16), AF.Abs, sub(KW, q, q + 1), -1.0)
@@ -435,12 +487,12 @@ def build(g, core, rank, T, topo, choice):
         mos, mol = ("MOS", t * 8, t * 8 + 8), ("MOL", t * 8, t * 8 + 8)
         ts(mos, MO, KK, ALU.add)
         ts(ZI, KW, 1.0 / KB, ALU.mult, 256.0, ALU.add)
-        ts(ZJ, ZI, 1023, ALU.bitwise_and)
+        ts(ZJ, ZI, 511 if ends else 1023, ALU.bitwise_and)
         copy(ZO, ZJ)
-        op("dve", lambda: g.vector.tensor_tensor(out=ap(AQ), in0=ind(CLT, ZO), in1=ap(CQ), op=ALU.add), [CLT, ZO, CQ], [AQ], gat(128))
-        mvs, mvl = ("MVS", t * 128, t * 128 + 128), ("MVL", t * 128, t * 128 + 128)
-        tt(mvs, AQ, C2, ALU.max)
-        send(partner, mvl, mvs, "rm%d" % t)
+        if not ends:
+            op("dve", lambda: g.vector.tensor_tensor(out=ap(AQ), in0=ind(CLT, ZO), in1=ap(CQF), op=ALU.add), [CLT, ZO, CQF], [AQ], gat(128))
+            tt(mvs, AQ, C2, ALU.max)
+            send(partner, mvl, mvs, "rm%d" % t)
         send(partner, mol, mos, "ro%d" % t)
         ts(GO, WO[pr], 127.5, ALU.is_lt)
         if t:
@@ -454,7 +506,7 @@ def build(g, core, rank, T, topo, choice):
             tt(LRF[pr], WO[pr], GO, ALU.mult)
         copy(LRU[pr], LRF[pr])
         for b in range(4):
-            gather(None, sub(ZG, b * 128, b * 128 + 128), ("SD", 0, 1024) if b == 0 else sub(ZH, b * 512 - 512, b * 512 + 512), ZO)
+            gather(None, sub(ZG, b * 128, b * 128 + 128), ("SD", 0, 1024 - 512 * ends) if b == 0 else sub(ZH, b * 512 - 512, b * 512 + 512 - 512 * ends), ZO)
         us = ("BD", 0, 32)
         sums(us, ZG)
         for m in range(2): act(sub(SQS, m * 32, m * 32 + 32), us, AF.Square, BIAS[m])
@@ -466,9 +518,9 @@ def build(g, core, rank, T, topo, choice):
         ts(CS, SIS, 4, ALU.arith_shift_right, 8191, ALU.bitwise_and)
         copy(sub(OFF, t * 64, t * 64 + 64), CS)
         mm([(("BD", 64, 128), AQ, RHE, True, True)])
-        ts(sub(CR, t * 64, t * 64 + 64), ("BD", 64, 128), 0.25, ALU.mult, CQ4, ALU.add)
+        ts(sub(CR, t * 64, t * 64 + 64), ("BD", 64, 128), CQ4, ALU.add)
         if not last:
-            gather(None, ("ZS", t * 128, t * 128 + 128), sub(ZF, 0, 1024), ZO)
+            gather(None, ("ZS", t * 128, t * 128 + 128), sub(ZF, 0, 1024 - 512 * ends), ZO)
             send(partner, ("ZL", t * 128, t * 128 + 128), ("ZS", t * 128, t * 128 + 128), "rz%d" % t)
         if t:
             mms([(("HP", c * 128 + k * 16, c * 128 + k * 16 + 16), ID, sub(fr, c * 16, c * 16 + 16), True, True) for c in range(2) for k in range(8)], 4)
@@ -481,41 +533,46 @@ def build(g, core, rank, T, topo, choice):
                 dma(T.yt[:], T.YT[:], [("YT", 0, 256)], [], "st_t", 2.4)
         scatter(MAP, mol, mvl)
         ts(OK, mol, W - 0.5, ALU.is_lt)
-        ts(MOF, mol, -6.0 * 4096, ALU.add)
-        hp, tp, ap16 = ("HP", 0, 64), ("P1", 0, 8), ("P0", 0, 1)
+        ts(sub(MOF, 0, 8), mol, 1.0 / 4096, ALU.mult, 1.0, ALU.add)
+        hp, ap16 = ("HP", 0, 64), ("P0", 0, 1)
         mm([(hp, ID, BASE, True, False)] + [(sub(hp, k * 8, k * 8 + 8), IDG[k], OK, False, False) for k in range(8)])
-        mm([(tp, IDF, MOF, True, False)], f32=True)
         u0 = 0
         for k, nt in enumerate(CFG["batch"][t]):
+            bymm, nt = nt > 0, abs(nt)
             xs = ("Q%d" % (k % 2), 0, nt * 8)
             for j in range(u0 // 2, (u0 + nt) // 2):
                 gather(None, ("G", j * 256, j * 256 + 256), MAPW, sub(OFF, j * 16, j * 16 + 16))
                 tn = CFG["turn"]
                 bank, c0 = CFG["banks"][j // tn % len(CFG["banks"])], j % tn * 256
                 tiles = [("G", u * 128, u * 128 + 128) for u in (2 * j, 2 * j + 1)]
-                mm([(sub(xs, (2 * j + w - u0) * 8, (2 * j + w - u0) * 8 + 8), tiles[w], RX, True, True) for w in range(2)])
 
                 def turn(tiles=tiles, bank=bank, c0=c0):
                     g.tensor.transpose(T[bank][:, c0:c0 + 128], ap(tiles[0]), ap(ID))
                     return g.tensor.transpose(T[bank][:, c0 + 128:c0 + 256], ap(tiles[1]), ap(ID))
-                if bank[0] == "T": op("pe", turn, tiles + [ID], [(bank, c0, c0 + 256)], 256 * PEC)
-                else: mm([((bank, c0 + w * 128, c0 + w * 128 + 128), tiles[w], ID, True, True) for w in range(2)])
-                if j % tn == tn - 1: move(("LO", j * 256 - c0, j * 256 + 256), (bank, 0, c0 + 256), relu=True)
-            yq = sub(YQ[k % 2], 0, nt * 8)
-            tt(yq, xs, sub(CR, u0 * 8, (u0 + nt) * 8), ALU.add)
+                op("pe", turn, tiles + [ID], [(bank, c0, c0 + 256)], 256 * PEC)
+                if bymm: mm([(sub(xs, (2 * j + w - u0) * 8, (2 * j + w - u0) * 8 + 8), tiles[w], BO8, True, True) for w in range(2)])
+                if j % tn == tn - 1:
+                    a0, a1 = j * 16 - c0 // 16, j * 16 + 16
+                    if not bymm:
+                        tt(sub(YA, a0, a1), sub(CR, a0, a1), (bank, 0, c0 + 256, 16), ALU.subtract)
+                        tt(sub(YQ, a0, a1), sub(YA, a0, a1), (bank, 8, c0 + 256, 16), ALU.subtract)
+                    move(("LO", j * 256 - c0, j * 256 + 256), (bank, 0, c0 + 256), relu=True)
+            yq = sub(YQ, u0 * 8, (u0 + nt) * 8)
+            if bymm: tt(yq, sub(CR, u0 * 8, (u0 + nt) * 8), xs, ALU.subtract)
             for d in range(8): ts(("HI", u0 * 64 + d, (u0 + nt) * 64, 8), yq, 130.0 + 4 * d, ALU.is_equal)
             mms([(hp, ("LO", u * 128, u * 128 + 128), ("HI", u * 64, u * 64 + 64), False, u == 8 * t + 7) for u in range(u0, u0 + nt)], 8)
             u0 += nt
         act(SG, hp, AF.Sign, acc_o=ACC)
         mm([(ap16, N8F, ACC, True, True)], f32=True)
-        mm([(tp, ID4K, sub(SG, k * 8, k * 8 + 8), False, k == 7) for k in range(8)])
+        op("dve", lambda: g.vector.tensor_tensor(out=ap(TP), in0=ind(SG, DL), in1=ap(MOF), op=ALU.add), [SG, DL, MOF], [TP], gat(16))
+        tp = sub(TP, 0, 8)
         if not last:
             for c in range(2): ts(sub(SIN, c * 32, c * 32 + 32), sub(SV0, c * 32, c * 32 + 32), ap16, ALU.add)
-            copy(TOFF[pr], tp)
+            ts(TOFF[pr], tp, 4096.0, ALU.mult)
             scatter(("X", 0, NX), TOFF[pr], ("ZL", t * 128, t * 128 + 128))
         ts(A16, ap16, 65536.0, ALU.add)
         nds, ndl = ("NDS", t * 8, t * 8 + 8), ("NDL", t * 8, t * 8 + 8)
-        ts(nds, tp, W - 0.5, ALU.is_ge)
+        ts(nds, tp, 2.0, ALU.is_ge)
         send(partner, ndl, nds, "rb%d" % t)
         if not last: ts(V16, VB16, A16, ALU.add)
         vn = VN[pr]
@@ -524,9 +581,14 @@ def build(g, core, rank, T, topo, choice):
         if not last:
             keys(vn)
             scatter(MAP, mol, ZERO)
-        dp, w = ("HP", 256, 264), 8 * t + 8
-        mm([(dp, ID2[q], sub(SG, q, 64, 8), q == 0, q == 7) for q in range(8)])
-        ts(DMS, dp, 255.0, ALU.add)
+        w = 8 * t + 8
+        if CFG["dm"] == "pe":
+            mm([(("HP", 256, 264), IDQ[q], sub(SG, q, 64, 8), q == 0, q == 7) for q in range(8)])
+            ts(DMS, ("HP", 256, 264), 1020.0, ALU.add)
+        else:
+            tt(sw, sub(SG, 0, 65), W64, ALU.mult)
+            red(DMC, sw, ALU.add)
+            times(DMS, BO8, DMC)
         for e0 in (0, 4):
             hq = ("HP" if e0 == 0 or not last else "Q1", e0 * w, e0 * w + 4 * w)
             mms([(sub(hq, (e - e0) * w + b * 8, (e - e0) * w + b * 8 + 8), ("G", (b * 8 + e) * 128, (b * 8 + e) * 128 + 128), DMS, True, True)
@@ -536,14 +598,21 @@ def build(g, core, rank, T, topo, choice):
             tt(sub(hb3, e0 * w // 2, e0 * w // 2 + 2 * w), sub(hb2, e0 * w, e0 * w + 2 * w), sub(hb2, e0 * w + 2 * w, e0 * w + 4 * w), ALU.max)
         tt(sub(hb4, 0, 2 * w), sub(hb3, 0, 2 * w), sub(hb3, 2 * w, 4 * w), ALU.max)
         tt(sub(KBZ, 0, 16 * w, 16), sub(hb4, 0, w), sub(hb4, w, 2 * w), ALU.max)
-        vt = ("Q0" if last else "BD", t * 128, t * 128 + 128)
-        if last:
-            mm([(("Q0", 256, 512), ZERO, sub(LH, 0, 256), True, False)])
-            mms([(sub(vt, i, 128, 16), ei(i), ndl, False, False) for i in range(16)], 4)
-        for b in range(t + 1):
-            kp = ("Q0" if last and b > 1 else "BD", b * 128, b * 128 + 128)
-            mm([(kp, sub(KBZ, b * 128, b * 128 + 128), ID, not (last and b > 1), b == 3 if last and b > 1 else b < t)])
-        if not last: mms([(sub(vt, i, 128, 16), ei(i), ndl, False, i == 15) for i in range(16)], 4)
+        if CFG["veto"] == "pe":
+            vt = ("Q0" if last else "BD", t * 128, t * 128 + 128)
+            if last:
+                mm([(("Q0", 256, 512), ZERO, sub(LR, 0, 256), True, False)])
+                mms([(sub(vt, i, 128, 16), EI[i], ndl, False, False) for i in range(16)], 4)
+            for b in range(t + 1):
+                kp = ("Q0" if last and b > 1 else "BD", b * 128, b * 128 + 128)
+                mm([(kp, sub(KBZ, b * 128, b * 128 + 128), ID, not (last and b > 1), b == 3 if last and b > 1 else b < t)])
+            if not last: mms([(sub(vt, i, 128, 16), EI[i], ndl, False, i == 15) for i in range(16)], 4)
+        else:
+            for q in range(8): times(sub(NDX, q * 16, q * 16 + 16), M16, sub(ndl, q, q + 1))
+            for b in range(t + 1):
+                kp = ("Q0" if last and b > 1 else "BD", b * 128, b * 128 + 128)
+                mm([(kp, sub(KBZ, b * 128, b * 128 + 128), ID, True, b < t)])
+            mm([(kp, BO, NDX, False, True)])
         e = 128 * t + 128
         if last:
             move(sub(KRP, 0, 256), ("BD", 0, 256))
@@ -566,6 +635,9 @@ def build(g, core, rank, T, topo, choice):
 
     dma(T.ys[:], T.YS[:], [("YS", 0, 64)], [], "st_s", 2.4)
     return ops, used[0]
+
+
+setup()
 
 
 def place(ops, links, first, order):
@@ -614,7 +686,8 @@ def schedule(ops, rounds, key=None):
     best = None
     for r in range(rounds):
         if r:
-            key = [float(x) for x in np.array(best[3]) + rng.uniform(0.0, CFG["shake"], n)]
+            near = np.abs(np.array(best[1]) - rng.uniform(10.0, best[0])) < CFG["near"]
+            key = [float(x) for x in np.array(best[3]) + rng.uniform(-CFG["shake"], CFG["shake"], n) * near]
         key = list(key)
         for i in range(n):
             for d, lag in fwd[i]:
@@ -622,7 +695,8 @@ def schedule(ops, rounds, key=None):
         for _ in range(CFG["passes"] if r else 6):
             start, end, choice = place(ops, fwd, zero, sorted(range(n), key=lambda i: (key[i], i)))
             span = max(end[i] + lat[i] for i in range(n))
-            if best is None or span < best[0]: best = (span, start, choice, key)
+            if best is None or span <= best[0] + 1e-6: best = (span, start, choice, key if CFG["kk"] else start)
+            if _ == CFG["passes"] - 1 and r: break
             back, bend, _c = place(ops, bwd, lat, sorted(range(n), key=lambda i: (-end[i], -i)))
             key = [-x for x in bend]
     CFG["span"].append(round(best[0], 1))

@@ -5,35 +5,40 @@ W, L, TS = 8192, 512, 4
 KS = (3, 29)
 NMAP = 8464
 NX = W + NMAP
+MID, UP = 4224.0 * 1024, 8448.0 * 1024
 KB, KK = 65536.0, 16777216.0
 
 SCRATCH = {
     "X": ("sbuf", [128, NX], "bfloat16"), "MAP": ("sbuf", [128, NMAP], "bfloat16"),
     "SEL": ("sbuf", [128, 2048], "bfloat16"),
-    "KX": ("sbuf", [128, 1024], "bfloat16"), "SD": ("sbuf", [128, 1024], "bfloat16"), "V0": ("sbuf", [128, 32], "int32"), "THI": ("sbuf", [128, 4], "int32"),
+    "SD": ("sbuf", [128, 512], "bfloat16"), "V0": ("sbuf", [128, 32], "int32"), "THI": ("sbuf", [128, 4], "int32"),
     "ZS": ("sbuf", [128, 384], "bfloat16"), "ZL": ("sbuf", [128, 384], "bfloat16"),
     "NDS": ("sbuf", [128, 32], "float32"), "NDL": ("sbuf", [128, 32], "float32"),
     "MVS": ("sbuf", [128, 512], "bfloat16"), "MVL": ("sbuf", [128, 512], "bfloat16"),
     "MOS": ("sbuf", [128, 32], "uint16"), "MOL": ("sbuf", [128, 32], "uint16"),
     "G": ("sbuf", [128, 4096], "bfloat16"), "LO": ("sbuf", [128, 4096], "bfloat16"), "HI": ("sbuf", [128, 2048], "bfloat16"),
-    "KEYR": ("sbuf", [128, 512], "float32"),
+    "SGL": ("sbuf", [128, 64], "bfloat16"), "KEYR": ("sbuf", [128, 512], "float32"),
     "YT": ("sbuf", [128, 256], "float32"), "YS": ("sbuf", [128, 64], "float32"),
     "PF": ("sbuf", [128, 7000], "float32"), "PI": ("sbuf", [128, 3000], "int32"),
-    "PU": ("sbuf", [128, 1000], "uint16"), "PB": ("sbuf", [128, 18000], "bfloat16"),
+    "PU": ("sbuf", [128, 1000], "uint16"), "PB": ("sbuf", [128, 19000], "bfloat16"),
 }
-for _t in range(TS): SCRATCH["KSD%d" % _t] = ("sbuf", [128, 1536], "float32")
+NK = 17920
+SCRATCH["KSD"] = ("sbuf", [128, NK], "float32")
 PSUM = ("P0", "Q0", "P1", "Q1", "HP", "BD", "TA", "TB")
 for _b in PSUM[:6]: SCRATCH[_b] = ("psum", [128, 512], "float32")
 for _b in PSUM[6:]: SCRATCH[_b] = ("psum", [128, 1024], "bfloat16")
 QUEUES = ("pe", "dve", "act", "gp")
 SEMAPHORES = (["c_" + q for q in QUEUES] + ["ld_x", "ld_sd", "ld_v", "ld_th", "st_t", "st_s", "lsem"]
-              + ["%s%d" % (k, t) for k in ("ro", "rm", "rz", "rb") for t in range(TS)])
+              + ["%s%d" % (k, t) for k in ("ro", "rm", "rz", "rb", "rf", "rc", "rp") for t in range(TS)])
 
-CYC, PEC, HOP = 0.00087, 0.00046, 0.14
+CYC, PEC, HOP = 0.00088, 0.00045, 0.16
 PLAN = {}
-CFG = {"cut": ((0, 10), (10, 16)), "batch": ((8,), (16,), (16, 8), (16, 16)), "ldx": 5.0, "net": 2.4, "iss": 0.8,
-       "keys": "pe", "dm": "dve", "veto": "pe", "mv": "ends", "toff": "dve", "span": [],
-       "every": 2, "banks": ("TA", "TB"), "turn": 2, "passes": 2, "r1": 400, "r2": 150, "shake": 0.4, "near": 3.0, "kk": 1}
+CFG = {"chains": ((0, 16, ((0, 8), (8, 16)), ((0, 8, "P0"), (8, 16, "Q0"))), (16, 32, ((0, 8), (8, 16)), ((0, 8, "P1"), (8, 16, "Q1")))),
+       "perm": 0, "uq": (0, 1, 2, 3, 4), "batch": ((-8,), (16,), (16, -8), (16, 16)), "far": ((), (), (), ()), "post": ((0, 32, "P1", "Q1"),), "ldx": 5.0, "net": 1.8, "iss": 0.45, "first": 2.5, "fine": 8, "vcut": ((0, 16), (16, 32)),
+       "ecut": (((0, 8),), ((0, 8),), ((0, 8),), ((0, 4), (4, 6), (6, 8))),
+       "keys": "pe", "dm": "pe", "veto": "pe", "mv": "ends", "toff": "dve", "span": [],
+       "every": 2, "banks": ("TA", "TB"), "turn": 2, "passes": 2, "r1": 1000, "r2": 350, "shake": 0.8, "near": 1.5, "lean": 0.05,
+       "other": ((1.13, 1.0, 1.0, 0.11, -0.3, 1.0), (1.0, 1.0, 1.0, 0.16, 0.8, 0.97), (0.95, 0.85, 0.8, 0.14, -0.4, 1.1), (1.3, 1.2, 1.3, 0.17, 0.3, 0.8))}
 
 
 def setup():
@@ -46,7 +51,7 @@ def dv(n, c=1.0):
 
 
 def ac(n):
-    return 0.065 + n * CYC
+    return 0.068 + n * CYC
 
 
 def gat(n, eng="dve"):
@@ -72,7 +77,7 @@ def build(g, core, rank, T, topo, choice):
         for r in reads:
             ex = r[0] in PSUM
             for (r2, m, wr) in acc.get(r[0], []):
-                if ex: need(m, ops[m]["eng"] != eng)
+                if ex: need(m, ops[m]["eng"] != eng or wr and meet(r, r2))
                 elif wr and meet(r, r2): need(m, True)
         for r in writes:
             ex = r[0] in PSUM
@@ -80,7 +85,8 @@ def build(g, core, rank, T, topo, choice):
                 if ex: need(m, ops[m]["eng"] != eng)
                 elif meet(r, r2): need(m, True)
         for m in after: need(m, False)
-        ops.append({"eng": eng, "fn": fn, "deps": deps, "dur": dur, "event": event, "lat": lat, "alts": alts})
+        ops.append({"eng": eng, "fn": fn, "deps": deps, "dur": dur, "event": event, "lat": lat, "alts": alts,
+                    "kind": 0 if not any(r[0] in ("PU", "MOS", "MOL", "OFL") for r in reads) or len(reads) < 2 else 2 if writes[0][2] - writes[0][1] > 1024 else 1})
         for r in reads:
             acc.setdefault(r[0], []).append((r, n, False))
         for r in writes:
@@ -148,7 +154,7 @@ def build(g, core, rank, T, topo, choice):
         op("dve", lambda: g.vector.memset(ap(o), v), [], [rg(o)], dv(wd(o), fastc(o)))
 
     def red(o, a, f, neg=False):
-        op("dve", lambda: g.vector.tensor_reduce(out=ap(o), in_=ap(a), axis=AxisListType.X, op=f, negate=neg), [rg(a)], [rg(o)], dv(wd(a)))
+        op("dve", lambda: g.vector.tensor_reduce(out=ap(o), in_=ap(a), axis=AxisListType.X, op=f, negate=neg, apply_absolute_value=neg), [rg(a)], [rg(o)], dv(wd(a)))
 
     def ind(win, off):
         return T[win[0]][:, win[1]:win[2]].indirect(ap(off))
@@ -185,6 +191,15 @@ def build(g, core, rank, T, topo, choice):
     def times(o, a, col):
         either({"dve": (ts_call(o, a, col, ALU.mult), dv(wd(o), fastc(o, a))), "act": (act_call(o, a, AF.Copy, scale=col), ac(wd(o)))}, [a, col], [o])
 
+    cols = {}
+
+    def aff(o, a, s, b):
+        if not isinstance(b, tuple) and b not in cols:
+            cols[b] = al("PF", 1)
+            fill(cols[b], b)
+        col = b if isinstance(b, tuple) else cols[b]
+        either({"dve": (ts_call(o, a, s, ALU.mult, b, ALU.add), dv(wd(o), fastc(o, a))), "act": (act_call(o, a, AF.Identity, col, s), ac(wd(o)))}, [a, col], [o])
+
     def mm(lst, f32=False):
         rd, wr = [], []
         d = 0.0
@@ -213,13 +228,14 @@ def build(g, core, rank, T, topo, choice):
 
     def send(dst, o, i, sem):
         rid, pid, _ = topo.addr(dst)
-        en = topo.engines(core, dst)[::CFG["every"]]
+        en = topo.engines(core, dst)
+        en = {"rm0": en[0::2], "ro0": en[0::2], "rz0": en[1::2]}.get(sem, en)
         m = sum(1 << e for e in en)
         used[0] += len(en)
 
         def fn():
             g.remote_dma(ap(o), ap(i), T.sem[sem], T.sem.lsem, pid, rid, m)
-        s = op("gp", fn, [rg(i)], [], CFG["iss"] + (0.0 if used[0] > len(en) else 1.0))
+        s = op("gp", fn, [rg(i)], [], CFG["iss"] + {"rm0": CFG["first"], "rz0": 1.5}.get(sem, 0.0))
         op("net", None, [], [rg(o)], 0.0, event=(sem, len(en)), after=(s,), lat=CFG["net"])
 
     def dma(o_ap, i_ap, rd, wr, sem, lat, eng="sp", after=()):
@@ -230,7 +246,7 @@ def build(g, core, rank, T, topo, choice):
     dma(T.V0[:], T.v0[:], [], [V0], "ld_v", 2.0, "act")
     d0 = dma(T.SD[:, 0:512], T.sd[:], [], [SD], "ld_sd", 3.0)
     d1 = dma(T.X[:, 0:W], T.x[:], [], [XW], "ld_x", CFG["ldx"], after=(d0,))
-    dma(T.THI[:], T.th[:], [], [THI], "ld_th", CFG["ldx"] + 0.5, after=(d1,))
+    d2 = dma(T.THI[:], T.th[:], [], [THI], "ld_th", CFG["ldx"] + 0.5, after=(d1,))
 
     ONE, BO, t0, ID = al("PB", 128), al("PB", 128), al("PB", 128), al("PB", 128)
     fill(ONE, 1.0)
@@ -248,7 +264,7 @@ def build(g, core, rank, T, topo, choice):
         r = al(p, wd(src))
         move(r, src, scale=c)
         return r
-    NID, NID16, IDH, ID2, N8F = scaled(ID, -1.0), scaled(ID, -16.0), scaled(ID, -0.125), scaled(ID, -0.5), scaled(ONE, -8.0, "PF")
+    NID, NID16, IDH, ID2, N8F = scaled(ID, -1.0), scaled(ID, -8192.0), scaled(ID, -0.125), scaled(ID, -0.5), scaled(ONE, -8.0, "PF")
     IDG = [al("PB", 128) for _ in range(8)]
     for k in range(8): ts(IDG[k], ID, sub(BO, 16 * k, 16 * k + 1), ALU.mult, -2.0 ** -10, ALU.mult)
     BIAS = (al("PF", 1), al("PF", 1))
@@ -264,17 +280,21 @@ def build(g, core, rank, T, topo, choice):
     iota(i16, [[1, 16]], 0, 0)
     tt(x16, M16, i16, ALU.mult)
     red(IC, x16, ALU.add)
-    INI, iq, TL, C16B, BASE = al("PF", 1), al("PF", 32), al("PF", 32), al("PB", 16), al("PB", 64)
+    INI, iq, TL, C16B, BASE = al("PF", 1), al("PF", 32), al("PF", 32), al("PB", 32), al("PB", 64)
     ts(INI, IC, 512.0 - 16.0, ALU.add)
-    iota(iq, [[16, 32]], 512, 0)
+    iota(iq, [[16, 32]], 512 + 8192, 0)
     ts(TL, iq, IC, ALU.add)
     fill(C16B, 16.0)
     fill(BASE, 2.0 ** -11)
     V16 = al("PF", 64)
 
     def v16ops(dst, src):
-        for c in range(2):
-            for m in range(2): ts(sub(dst, c * 32 + m * 16, c * 32 + m * 16 + 16), sub(src, c * 16, c * 16 + 16), 16.0, ALU.mult, -64.0 * KS[m] ** 2, ALU.add)
+        for q0, q1, _g, _d in CH:
+            for m in range(2):
+                o = sub(dst, 2 * q0 + m * (q1 - q0), q0 + q1 + m * (q1 - q0))
+                if src[0] == "V0": ts(o, sub(src, q0, q1), 16.0, ALU.mult, -64.0 * KS[m] ** 2, ALU.add)
+                else: aff(o, sub(src, q0, q1), 16.0, -64.0 * KS[m] ** 2)
+    CH = CFG["chains"]
     v16ops(V16, V0)
 
     def sums(o, zr, extra=None):
@@ -283,12 +303,12 @@ def build(g, core, rank, T, topo, choice):
         mms(lst, 4)
     SQ0, SQ1 = al("PF", 64), al("PF", 64)
     sums(("P0", 0, 32), SD)
-    for c in range(2):
-        for m in range(2): act(sub(SQ0, c * 32 + m * 16, c * 32 + m * 16 + 16), ("P0", c * 16, c * 16 + 16), AF.Square, BIAS[m])
+    for q0, q1, _g, _d in CH:
+        for m in range(2): act(sub(SQ0, 2 * q0 + m * (q1 - q0), q0 + q1 + m * (q1 - q0)), ("P0", q0, q1), AF.Square, BIAS[m])
     ts(SQ1, SQ0, 65536.0, ALU.add)
 
     MAP, MAPW = ("MAP", 0, NMAP), ("MAP", 0, W)
-    for k in range(4): fill(("MAP", k * 2048, k * 2048 + 2048), 0.0)
+    for k in range(16): fill(("MAP", k * 512, k * 512 + 512), 0.0)
     TH = al("PF", 4)
     copy(TH, THI)
     UT, LT = al("PB", 128), al("PB", 128)
@@ -306,7 +326,7 @@ def build(g, core, rank, T, topo, choice):
     if "pe" in (CFG["keys"], CFG["veto"]):
         EI = [al("PB", 128) for _ in range(16)]
         for i in range(16): times(EI[i], BO, m16(i))
-    if CFG["dm"] == "pe": IDQ = [scaled(ID, -2.0 ** (q + 2)) for q in range(8)]
+    if CFG["dm"] != "dve": IDQ = [scaled(ID, -2.0 ** (q + 2)) for q in range(8)]
     if CFG["mv"] == "list":
         CLT, CQF = al("PB", 1024), al("PF", 128)
         iota(CLT, [[-1, 8], [0, 128]], 0, 0)
@@ -315,11 +335,13 @@ def build(g, core, rank, T, topo, choice):
         fill(("SD", 512, 1024), 0.0)
     RHE = al("PB", 64)
     for k in range(8): ts(sub(RHE, k * 8, k * 8 + 8), BO8, m16(0), ALU.mult)
-    DM, dm1, dm2 = al("PF", 32), al("PF", 16), al("PF", 16)
-    ts(dm1, M16, 33554432.0 * KB, ALU.mult, -17.0 * KB, ALU.add)
-    ts(sub(dm2, 1, 16), sub(M16, 0, 15), -KB, ALU.mult)
-    ts(sub(dm2, 0, 1), m16(15), -KB, ALU.mult)
-    for k in range(2): tt(sub(DM, k * 16, k * 16 + 16), dm1, dm2, ALU.add)
+    D0, dm2, OFC, EXC = al("PF", 128), al("PF", 16), al("PF", 1), al("PF", 1)
+    ts(sub(D0, 0, 16), M16, -2.0 * UP * KB, ALU.mult)
+    ts(sub(dm2, 0, 15), sub(M16, 0, 15), UP * KB, ALU.mult)
+    tt(sub(D0, 1, 16), sub(D0, 1, 16), sub(dm2, 0, 15), ALU.add)
+    for k in (16, 32, 64): move(sub(D0, k, 2 * k), sub(D0, 0, k))
+    ts(OFC, m16(15), -UP * KB, ALU.mult, (UP + 256.0) * KB, ALU.add)
+    ts(EXC, m16(15), -UP / 1024, ALU.mult, KK + (UP - MID) / 1024, ALU.add)
     pc, g8, CQ4 = al("PF", 1), al("PF", 1), al("PF", 1)
     iota(pc, [[0, 1]], 0, 1)
     tt(g8, pc, IC, ALU.subtract)
@@ -328,25 +350,27 @@ def build(g, core, rank, T, topo, choice):
     iota(i8, [[16, 8]], W + 129, 0)
     ts(TRW, i8, IC, ALU.add, -KK, ALU.add)
     iota(SROW, [[1024, 128]], W * 1024 + 896, 0)
-    for t in range(TS): move(("KSD%d" % t, 0, 128), SROW, scale=KB)
     CQ, C2, dd, dr, cq, SLH = al("PB", 128), al("PB", 128), al("PF", 16), al("PF", 16), al("PF", 128), al("PF", 128)
     iota(cq, [[-32, 8], [0, 16]], -23, 0)
     move(CQ, cq, scale=0.125)
     ts(SLH, SROW, 1.0 / 1024, ALU.mult, -W - 0.375, ALU.add)
-    ts(sub(dr, 0, 8), sub(ONE, 0, 8), m16(8), ALU.mult, -2.0 ** 20, ALU.mult)
-    ts(sub(dr, 8, 16), sub(ONE, 0, 8), m16(0), ALU.mult, -2.0 ** 20, ALU.mult)
-    tt(dd, dr, M16, ALU.add)
-    for q in range(8): move(sub(C2, q * 16, q * 16 + 16), dd, scale=2.0 ** (-q - 3))
-    KRP, KBZ, ZERO = al("PB", 512), al("PB", 512), al("PB", 128)
+    hot, neg = al("PF", 128), al("PF", 128)
+    for q in range(8): move(sub(hot, q * 16, q * 16 + 16), M16, scale=2.0 ** (-q - 3))
+    for w in range(2): times(sub(neg, w, 128, 2), sub(CQ, w, 128, 2), m16(1 - w))
+    tt(C2, hot, neg, ALU.add)
+    ROW = [[al("PB", 128), al("PB", 128)] for w in range(2)]
+    for w in range(2):
+        for k in range(2): times(ROW[w][k], (IDH, ID2)[k], m16(1 - w))
+    KRP, KBZ, ZERO = al("PB", 512), [al("PB", 512) for _ in range(3)], al("PB", 128)
     fill(KRP, 0.0)
-    fill(KBZ, 0.0)
+    for x in KBZ: fill(x, 0.0)
     fill(ZERO, 0.0)
 
     SQ, SI, C16, Y1, HB = two("PF", 64), two("PI", 64), two("PU", 64), two("PB", 512), two("PB", 512)
     ZH, ZF, GE = al("PB", 1536), al("PB", 512), al("PB", 512)
     CN, TM = two("PI", 256), two("PF", 256)
-    tda, tdb = al("PF", 256), al("PF", 256)
-    OFF, CR, crk = al("PU", 256), al("PF", 256), al("PF", 256)
+    tda, NF, NBIG = al("PF", 256), al("PB", 32), scaled(ID, -16384.0)
+    OFF, CR, crk = al("PU", 256), [al("PF", 64 * t + 64) for t in range(TS)], al("PF", 256)
     ZG, SQS, VSE, SIS, CS = al("PB", 512), al("PF", 64), al("PF", 64), al("PI", 64), al("PI", 64)
     AQ, KKC, NC, SGN = al("PB", 128), al("PF", 1), al("PF", 4), al("PB", 512)
     fill(KKC, KK)
@@ -354,14 +378,16 @@ def build(g, core, rank, T, topo, choice):
     LG, WO = al("PB", 512), two("PF", 32)
     HAL, HTT, GO, FRA, FR = al("PB", 48), al("PF", 48), al("PB", 32), al("PB", 32), two("PB", 32)
     fill(HAL, 0.0)
-    fill(HTT, 0.0)
+    fill(HTT, 8192.0)
     HALT, HT = sub(HAL, 16, 48), sub(HTT, 16, 48)
     dht, SOFF = al("PF", 32), al("PU", 32)
-    vm, vw, vq, vr, VB = (al("PI", 32) for _ in range(5))
+    vm, vw, vq, vr = (al("PI", 32) for _ in range(4))
+    VB = al("PF", 32)
     SV0, SIN = al("PF", 64), al("PI", 64)
     VB16, VN, VNs, VC = al("PF", 64), two("PI", 32), al("PI", 32), two("PI", 32)
     vd, vd2, VD, VDB = al("PF", 32), al("PF", 32), al("PI", 64), al("PB", 64)
-    KJ, KM, KW, MN, MO = al("PF", 128), al("PF", 128), al("PF", 8), al("PF", 8), al("PF", 8)
+    KJ, KM, KS2, MN, MO = al("PF", 128), al("PF", 128), al("PF", 128), al("PF", 8), al("PF", 8)
+    KW = sub(KM, 15, 128, 16)
     AB = al("PF", 8 * 144)
     EXT = sub(AB, 0, 8 * 144, 144)
     OK, MOF, TP, TOFF, NDX = al("PB", 8), al("PF", 16), al("PF", 16), two("PU", 8), al("PB", 128)
@@ -373,11 +399,12 @@ def build(g, core, rank, T, topo, choice):
     tt(dl0, g9, c9, ALU.add)
     copy(DL, dl0)
     ZI, ZJ, ZO = al("PI", 8), al("PI", 8), al("PU", 8)
-    YA, YQ = al("PF", 256), al("PB", 256)
+    YQ, MK, LV, VL, FRB = al("PB", 256), al("PB", 512), al("PB", 512), al("PU", 32), al("PF", 32)
+    w1, w2, w3, w4 = al("PI", 32), al("PI", 32), al("PI", 32), al("PB", 32)
     SG, ACC, A16, DMS, DMC, sw = al("PB", 65), al("PF", 1), al("PF", 1), al("PB", 8), al("PF", 1), al("PF", 65)
     fill(sub(SG, 64, 65), 1.0)
     SG = sub(SG, 0, 64)
-    hb1, hb2, hb3, hb4 = al("PI", 256), al("PI", 256), al("PI", 128), al("PI", 64)
+    hb1, hb2 = al("PI", 256), al("PI", 256)
 
     def vbase(v):
         ts(vm, v, 4095, ALU.bitwise_and)
@@ -401,8 +428,52 @@ def build(g, core, rank, T, topo, choice):
             o = ("BD", h * 256, h * 256 + 256)
             mms([(o, BO, sub(LR, h * 256, h * 256 + 256), True, False), (o, BO, ("KX", h * 256, h * 256 + 256), False, False),
                  (o, BO, ("KX", 512 + h * 256, 768 + h * 256), False, True)], 1)
-        for h in range(2): move(("KEYR", h * 256, h * 256 + 256), ("BD", h * 256, h * 256 + 256), scale=1024.0 * KB)
+        for h in range(2): aff(("KEYR", h * 256, h * 256 + 256), ("BD", h * 256, h * 256 + 256), 1024.0 * KB, -(MID + 256.0) * KB)
 
+    turns = [0]
+    RHX = al("PB", 136)
+    fill(RHX, 0.0)
+    for k in range(8): move(sub(RHX, 8 + 16 * k, 16 + 16 * k), sub(RHE, 0, 8))
+
+    def tile(u):
+        return ("G", u * 128, u * 128 + 128)
+    NB8, FRC, RND = scaled(BO8, -1.0), al("PB", 64), al("PF", 1)
+    fill(FRC, -0.3125)
+    ts(RND, g8, 0.25, ALU.mult, 12582914.0, ALU.add)
+
+    def join(win, off, cr, gb, u0, batches, hp, start, stop):
+        for k, nt in enumerate(batches):
+            new, nt = nt < 0, abs(nt)
+            xs = ("Q%d" % (k % 2), 0, nt * 8)
+            if new: mm([(xs, ID, FRC, True, False), (xs, AQ, RHE, False, False)])
+            j1 = (u0 + nt) // 2
+            for j0 in range(u0 // 2, j1, CFG["turn"]):
+                bank = CFG["banks"][turns[0] % len(CFG["banks"])]
+                turns[0] += 1
+                je = min(j1, j0 + CFG["turn"])
+                for j in range(j0, je):
+                    if u0 + nt + sum(map(abs, batches[k + 1:])) - 2 * j0 <= CFG["fine"]: gather(None, (gb, j * 256, j * 256 + 256), win, sub(off, j * 16, j * 16 + 16))
+                    elif j == j0: gather(None, (gb, j0 * 256, je * 256), win, sub(off, j0 * 16, je * 16))
+                    tiles, c0 = [(gb, u * 128, u * 128 + 128) for u in (2 * j, 2 * j + 1)], (j - j0) * 256
+
+                    def turn(tiles=tiles, bank=bank, c0=c0):
+                        g.tensor.transpose(T[bank][:, c0:c0 + 128], ap(tiles[0]), ap(ID))
+                        return g.tensor.transpose(T[bank][:, c0 + 128:c0 + 256], ap(tiles[1]), ap(ID))
+                    if bank[0] == "T": op("pe", turn, tiles + [ID], [(bank, c0, c0 + 256)], 256 * PEC)
+                    else: mm([((bank, c0 + w * 128, c0 + w * 128 + 128), tiles[w], ID, True, True) for w in range(2)])
+                    mm([(sub(xs, (2 * j + w - u0) * 8, (2 * j + w - u0) * 8 + 8), tiles[w], NB8 if new else BO8, not new, not new or j == j1 - 1 and w == 1) for w in range(2)])
+                move(("LO", j0 * 256, je * 256), (bank, 0, (je - j0) * 256), relu=True)
+            if new:
+                for d in range(8): ts(("HI", u0 * 64 + d, (u0 + nt) * 64, 8), xs, RND, ALU.add, 12582914.0 + 4 * d, ALU.is_equal)
+            else:
+                yq = sub(YQ, u0 * 8, (u0 + nt) * 8)
+                tt(yq, sub(cr, u0 * 8, (u0 + nt) * 8), xs, ALU.subtract)
+                for d in range(8): ts(("HI", u0 * 64 + d, (u0 + nt) * 64, 8), yq, 130.0 + 4 * d, ALU.is_equal)
+            mms([(hp, ("LO", u * 128, u * 128 + 128), ("HI", u * 64, u * 64 + 64), start and not k and u == u0, stop and k == len(batches) - 1 and u == u0 + nt - 1)
+                 for u in range(u0, u0 + nt)], 8)
+            u0 += nt
+
+    MAP2 = ("MAP2", 0, NMAP)
     keys(V0)
     vbase(V0)
 
@@ -410,171 +481,171 @@ def build(g, core, rank, T, topo, choice):
         pr, nx, last = t % 2, (t + 1) % 2, t == TS - 1
         partner = T.cores[rank ^ (1 + t % 7)]
         cn, fr, vc = CN[pr], FR[pr], VC[pr] if t else V0
-        ksd = "KSD%d" % t
+        ksd = "KSD"
         for b in range(4):
             p = b % 2
             zc = SD if b == 0 else sub(ZH, b * 512 - 512, b * 512)
             zn = sub(ZH, b * 512, b * 512 + 512) if b < 3 else ZF
-            for c in range(2):
-                banks = ("P%d" % c, "Q%d" % c)
-                k0, z0 = c * 32, c * 256
-                si = sub(SI[p], k0, k0 + 32)
+            for q0, q1, gcut, dcut in CH:
+                nq, k0, z0 = q1 - q0, 2 * q0, 16 * q0
+                o = (dcut[0][2], 320, 320 + nq)
                 if b:
-                    o = (banks[0], 256, 272)
-                    sums(o, sub(zc, z0, z0 + 256))
-                    for m in (1, 0): act(sub(SQ[p], k0 + m * 16, k0 + m * 16 + 16), o, AF.Square, BIAS[m])
-                    tt(si, sub(SQ[p], k0, k0 + 32), sub(V16, k0, k0 + 32), ALU.add)
-                elif t: si = sub(SIN, k0, k0 + 32)
-                else: tt(si, sub(SQ0, k0, k0 + 32), sub(V16, k0, k0 + 32), ALU.add)
-                cc = sub(cn, c * 128 + b * 32, c * 128 + b * 32 + 32)
-                ts(cc, si, 4, ALU.arith_shift_right, 8191, ALU.bitwise_and)
-                c16 = sub(C16[p], k0, k0 + 32)
-                copy(c16, cc)
-                for h, (c0, c1) in enumerate(CFG["cut"]):
+                    sums(o, sub(zc, z0, 16 * q1))
+                    for m in (1, 0): act(sub(SQ[p], k0 + m * nq, k0 + m * nq + nq), o, AF.Square, BIAS[m])
+                c16 = sub(C16[p], k0, k0 + 2 * nq)
+                for m0, m1 in (((nq, 2 * nq), (0, nq)) if CFG["perm"] and b else ((0, 2 * nq),)):
+                    si = sub(SIN if t and not b else SI[p], k0 + m0, k0 + m1)
+                    if b or not t: tt(si, sub(SQ[p] if b else SQ0, k0 + m0, k0 + m1), sub(V16, k0 + m0, k0 + m1), ALU.add)
+                    cc = sub(cn, 8 * q0 + b * 2 * nq + m0, 8 * q0 + b * 2 * nq + m1)
+                    ts(cc, si, 4, ALU.arith_shift_right, 8191, ALU.bitwise_and)
+                    copy(sub(c16, m0, m1), cc)
+                for c0, c1 in gcut:
                     r0, r1 = z0 + c0 * 16, z0 + c1 * 16
                     yy, hu, o16 = sub(Y1[p], r0, r1), sub(HB[p], r0, r1), sub(c16, c0, c1)
-                    gather("act", yy, XW, sub(c16, 16 + c0, 16 + c1))
+                    gather("act", yy, XW, sub(c16, nq + c0, nq + c1))
                     op("dve", lambda o16=o16, yy=yy, hu=hu: g.vector.tensor_tensor(out=ap(hu), in0=ind(XW, o16), in1=ap(yy), op=ALU.max),
                        [XW, o16, yy], [hu], gat(r1 - r0))
-                    dps = (banks[h], 0, r1 - r0)
+                for c0, c1, bank in dcut:
+                    r0, r1 = z0 + c0 * 16, z0 + c1 * 16
+                    dps = (bank, 0, r1 - r0)
                     mm([(dps, NID, sub(zc, r0, r1), True, False)])
-                    mm([(dps, ID, hu, False, True)])
+                    mm([(dps, ID, sub(HB[p], r0, r1), False, True)])
                     act(sub(zn, r0, r1), dps, AF.Abs)
-                    if b == 3: ts(sub(GE, r0, r1), sub(zn, r0, r1), sub(TH, t, t + 1), ALU.is_ge)
-        for c in range(2):
-            q0, q1 = c * 16, c * 16 + 16
-            o, dl = ("P%d" % c, 256, 272), ("Q%d" % c, 256, 272)
-            sums(o, sub(GE, c * 256, c * 256 + 256), sub(fr, q0, q1) if t else None)
-            ts(sub(HALT, q0, q1), o, 8.5, ALU.is_ge)
-            mm([(dl, ID, C16B, True, False)])
+                    if b == 3: ts(sub(GE, r0, r1), sub(zn, r0, r1), sub(TH, t, t + 1), ALU.is_ge, 1024.0, ALU.mult)
+        aff((ksd, 0, 128), SROW, KB, -(MID + 256.0) * KB)
+        for q0, q1, b0, b1 in CFG["post"]:
+            nq = q1 - q0
+            o, dl = (b0, 320, 320 + nq), (b1, 352, 352 + nq)
+            sums(o, sub(GE, 16 * q0, 16 * q1), sub(fr, q0, q1) if t else None)
+            ts(sub(HALT, q0, q1), o, 8704.0, ALU.is_ge)
+            tt(sub(HT, q0, q1), o, sub(TL, q0, q1), ALU.min)
+            mm([(dl, ID, sub(C16B, 0, nq), True, False)])
             mm([(dl, UT, sub(HALT, q0 - 1, q1 - 1), False, False), (dl, LT, sub(HALT, q0, q1), False, True)])
-            tt(sub(HT, q0, q1), sub(HALT, q0, q1), sub(TL, q0, q1), ALU.mult)
             tt(sub(dht, q0, q1), sub(HT, q0 - 1, q1 - 1), sub(HT, q0, q1), ALU.subtract)
-            ini, wo, da = sub(WO[pr], 15, 16) if c else INI, sub(WO[pr], q0, q1), sub(dht, q0, q1)
+            ini, wo, da = sub(WO[pr], q0 - 1, q0) if q0 else INI, sub(WO[pr], q0, q1), sub(dht, q0, q1)
             op("dve", lambda ini=ini, wo=wo, da=da, dl=dl: g.vector.tensor_tensor_scan(out=ap(wo), data0=ap(da), data1=ap(dl), initial=ap(ini), op0=ALU.add, op1=ALU.add),
                [da, dl, ini], [wo], dv(16))
             copy(sub(SOFF, q0, q1), wo)
-            scatter((ksd, 0, 1536), sub(SOFF, q0, q1), ("KEYR", c * 256, c * 256 + 256))
+            scatter((ksd, 0, NK), sub(SOFF, q0, q1), ("KEYR", 16 * q0, 16 * q1))
         ks = (ksd, 0, 128)
         aq = ("P0", 0, 128)
         ends = CFG["mv"] == "ends"
-        if ends: mm([(aq, ID, CQ, True, False)])
-        for c in range(2 * ends):
-            mm([(("BD", c * 16, c * 16 + 16), BO, sub(HALT, c * 16, c * 16 + 16), True, True)])
-            for k in (2 * c, 2 * c + 1):
-                act(sub(KJ, 0, 8 * k + 8), ("BD", 0, 8 * k + 8), AF.Copy, scale=-1.0, acc_o=sub(NC, k, k + 1))
+        mq = ("Q0", 0, 128)
+        if ends: mm([(aq, ID, CQ, True, False), (mq, ID, C2, True, False)])
+        for c in range(1 * ends):
+            mm([(("BD", 0, 32), BO, HALT, True, True)])
+            for k in range(4):
+                act(sub(KJ, 32 * k, 40 * k + 8), ("BD", 0, 8 * k + 8), AF.Copy, scale=-1.0, acc_o=sub(NC, k, k + 1))
                 act(sub(SGN, k * 128, k * 128 + 128), SLH, AF.Sign, sub(NC, k, k + 1))
+                mm([(sub(mq, w, 128, 2), ROW[w][k == 3], sub(SGN, k * 128 + w, k * 128 + 128, 2), False, k == 3 and w == 1) for w in range(2)])
                 mm([(aq, ID2 if k == 3 else IDH, sub(SGN, k * 128, k * 128 + 128), False, k == 3)])
         mvs, mvl = ("MVS", t * 128, t * 128 + 128), ("MVL", t * 128, t * 128 + 128)
         if ends:
-            tt(mvs, aq, C2, ALU.max)
+            act(mvs, mq, AF.Copy)
             send(partner, mvl, mvs, "rm%d" % t)
-            move(AQ, aq)
-        for k in (3, 2, 1, 0): tt(sub(KM, k * 32, k * 32 + 32), sub(ks, k * 32, k * 32 + 32), DM, ALU.min)
+            if not last: move(AQ, aq)
+        op("dve", lambda ks=ks: g.vector.tensor_tensor_scan(out=ap(KM), data0=ap(D0), data1=ap(ks), initial=0.0, op0=ALU.add, op1=ALU.max), [D0, ks], [KM], dv(128))
+        act(KS2, ks, AF.Identity, OFC)
+        aff(EXT, KW, -1.0 / (1024.0 * KB), EXC)
         for q in range(7, -1, -1):
-            km, kw = sub(KM, q * 16, q * 16 + 16), sub(KW, q, q + 1)
-            either({"act": (act_call(sub(KJ, q * 16, q * 16 + 16), km, AF.Copy, acc_o=kw), ac(16) + 0.02),
-                    "dve": (lambda km=km, kw=kw: g.vector.tensor_reduce(out=ap(kw), in_=ap(km), axis=AxisListType.X, op=ALU.add), dv(16))},
-                   [km], [kw, sub(KJ, q * 16, q * 16 + 16)])
-        for h in (1, 0):
-            ex, kw = sub(AB, h * 576, h * 576 + 576, 144), sub(KW, h * 4, h * 4 + 4)
-            either({"act": (act_call(ex, kw, AF.Identity, KKC, -1.0 / (1024.0 * KB)), ac(4)),
-                    "dve": (ts_call(ex, kw, -1.0 / (1024.0 * KB), ALU.mult, KK, ALU.add), dv(4))}, [kw, KKC], [ex])
-        for q in range(7, -1, -1):
-            act(sub(AB, q * 144 + 1, q * 144 + 16 * q + 17), sub(ks, 0, 16 * q + 16), AF.Abs, sub(KW, q, q + 1), -1.0)
+            ab, kw = sub(AB, q * 144 + 1, q * 144 + 16 * q + 17), sub(KM, q * 16 + 15, q * 16 + 16)
+            if q in CFG["uq"]: act(ab, sub(KS2, 0, 16 * q + 16), AF.Abs, kw, -1.0)
+            else: ts(ab, sub(ks, 0, 16 * q + 16), kw, ALU.subtract, OFC, ALU.add)
             red(sub(MN, q, q + 1), sub(AB, q * 144, q * 144 + 16 * q + 17), ALU.min, True)
         tt(MO, MN, TRW, ALU.min)
         mos, mol = ("MOS", t * 8, t * 8 + 8), ("MOL", t * 8, t * 8 + 8)
         ts(mos, MO, KK, ALU.add)
-        ts(ZI, KW, 1.0 / KB, ALU.mult, 256.0, ALU.add)
-        ts(ZJ, ZI, 511 if ends else 1023, ALU.bitwise_and)
-        copy(ZO, ZJ)
-        if not ends:
-            op("dve", lambda: g.vector.tensor_tensor(out=ap(AQ), in0=ind(CLT, ZO), in1=ap(CQF), op=ALU.add), [CLT, ZO, CQF], [AQ], gat(128))
-            tt(mvs, AQ, C2, ALU.max)
-            send(partner, mvl, mvs, "rm%d" % t)
         send(partner, mol, mos, "ro%d" % t)
         ts(GO, WO[pr], 127.5, ALU.is_lt)
         if t:
             tt(FRA, fr, GO, ALU.add)
-            tt(lr1, WO[pr], LRF[nx], ALU.subtract)
-            ts(lr2, lr1, 128.0 * t, ALU.add)
-            tt(lr3, lr2, GO, ALU.mult)
-            tt(LRF[pr], LRF[nx], lr3, ALU.add)
+            if not last:
+                aff(lr2, WO[pr], 1.0, 128.0 * t)
+                tt(lr3, lr2, GO, ALU.mult)
+                tt(LRF[pr], LRF[nx], lr3, ALU.max)
         else:
             copy(FRA, GO)
             tt(LRF[pr], WO[pr], GO, ALU.mult)
-        copy(LRU[pr], LRF[pr])
-        for b in range(4):
-            gather(None, sub(ZG, b * 128, b * 128 + 128), ("SD", 0, 1024 - 512 * ends) if b == 0 else sub(ZH, b * 512 - 512, b * 512 + 512 - 512 * ends), ZO)
-        us = ("BD", 0, 32)
-        sums(us, ZG)
-        for m in range(2): act(sub(SQS, m * 32, m * 32 + 32), us, AF.Square, BIAS[m])
-        ts(sub(VSE, 0, 8), EXT, -16.0, ALU.mult, 16.0 * KK - 64.0 * KS[0] ** 2, ALU.add)
-        copy(sub(VSE, 8, 16), sub(VSE, 0, 8))
-        copy(sub(VSE, 16, 32), sub(VSE, 0, 16))
-        ts(sub(VSE, 32, 64), sub(VSE, 0, 32), 64.0 * (KS[0] ** 2 - KS[1] ** 2), ALU.add)
-        tt(SIS, SQS, VSE, ALU.add)
-        ts(CS, SIS, 4, ALU.arith_shift_right, 8191, ALU.bitwise_and)
-        copy(sub(OFF, t * 64, t * 64 + 64), CS)
-        mm([(("BD", 64, 128), AQ, RHE, True, True)])
-        ts(sub(CR, t * 64, t * 64 + 64), ("BD", 64, 128), CQ4, ALU.add)
         if not last:
-            gather(None, ("ZS", t * 128, t * 128 + 128), sub(ZF, 0, 1024 - 512 * ends), ZO)
+            copy(LRU[pr], LRF[pr])
+            ts(ZI, KW, 1.0 / KB, ALU.mult, 256.0, ALU.add)
+            ts(ZJ, ZI, 511, ALU.bitwise_and)
+            copy(ZO, ZJ)
+            for b in range(4): gather(None, sub(ZG, b * 128, b * 128 + 128), SD if b == 0 else sub(ZH, b * 512 - 512, b * 512), ZO)
+            us = ("BD", 0, 32)
+            sums(us, ZG)
+            for m in range(2): act(sub(SQS, m * 32, m * 32 + 32), us, AF.Square, BIAS[m])
+            aff(sub(VSE, 0, 8), EXT, -16.0, 16.0 * KK - 64.0 * KS[0] ** 2)
+            move(sub(VSE, 8, 16), sub(VSE, 0, 8))
+            move(sub(VSE, 16, 32), sub(VSE, 0, 16))
+            aff(sub(VSE, 32, 64), sub(VSE, 0, 32), 1.0, 64.0 * (KS[0] ** 2 - KS[1] ** 2))
+            tt(SIS, SQS, VSE, ALU.add)
+            ts(CS, SIS, 4, ALU.arith_shift_right, 8191, ALU.bitwise_and)
+            copy(sub(OFF, t * 64, t * 64 + 64), CS)
+            mm([(("BD", 64, 128), AQ, RHE, True, True)])
+            aff(sub(CR[t], t * 64, t * 64 + 64), ("BD", 64, 128), 1.0, CQ4)
+            gather(None, ("ZS", t * 128, t * 128 + 128), ZF, ZO)
             send(partner, ("ZL", t * 128, t * 128 + 128), ("ZS", t * 128, t * 128 + 128), "rz%d" % t)
+        else:
+            mms([(("BD", i, 512, 16), EI[i], FRA, True, True) for i in range(16)], 4)
+            for k in range(4): move(sub(LG, k * 128, k * 128 + 128), ("BD", k * 128, k * 128 + 128), scale=200.0 - k)
+            mm([(("P0", 128 + k // 2 * 128, 256 + k // 2 * 128), sub(LG, k * 128, k * 128 + 128), sub(RHX, 8 - k % 2 * 8, 136 - k % 2 * 8), k % 2 == 0, k % 2 == 1) for k in range(4)])
+            aff(CR[t], ("P0", 128, 384), 0.25, 77.6875)
+            copy(w1, WO[pr])
+            ts(w2, w1, 4, ALU.arith_shift_right, 7, ALU.bitwise_and)
+            ts(VL, w2, g9, ALU.add)
+            ts(w3, w1, 15, ALU.bitwise_and)
+            ts(lr1, GO, -16.0, ALU.mult, 16.0, ALU.add)
+            tt(w4, w3, lr1, ALU.add)
+            mms([(("BD", i, 512, 16), EI[i], w4, True, True) for i in range(16)], 4)
+            for h in range(2): ts(sub(MK, h * 256, h * 256 + 256), ("BD", h * 256, h * 256 + 256), IC, ALU.is_equal)
+            ts(lr2, fr, 5.5, ALU.mult, -5.0, ALU.add)
+            ts(lr3, GO, 4.5, ALU.mult)
+            tt(FRB, lr2, lr3, ALU.add)
         if t:
-            mms([(("HP", c * 128 + k * 16, c * 128 + k * 16 + 16), ID, sub(fr, c * 16, c * 16 + 16), True, True) for c in range(2) for k in range(8)], 4)
-            tt(tda, TM[nx] if t > 1 else CN[0], cn, ALU.subtract)
-            tt(tdb, ("HP", 0, 256), tda, ALU.mult)
-            tt(TM[pr], tdb, cn, ALU.add)
+            for h, (x, sg) in enumerate(((fr, fr), (NF, NF))):
+                mms([(("HP", h * 256 + 8 * q0 + e * (q1 - q0), h * 256 + 8 * q0 + (e + 1) * (q1 - q0)), NBIG, sub(x, q0, q1), True, True)
+                     for q0, q1, _g, _d in CH for e in range(8)], 4)
+            tt(tda, ("HP", 256, 512), TM[nx] if t > 1 else CN[0], ALU.add)
+            tt(("HP", 0, 256), ("HP", 0, 256), cn, ALU.add)
+            tt(TM[pr], ("HP", 0, 256), tda, ALU.max)
             if last:
-                for c in range(2):
-                    for e in range(8): move(("YT", e * 32 + c * 16, e * 32 + c * 16 + 16), sub(TM[pr], c * 128 + e * 16, c * 128 + e * 16 + 16))
+                for h in range(2): copy(sub(OFF, h * 128, h * 128 + 128), sub(TM[pr], h * 128, h * 128 + 128))
+                for q0, q1, _g, _d in CH:
+                    for e in range(8): move(("YT", e * 32 + q0, e * 32 + q1), sub(TM[pr], 8 * q0 + e * (q1 - q0), 8 * q0 + (e + 1) * (q1 - q0)))
                 dma(T.yt[:], T.YT[:], [("YT", 0, 256)], [], "st_t", 2.4)
+        far = sum(CFG["far"][t])
+        if far:
+            ps, pl = ("PS", t * 64, t * 64 + 64), ("PL", t * 64, t * 64 + 64)
+            scatter(MAP2, mos, mvs)
+            join(("MAP2", 0, W), ("OFL", t * 128, t * 128 + 128), ("CRL", t * 128, t * 128 + 128), "GW", 0, CFG["far"][t], ("P1", 0, 64), True, True)
+            move(ps, ("P1", 0, 64))
+            send(partner, pl, ps, "rp%d" % t)
+            if not last: scatter(MAP2, mos, ZERO)
         scatter(MAP, mol, mvl)
         ts(OK, mol, W - 0.5, ALU.is_lt)
         ts(sub(MOF, 0, 8), mol, 1.0 / 4096, ALU.mult, 1.0, ALU.add)
         hp, ap16 = ("HP", 0, 64), ("P0", 0, 1)
         mm([(hp, ID, BASE, True, False)] + [(sub(hp, k * 8, k * 8 + 8), IDG[k], OK, False, False) for k in range(8)])
-        u0 = 0
-        for k, nt in enumerate(CFG["batch"][t]):
-            bymm, nt = nt > 0, abs(nt)
-            xs = ("Q%d" % (k % 2), 0, nt * 8)
-            for j in range(u0 // 2, (u0 + nt) // 2):
-                gather(None, ("G", j * 256, j * 256 + 256), MAPW, sub(OFF, j * 16, j * 16 + 16))
-                tn = CFG["turn"]
-                bank, c0 = CFG["banks"][j // tn % len(CFG["banks"])], j % tn * 256
-                tiles = [("G", u * 128, u * 128 + 128) for u in (2 * j, 2 * j + 1)]
-
-                def turn(tiles=tiles, bank=bank, c0=c0):
-                    g.tensor.transpose(T[bank][:, c0:c0 + 128], ap(tiles[0]), ap(ID))
-                    return g.tensor.transpose(T[bank][:, c0 + 128:c0 + 256], ap(tiles[1]), ap(ID))
-                op("pe", turn, tiles + [ID], [(bank, c0, c0 + 256)], 256 * PEC)
-                if bymm: mm([(sub(xs, (2 * j + w - u0) * 8, (2 * j + w - u0) * 8 + 8), tiles[w], BO8, True, True) for w in range(2)])
-                if j % tn == tn - 1:
-                    a0, a1 = j * 16 - c0 // 16, j * 16 + 16
-                    if not bymm:
-                        tt(sub(YA, a0, a1), sub(CR, a0, a1), (bank, 0, c0 + 256, 16), ALU.subtract)
-                        tt(sub(YQ, a0, a1), sub(YA, a0, a1), (bank, 8, c0 + 256, 16), ALU.subtract)
-                    move(("LO", j * 256 - c0, j * 256 + 256), (bank, 0, c0 + 256), relu=True)
-            yq = sub(YQ, u0 * 8, (u0 + nt) * 8)
-            if bymm: tt(yq, sub(CR, u0 * 8, (u0 + nt) * 8), xs, ALU.subtract)
-            for d in range(8): ts(("HI", u0 * 64 + d, (u0 + nt) * 64, 8), yq, 130.0 + 4 * d, ALU.is_equal)
-            mms([(hp, ("LO", u * 128, u * 128 + 128), ("HI", u * 64, u * 64 + 64), False, u == 8 * t + 7) for u in range(u0, u0 + nt)], 8)
-            u0 += nt
+        join(MAPW, OFF, CR[t], "G", far, CFG["batch"][t], hp, False, not far)
+        if far:
+            mm([(hp, ID, pl, False, True)])
+            for j in range(far // 2): gather(None, ("G", j * 256, j * 256 + 256), MAPW, sub(OFF, j * 16, j * 16 + 16))
         act(SG, hp, AF.Sign, acc_o=ACC)
         mm([(ap16, N8F, ACC, True, True)], f32=True)
-        op("dve", lambda: g.vector.tensor_tensor(out=ap(TP), in0=ind(SG, DL), in1=ap(MOF), op=ALU.add), [SG, DL, MOF], [TP], gat(16))
-        tp = sub(TP, 0, 8)
-        if not last:
-            for c in range(2): ts(sub(SIN, c * 32, c * 32 + 32), sub(SV0, c * 32, c * 32 + 32), ap16, ALU.add)
+        if last: send(partner, ("SGL", 0, 64), SG, "rb%d" % t)
+        else:
+            op("dve", lambda: g.vector.tensor_tensor(out=ap(TP), in0=ind(SG, DL), in1=ap(MOF), op=ALU.add), [SG, DL, MOF], [TP], gat(16))
+            tp = sub(TP, 0, 8)
+            for q0, q1, _g, _d in CH: ts(sub(SIN, 2 * q0, 2 * q1), sub(SV0, 2 * q0, 2 * q1), ap16, ALU.add)
             ts(TOFF[pr], tp, 4096.0, ALU.mult)
             scatter(("X", 0, NX), TOFF[pr], ("ZL", t * 128, t * 128 + 128))
         ts(A16, ap16, 65536.0, ALU.add)
-        nds, ndl = ("NDS", t * 8, t * 8 + 8), ("NDL", t * 8, t * 8 + 8)
-        ts(nds, tp, 2.0, ALU.is_ge)
-        send(partner, ndl, nds, "rb%d" % t)
-        if not last: ts(V16, VB16, A16, ALU.add)
+        if not last:
+            nds, ndl = ("NDS", t * 8, t * 8 + 8), ("NDL", t * 8, t * 8 + 8)
+            ts(nds, tp, 2.0, ALU.is_ge)
+            send(partner, ndl, nds, "rb%d" % t)
+            aff(V16, VB16, 1.0, A16)
         vn = VN[pr]
         ts(VNs, VB, 16.0, ALU.mult, A16, ALU.add)
         ts(vn, VNs, 4, ALU.arith_shift_right, 8191, ALU.bitwise_and)
@@ -582,51 +653,65 @@ def build(g, core, rank, T, topo, choice):
             keys(vn)
             scatter(MAP, mol, ZERO)
         w = 8 * t + 8
-        if CFG["dm"] == "pe":
+        if CFG["dm"] == "pe" or last and CFG["dm"] == "end":
             mm([(("HP", 256, 264), IDQ[q], sub(SG, q, 64, 8), q == 0, q == 7) for q in range(8)])
             ts(DMS, ("HP", 256, 264), 1020.0, ALU.add)
         else:
             tt(sw, sub(SG, 0, 65), W64, ALU.mult)
             red(DMC, sw, ALU.add)
             times(DMS, BO8, DMC)
-        for e0 in (0, 4):
-            hq = ("HP" if e0 == 0 or not last else "Q1", e0 * w, e0 * w + 4 * w)
-            mms([(sub(hq, (e - e0) * w + b * 8, (e - e0) * w + b * 8 + 8), ("G", (b * 8 + e) * 128, (b * 8 + e) * 128 + 128), DMS, True, True)
-                 for e in range(e0, e0 + 4) for b in range(t + 1)], 4)
-            ts(sub(hb1, e0 * w, e0 * w + 4 * w), hq, -0.5 + 2.0 ** -8, ALU.add)
-            ts(sub(hb2, e0 * w, e0 * w + 4 * w), sub(hb1, e0 * w, e0 * w + 4 * w), 1, ALU.bitwise_and)
-            tt(sub(hb3, e0 * w // 2, e0 * w // 2 + 2 * w), sub(hb2, e0 * w, e0 * w + 2 * w), sub(hb2, e0 * w + 2 * w, e0 * w + 4 * w), ALU.max)
-        tt(sub(hb4, 0, 2 * w), sub(hb3, 0, 2 * w), sub(hb3, 2 * w, 4 * w), ALU.max)
-        tt(sub(KBZ, 0, 16 * w, 16), sub(hb4, 0, w), sub(hb4, w, 2 * w), ALU.max)
-        if CFG["veto"] == "pe":
-            vt = ("Q0" if last else "BD", t * 128, t * 128 + 128)
-            if last:
-                mm([(("Q0", 256, 512), ZERO, sub(LR, 0, 256), True, False)])
-                mms([(sub(vt, i, 128, 16), EI[i], ndl, False, False) for i in range(16)], 4)
-            for b in range(t + 1):
-                kp = ("Q0" if last and b > 1 else "BD", b * 128, b * 128 + 128)
-                mm([(kp, sub(KBZ, b * 128, b * 128 + 128), ID, not (last and b > 1), b == 3 if last and b > 1 else b < t)])
-            if not last: mms([(sub(vt, i, 128, 16), EI[i], ndl, False, i == 15) for i in range(16)], 4)
-        else:
-            for q in range(8): times(sub(NDX, q * 16, q * 16 + 16), M16, sub(ndl, q, q + 1))
-            for b in range(t + 1):
-                kp = ("Q0" if last and b > 1 else "BD", b * 128, b * 128 + 128)
-                mm([(kp, sub(KBZ, b * 128, b * 128 + 128), ID, True, b < t)])
-            mm([(kp, BO, NDX, False, True)])
+        ecut, run = CFG["ecut"][t], None
+        for k, (e0, e1) in enumerate(ecut):
+            hq = (("HP", "Q1", "Q0")[k % 3] if last else "HP", e0 * w, e1 * w)
+            mms([(sub(hq, (e - e0) * w + b * 8, (e - e0) * w + b * 8 + 8), tile(b // 2 * 16 + 2 * e + b % 2 if last else b * 8 + e), DMS, True, True)
+                 for e in range(e0, e1) for b in range(t + 1)], 4)
+            ts(sub(hb1, e0 * w, e1 * w), hq, -0.5 + 2.0 ** -8, ALU.add)
+            x, n = sub(hb2, e0 * w, e1 * w), e1 - e0
+            ts(x, sub(hb1, e0 * w, e1 * w), 1, ALU.bitwise_and)
+            while n > 1:
+                n //= 2
+                y = sub(KBZ[k], 0, 16 * w, 16) if n == 1 else al("PI", n * w)
+                tt(y, sub(x, 0, n * w), sub(x, n * w, 2 * n * w), ALU.max)
+                x = y
+        if last:
+            for bank, c0 in (("BD", 0), ("P0", 256)): mm([((bank, c0, c0 + 256), ZERO, sub(LR, 0, 256), True, False)])
+            for k in range(len(ecut)):
+                for b in range(4): mm([((("BD", "P0")[b // 2], b * 128, b * 128 + 128), sub(KBZ[k], b * 128, b * 128 + 128), ID, False, k == len(ecut) - 1 and b % 2 == 1)])
+        for b in range((t + 1) * (not last)):
+            kp = ("BD", b * 128, b * 128 + 128)
+            mm([(kp, sub(KBZ[0], b * 128, b * 128 + 128), ID, True, b < t)])
+        if not last: mms([(sub(kp, i, 128, 16), EI[i], ndl, False, i == 15) for i in range(16)], 4)
         e = 128 * t + 128
         if last:
             move(sub(KRP, 0, 256), ("BD", 0, 256))
-            move(sub(KRP, 256, 512), ("Q0", 256, 512))
+            move(sub(KRP, 256, 512), ("P0", 256, 512))
         else:
             move(sub(KRP, 0, e), ("BD", 0, e))
-            mm([(("HP", 256 + b * 64, 320 + b * 64), sub(KRP, b * 128, b * 128 + 128), RHE, True, True) for b in range(t + 1)])
-            ts(sub(crk, 0, e // 2), ("HP", 256, 256 + e // 2), 0.5, ALU.is_lt, 200.0, ALU.mult)
-            tt(sub(CR, 0, e // 2), sub(CR, 0, e // 2), sub(crk, 0, e // 2), ALU.min)
-        for h in range(2): gather(None, sub(LG, h * 256, h * 256 + 256), KRP, sub(LRU[pr], h * 16, h * 16 + 16))
-        bw = ("HP", 0, 32)
-        sums(bw, LG)
+            if t < TS - 2:
+                mm([(("HP", 256 + b * 64, 320 + b * 64), sub(KRP, b * 128, b * 128 + 128), RHE, True, True) for b in range(t + 1)])
+                aff(sub(crk, 0, e // 2), ("HP", 256, 256 + e // 2), -200.0, 200.0)
+                tt(sub(CR[t + 1], 0, e // 2), sub(CR[t], 0, e // 2), sub(crk, 0, e // 2), ALU.min)
+            n8 = 8 * sum(CFG["far"][t + 1])
+            if n8:
+                nxt, a = T.cores[rank ^ (1 + (t + 1) % 7)], t * 128 + 128
+                send(nxt, ("OFL", a, a + n8), sub(OFF, 0, n8), "rf%d" % (t + 1))
+                send(nxt, ("CRL", a, a + n8), sub(CR[t + 1], 0, n8), "rc%d" % (t + 1))
+        for h in range(2 * (not last)): gather(None, sub(LG, h * 256, h * 256 + 256), KRP, sub(LRU[pr], h * 16, h * 16 + 16))
+        bw = ("P1" if last else "HP", 0, 32)
         frn = ("YS", 32, 64) if last else FR[nx]
-        tt(frn, FRA, bw, ALU.is_gt)
+        if last:
+            for c0, c1 in CFG["vcut"]:
+                lv, mk, li = sub(LV, c0 * 16, c1 * 16), sub(MK, c0 * 16, c1 * 16), sub(VL, c0, c1)
+                op("dve", lambda lv=lv, mk=mk, li=li: g.vector.tensor_tensor(out=ap(lv), in0=ind(("SGL", 0, 64), li), in1=ap(mk), op=ALU.mult),
+                   [("SGL", 0, 64), li, mk], [lv], gat(wd(lv)))
+            sums(bw, LV)
+            sums(("HP", 0, 32), KRP)
+            tt(lr1, FRB, bw, ALU.subtract)
+            tt(frn, lr1, ("HP", 0, 32), ALU.is_gt)
+        else:
+            sums(bw, LG)
+            tt(frn, FRA, bw, ALU.is_gt)
+            aff(NF, frn, -1.0, 1.0)
         vcn = ("YS", 0, 32) if last else VC[nx]
         tt(vd, vc, vn, ALU.subtract)
         tt(vd2, vd, frn, ALU.mult)
@@ -662,12 +747,27 @@ def place(ops, links, first, order):
                 while k < len(sl) and sl[k][0] < at + du - 1e-9:
                     at = max(at, sl[k][1])
                     k += 1
-            if best is None or at + du < best[0] + best[1] - 1e-9: best = (at, du, q, k)
+            if best is None or at + du < best[0] + best[1] - CFG["lean"]: best = (at, du, q, k)
         at, du, q, k = best
+        o["at"] = q
         if q != "net": busy[q].insert(k, (at, at + du))
         if o["alts"]: choice[i] = q
         start[i], end[i] = at, at + du
     return start, end, choice
+
+
+def replay(ops, order, start, end, slow, ga, sc, hop, late, norm):
+    free, fin = {}, [0.0] * len(ops)
+    for i in order:
+        o = ops[i]
+        q = o["at"]
+        at = free.get(q, 0.0)
+        for d, w in o["deps"].items():
+            e = fin[d] + (ops[d]["lat"] + hop + (late if ops[d]["at"] == "net" else 0.0) if w else 0.0)
+            if e > at: at = e
+        fin[i] = at + (end[i] - start[i]) * (slow * (1.0, ga, sc)[o["kind"]] if q in ("pe", "dve", "act") else 1.0)
+        if q != "net": free[q] = fin[i]
+    return max(fin[i] + ops[i]["lat"] for i in order) * norm
 
 
 def schedule(ops, rounds, key=None):
@@ -695,7 +795,10 @@ def schedule(ops, rounds, key=None):
         for _ in range(CFG["passes"] if r else 6):
             start, end, choice = place(ops, fwd, zero, sorted(range(n), key=lambda i: (key[i], i)))
             span = max(end[i] + lat[i] for i in range(n))
-            if best is None or span <= best[0] + 1e-6: best = (span, start, choice, key if CFG["kk"] else start)
+            if best is None or span < best[0] + 1.0:
+                order = sorted(range(n), key=lambda i: (start[i], i))
+                span = (span + sum(replay(ops, order, start, end, *m) for m in CFG["other"])) / (1 + len(CFG["other"]))
+                if best is None or span <= best[0] + 1e-6: best = (span, start, choice, key)
             if _ == CFG["passes"] - 1 and r: break
             back, bend, _c = place(ops, bwd, lat, sorted(range(n), key=lambda i: (-end[i], -i)))
             key = [-x for x in bend]

@@ -7,20 +7,23 @@ NMAP = 8464
 NX = W + NMAP
 MID, UP = 4224.0 * 1024, 8448.0 * 1024
 KB, KK = 65536.0, 16777216.0
+RM0 = 12582912.0
 
 SCRATCH = {
     "X": ("sbuf", [128, NX], "bfloat16"), "MAP": ("sbuf", [128, NMAP], "bfloat16"),
-    "SEL": ("sbuf", [128, 2048], "bfloat16"),
     "SD": ("sbuf", [128, 512], "bfloat16"), "V0": ("sbuf", [128, 32], "int32"), "THI": ("sbuf", [128, 4], "int32"),
-    "ZS": ("sbuf", [128, 384], "bfloat16"), "ZL": ("sbuf", [128, 384], "bfloat16"),
-    "NDS": ("sbuf", [128, 32], "float32"), "NDL": ("sbuf", [128, 32], "float32"),
+    "ZS": ("sbuf", [128, 384], "bfloat16"), "ZL": ("sbuf", [128, 896], "bfloat16"),
+    "NDS": ("sbuf", [128, 32], "bfloat16"), "NDL": ("sbuf", [128, 32], "bfloat16"),
     "MVS": ("sbuf", [128, 512], "bfloat16"), "MVL": ("sbuf", [128, 512], "bfloat16"),
-    "MOS": ("sbuf", [128, 32], "uint16"), "MOL": ("sbuf", [128, 32], "uint16"),
+    "NCS": ("sbuf", [128, 16], "float32"), "NCL": ("sbuf", [128, 16], "float32"),
+    "MOS": ("sbuf", [128, 48], "uint16"), "MOL": ("sbuf", [128, 48], "uint16"),
     "G": ("sbuf", [128, 4096], "bfloat16"), "LO": ("sbuf", [128, 4096], "bfloat16"), "HI": ("sbuf", [128, 2048], "bfloat16"),
     "SGL": ("sbuf", [128, 64], "bfloat16"), "KEYR": ("sbuf", [128, 512], "float32"),
     "YT": ("sbuf", [128, 256], "float32"), "YS": ("sbuf", [128, 64], "float32"),
-    "PF": ("sbuf", [128, 7000], "float32"), "PI": ("sbuf", [128, 3000], "int32"),
-    "PU": ("sbuf", [128, 1000], "uint16"), "PB": ("sbuf", [128, 19000], "bfloat16"),
+    "PF": ("sbuf", [128, 6300], "float32"), "PI": ("sbuf", [128, 2700], "int32"),
+    "PU": ("sbuf", [128, 900], "uint16"), "PB": ("sbuf", [128, 20200], "bfloat16"),
+    "GW1": ("sbuf", [128, 1024], "bfloat16"), "GW2": ("sbuf", [128, 1536], "bfloat16"), "GW3": ("sbuf", [128, 2048], "bfloat16"), "OFL": ("sbuf", [128, 384], "uint16"), "CRL": ("sbuf", [128, 384], "float32"),
+    "PS": ("sbuf", [128, 192], "bfloat16"), "PL": ("sbuf", [128, 192], "bfloat16"),
 }
 NK = 17920
 SCRATCH["KSD"] = ("sbuf", [128, NK], "float32")
@@ -29,21 +32,18 @@ for _b in PSUM[:6]: SCRATCH[_b] = ("psum", [128, 512], "float32")
 for _b in PSUM[6:]: SCRATCH[_b] = ("psum", [128, 1024], "bfloat16")
 QUEUES = ("pe", "dve", "act", "gp")
 SEMAPHORES = (["c_" + q for q in QUEUES] + ["ld_x", "ld_sd", "ld_v", "ld_th", "st_t", "st_s", "lsem"]
-              + ["%s%d" % (k, t) for k in ("ro", "rm", "rz", "rb", "rf", "rc", "rp") for t in range(TS)])
+              + ["%s%d" % (k, t) for k in ("ro", "rm", "rz", "rb", "rf", "rc", "rp", "rg", "rx", "ry") for t in range(TS)])
 
 CYC, PEC, HOP = 0.00088, 0.00045, 0.16
 PLAN = {}
 CFG = {"chains": ((0, 16, ((0, 8), (8, 16)), ((0, 8, "P0"), (8, 16, "Q0"))), (16, 32, ((0, 8), (8, 16)), ((0, 8, "P1"), (8, 16, "Q1")))),
-       "perm": 0, "uq": (0, 1, 2, 3, 4), "batch": ((-8,), (16,), (16, -8), (16, 16)), "far": ((), (), (), ()), "post": ((0, 32, "P1", "Q1"),), "ldx": 5.0, "net": 1.8, "iss": 0.45, "first": 2.5, "fine": 8, "vcut": ((0, 16), (16, 32)),
-       "ecut": (((0, 8),), ((0, 8),), ((0, 8),), ((0, 4), (4, 6), (6, 8))),
-       "keys": "pe", "dm": "pe", "veto": "pe", "mv": "ends", "toff": "dve", "span": [],
-       "every": 2, "banks": ("TA", "TB"), "turn": 2, "passes": 2, "r1": 1000, "r2": 350, "shake": 0.8, "near": 1.5, "lean": 0.05,
-       "other": ((1.13, 1.0, 1.0, 0.11, -0.3, 1.0), (1.0, 1.0, 1.0, 0.16, 0.8, 0.97), (0.95, 0.85, 0.8, 0.14, -0.4, 1.1), (1.3, 1.2, 1.3, 0.17, 0.3, 0.8))}
-
-
-def setup():
-    if CFG["veto"] == "pe":
-        for k in ("NDS", "NDL"): SCRATCH[k] = ("sbuf", [128, 32], "bfloat16")
+       "uq": (0, 1, 2, 3, 4), "early": (), "zall": (0,), "cnt": ("HP", "BD"), "kcut": 4, "lcut": 4, "hat": 32, "tbank": "Q0", "tcut": ((0, 256),), "late": False, "far": ((), (), (), ()), "glat": 2.0,
+       "batch": (((4, "n", 2), (4, "r", 1)), ((12, "o", 2), (4, "r", 1)), ((16, "o", 4), (8, "n", 2)), ((16, "o", 4), (16, "o", 2))),
+       "ldx": 5.0, "net": 0.95, "iss": 0.45, "first": 2.5, "vcut": ((0, 16), (16, 32)),
+       "ecut": (((0, 8),), ((0, 8),), ((0, 8),), ((0, 4), (4, 6), (6, 8))), "span": [],
+       "banks": ("TA", "TB"), "turn": 2, "passes": 2, "r1": 40, "p1": 36000, "p2": 6000, "load": (0.0, -2.0, 1.0, -1.5, -1.0, 0.5), "calm": 120, "side": 0.5, "shake": 0.8, "near": 1.5, "lean": 0.05,
+       "other": ((0.95, 1.0, 1.0, 0.18, -0.3, 1.0), (1.18, 0.77, 0.66, 0.12, 0.2, 1.0), (1.32, 1.2, 1.3, 0.15, -0.2, 0.8),
+                 (1.32, 0.77, 0.47, 0.10, 0.3, 1.0), (1.09, 1.28, 0.6, 0.2, 0.8, 0.9))}
 
 
 def dv(n, c=1.0):
@@ -86,7 +86,7 @@ def build(g, core, rank, T, topo, choice):
                 elif meet(r, r2): need(m, True)
         for m in after: need(m, False)
         ops.append({"eng": eng, "fn": fn, "deps": deps, "dur": dur, "event": event, "lat": lat, "alts": alts,
-                    "kind": 0 if not any(r[0] in ("PU", "MOS", "MOL", "OFL") for r in reads) or len(reads) < 2 else 2 if writes[0][2] - writes[0][1] > 1024 else 1})
+                    "kind": 0 if not any(r[0] in ("PU", "MOS", "MOL") for r in reads) or len(reads) < 2 else 2 if writes[0][2] - writes[0][1] > 1024 else 1})
         for r in reads:
             acc.setdefault(r[0], []).append((r, n, False))
         for r in writes:
@@ -156,6 +156,10 @@ def build(g, core, rank, T, topo, choice):
     def red(o, a, f, neg=False):
         op("dve", lambda: g.vector.tensor_reduce(out=ap(o), in_=ap(a), axis=AxisListType.X, op=f, negate=neg, apply_absolute_value=neg), [rg(a)], [rg(o)], dv(wd(a)))
 
+    def scan(o, a, b, ini, f0, f1):
+        op("dve", lambda: g.vector.tensor_tensor_scan(out=ap(o), data0=ap(a), data1=ap(b), initial=ap(ini) if isinstance(ini, tuple) else ini, op0=f0, op1=f1),
+           [a, b] + [ini] * isinstance(ini, tuple), [o], dv(wd(o)))
+
     def ind(win, off):
         return T[win[0]][:, win[1]:win[2]].indirect(ap(off))
 
@@ -167,6 +171,9 @@ def build(g, core, rank, T, topo, choice):
                 "dve": (lambda: g.vector.tensor_copy(out=ap(o), in_=ind(win, off)), gat(wd(o)))}
         if eng: op(eng, alts[eng][0], [rg(win), rg(off)], [rg(o)], alts[eng][1])
         else: either(alts, [rg(win), rg(off)], [rg(o)])
+
+    def gtt(o, win, off, b, f):
+        op("dve", lambda: g.vector.tensor_tensor(out=ap(o), in0=ind(win, off), in1=ap(b), op=f), [win, off, b], [o], gat(wd(o)))
 
     def act_call(o, a, f, bias=None, scale=None, acc_o=None):
         def fn():
@@ -229,14 +236,14 @@ def build(g, core, rank, T, topo, choice):
     def send(dst, o, i, sem):
         rid, pid, _ = topo.addr(dst)
         en = topo.engines(core, dst)
-        en = {"rm0": en[0::2], "ro0": en[0::2], "rz0": en[1::2]}.get(sem, en)
+        if not CFG["zall"]: en = {"rm0": en[0::2], "ro0": en[0::2], "rz0": en[1::2]}.get(sem, en)
         m = sum(1 << e for e in en)
         used[0] += len(en)
 
         def fn():
             g.remote_dma(ap(o), ap(i), T.sem[sem], T.sem.lsem, pid, rid, m)
-        s = op("gp", fn, [rg(i)], [], CFG["iss"] + {"rm0": CFG["first"], "rz0": 1.5}.get(sem, 0.0))
-        op("net", None, [], [rg(o)], 0.0, event=(sem, len(en)), after=(s,), lat=CFG["net"])
+        s = op("gp", fn, [rg(i)], [], CFG["iss"] + ({"ry0": CFG["first"] + 1.5} if CFG["zall"] else {"rm0": CFG["first"], "rz0": 1.5}).get(sem, 0.0))
+        op("net", None, [], [rg(o)], 0.0, event=(sem, len(en)), after=(s,), lat=CFG["net"] + CFG["glat"] * (sem[:2] == "rg"))
 
     def dma(o_ap, i_ap, rd, wr, sem, lat, eng="sp", after=()):
         return op(eng, lambda: (g.sync if eng == "sp" else g.scalar).dma_start(o_ap, i_ap).then_inc(T.sem[sem], 16), rd, wr, 0.1,
@@ -244,21 +251,22 @@ def build(g, core, rank, T, topo, choice):
 
     V0, THI, SD, XW = ("V0", 0, 32), ("THI", 0, 4), ("SD", 0, 512), ("X", 0, W)
     dma(T.V0[:], T.v0[:], [], [V0], "ld_v", 2.0, "act")
-    d0 = dma(T.SD[:, 0:512], T.sd[:], [], [SD], "ld_sd", 3.0)
+    d0 = dma(T.SD[:, 0:512], T.sd[:], [], [SD], "ld_sd", 2.0)
     d1 = dma(T.X[:, 0:W], T.x[:], [], [XW], "ld_x", CFG["ldx"], after=(d0,))
-    d2 = dma(T.THI[:], T.th[:], [], [THI], "ld_th", CFG["ldx"] + 0.5, after=(d1,))
+    dma(T.THI[:], T.th[:], [], [THI], "ld_th", CFG["ldx"] + 0.5, after=(d1,))
 
-    ONE, BO, t0, ID = al("PB", 128), al("PB", 128), al("PB", 128), al("PB", 128)
+    ONE, BO, t0, t8, ID, BO8, YW = al("PB", 128), al("PB", 128), al("PB", 128), al("PB", 8), al("PB", 128), al("PB", 8), al("PB", 144)
     fill(ONE, 1.0)
+    fill(YW, 0.0)
+    asel(t8, sub(ONE, 0, 8), [[-16, 8]], ALU.is_ge, 0, 1)
+    asel(BO8, t8, [[16, 8]], ALU.is_ge, 15, -1)
+    copy(sub(YW, 15, 143, 16), BO8)
+    asel(ID, ONE, [[-1, 128]], ALU.is_equal, 0, 1)
     asel(t0, ONE, [[-16, 8], [0, 16]], ALU.is_ge, 0, 1)
     asel(BO, t0, [[16, 8], [0, 16]], ALU.is_ge, 15, -1)
-    asel(ID, ONE, [[-1, 128]], ALU.is_equal, 0, 1)
-    BO8 = sub(BO, 0, 128, 16)
-    fill(("SEL", 0, 2048), 0.0)
-    for i in range(16): copy(("SEL", i * 128 + i, (i + 1) * 128, 16), sub(BO, i, 128, 16))
 
     def sel(i):
-        return ("SEL", i * 128, (i + 1) * 128)
+        return sub(YW, 15 - i, 143 - i)
 
     def scaled(src, c, p="PB"):
         r = al(p, wd(src))
@@ -266,7 +274,7 @@ def build(g, core, rank, T, topo, choice):
         return r
     NID, NID16, IDH, ID2, N8F = scaled(ID, -1.0), scaled(ID, -8192.0), scaled(ID, -0.125), scaled(ID, -0.5), scaled(ONE, -8.0, "PF")
     IDG = [al("PB", 128) for _ in range(8)]
-    for k in range(8): ts(IDG[k], ID, sub(BO, 16 * k, 16 * k + 1), ALU.mult, -2.0 ** -10, ALU.mult)
+    for k in range(8): ts(IDG[k], ID, sub(BO8, k, k + 1), ALU.mult, -2.0 ** -10, ALU.mult)
     BIAS = (al("PF", 1), al("PF", 1))
     for m in range(2): fill(BIAS[m], 8.0 * KS[m])
     h1, h2, M16 = al("PF", 64), al("PF", 32), al("PF", 16)
@@ -280,11 +288,13 @@ def build(g, core, rank, T, topo, choice):
     iota(i16, [[1, 16]], 0, 0)
     tt(x16, M16, i16, ALU.mult)
     red(IC, x16, ALU.add)
-    INI, iq, TL, C16B, BASE = al("PF", 1), al("PF", 32), al("PF", 32), al("PB", 32), al("PB", 64)
-    ts(INI, IC, 512.0 - 16.0, ALU.add)
-    iota(iq, [[16, 32]], 512 + 8192, 0)
-    ts(TL, iq, IC, ALU.add)
-    fill(C16B, 16.0)
+    INI, iq, TL, C64, BASE, c32 = al("PF", 1), al("PF", 32), al("PF", 32), al("PB", 64), al("PB", 64), al("PF", 1)
+    ts(INI, IC, 32.0, ALU.mult, 511.0, ALU.add)
+    ts(c32, IC, 32.0, ALU.mult)
+    iota(iq, [[1, 32]], 512 + 8192, 0)
+    ts(TL, iq, c32, ALU.add)
+    fill(sub(C64, 0, 32), 0.0)
+    fill(sub(C64, 32, 64), 1.0)
     fill(BASE, 2.0 ** -11)
     V16 = al("PF", 64)
 
@@ -297,44 +307,48 @@ def build(g, core, rank, T, topo, choice):
     CH = CFG["chains"]
     v16ops(V16, V0)
 
-    def sums(o, zr, extra=None):
-        lst = [(o, NID16, extra, True, False)] if extra is not None else []
-        for i in range(16): lst.append((o, sel(i), sub(zr, i, wd(zr), 16), extra is None and i == 0, i == 15))
-        mms(lst, 4)
+    def sums(o, zr):
+        mms([(o, sel(i), sub(zr, i, wd(zr), 16), i == 0, i == 15) for i in range(16)], 4)
+
+    def lanes(o, zr, c0, c1, own, stop):
+        mms([(sub(o, c // 16, 32, 2), sel(c % 16), sub(zr, 16 * c, 16 * c + 16), own and c % 16 == 0, own and c % 16 == 15 or stop and c == c1 - 1)
+             for c in range(c0, c1)], 4)
     SQ0, SQ1 = al("PF", 64), al("PF", 64)
     sums(("P0", 0, 32), SD)
     for q0, q1, _g, _d in CH:
         for m in range(2): act(sub(SQ0, 2 * q0 + m * (q1 - q0), q0 + q1 + m * (q1 - q0)), ("P0", q0, q1), AF.Square, BIAS[m])
     ts(SQ1, SQ0, 65536.0, ALU.add)
 
-    MAP, MAPW = ("MAP", 0, NMAP), ("MAP", 0, W)
-    for k in range(16): fill(("MAP", k * 512, k * 512 + 512), 0.0)
-    TH = al("PF", 4)
-    copy(TH, THI)
-    UT, LT = al("PB", 128), al("PB", 128)
-    asel(UT, BO, [[-1, 128]], ALU.is_ge, 0, 1)
+    MAP, MAPW, MAP2, MAP2W = ("X", W, NX), ("X", W, 2 * W), ("MAP", 0, NMAP), ("MAP", 0, W)
+    for k in range(16): fill(sub(MAP, k * 512, k * 512 + 512), 0.0)
+    for k in range(16 * any(CFG["far"])): fill(sub(MAP2, k * 512, k * 512 + 512), 0.0)
+    TH, TM0, fr0, f1, F12, FD = al("PF", 4), al("PF", 4), al("PF", 4), al("PB", 4), al("PF", 8), [al("PB", 128) for _ in range(4)]
+    ts(TH, THI, 2.0, ALU.mult, -1.0, ALU.add)
+    ts(TM0, THI, 0.5, ALU.is_gt, RM0, ALU.mult)
+    op("dve", lambda: g.vector.reciprocal(out=ap(fr0), in_=ap(TH)), [TH], [fr0], 0.22)
+    copy(f1, fr0)
+    copy(sub(F12, 0, 4), f1)
+    tt(sub(F12, 4, 8), fr0, f1, ALU.subtract)
+    YK = scaled(YW, 1024.0)
+    LT = al("PB", 128)
     asel(LT, BO, [[1, 128]], ALU.is_gt, 0, -1)
-    LR, lh, ll = al("PB", 512), al("PB", 512), al("PB", 512)
-    iota(lh, [[1, 32], [0, 16]], 0, 0)
-    iota(ll, [[0, 32], [1, 16]], 0, 0)
-    ts(lh, lh, m16(0), ALU.mult, 2.0 ** -6, ALU.mult)
-    ts(ll, ll, m16(1), ALU.mult, 2.0 ** -10, ALU.mult)
-    for k in range(4): tt(sub(LR, k * 128, k * 128 + 128), sub(lh, k * 128, k * 128 + 128), sub(ll, k * 128, k * 128 + 128), ALU.add)
-    W64 = al("PF", 65)
-    for q in range(8): move(sub(W64, q, 64, 8), BO8, scale=-2.0 ** (q + 2))
-    fill(sub(W64, 64, 65), 1020.0)
-    if "pe" in (CFG["keys"], CFG["veto"]):
-        EI = [al("PB", 128) for _ in range(16)]
-        for i in range(16): times(EI[i], BO, m16(i))
-    if CFG["dm"] != "dve": IDQ = [scaled(ID, -2.0 ** (q + 2)) for q in range(8)]
-    if CFG["mv"] == "list":
-        CLT, CQF = al("PB", 1024), al("PF", 128)
-        iota(CLT, [[-1, 8], [0, 128]], 0, 0)
-        ts(CLT, CLT, 0.25, ALU.mult)
-        iota(CQF, [[-4, 8], [0, 16]], -2, 0)
-        fill(("SD", 512, 1024), 0.0)
+    LR, LW = al("PB", 512), al("PB", 128)
+    ll = al("PB", 512)
+    iota(LR, [[0, 16], [1, 32]], 0, 0)
+    iota(ll, [[1, 16], [0, 32]], 0, 0)
+    op("dve", lambda: g.vector.tensor_copy(out=T.PB[64:128, LR[1]:LR[2]], in_=T.PB[64:128, ll[1]:ll[2]]), [ll], [LR], dv(256))
+    for p0, c in ((0, 2.0 ** -12), (64, 2.0 ** -16)):
+        op("dve", lambda p0=p0, c=c: g.vector.memset(T.PB[p0:p0 + 64, LW[1]:LW[2]], c), [], [LW], dv(64))
+    EI = [al("PB", 128) for _ in range(16)]
+    for i in range(16): times(EI[i], BO, m16(i))
+    IDQ = [scaled(ID, -2.0 ** (q + 2)) for q in range(8)]
+    CM, cmc = [al("PB", 128) for _ in range(3)] + [BO], al("PF", 3)
+    for k in range(3):
+        ts(sub(cmc, k, k + 1), IC, 4.0 * k + 3.5, ALU.is_lt)
+        times(CM[k], BO, sub(cmc, k, k + 1))
     RHE = al("PB", 64)
-    for k in range(8): ts(sub(RHE, k * 8, k * 8 + 8), BO8, m16(0), ALU.mult)
+    times(sub(RHE, 0, 8), BO8, m16(0))
+    for k in (8, 16, 32): move(sub(RHE, k, 2 * k), sub(RHE, 0, k))
     D0, dm2, OFC, EXC = al("PF", 128), al("PF", 16), al("PF", 1), al("PF", 1)
     ts(sub(D0, 0, 16), M16, -2.0 * UP * KB, ALU.mult)
     ts(sub(dm2, 0, 15), sub(M16, 0, 15), UP * KB, ALU.mult)
@@ -350,7 +364,7 @@ def build(g, core, rank, T, topo, choice):
     iota(i8, [[16, 8]], W + 129, 0)
     ts(TRW, i8, IC, ALU.add, -KK, ALU.add)
     iota(SROW, [[1024, 128]], W * 1024 + 896, 0)
-    CQ, C2, dd, dr, cq, SLH = al("PB", 128), al("PB", 128), al("PF", 16), al("PF", 16), al("PF", 128), al("PF", 128)
+    CQ, C2, cq, SLH = al("PB", 128), al("PB", 128), al("PF", 128), al("PF", 128)
     iota(cq, [[-32, 8], [0, 16]], -23, 0)
     move(CQ, cq, scale=0.125)
     ts(SLH, SROW, 1.0 / 1024, ALU.mult, -W - 0.375, ALU.add)
@@ -361,26 +375,30 @@ def build(g, core, rank, T, topo, choice):
     ROW = [[al("PB", 128), al("PB", 128)] for w in range(2)]
     for w in range(2):
         for k in range(2): times(ROW[w][k], (IDH, ID2)[k], m16(1 - w))
-    KRP, KBZ, ZERO = al("PB", 512), [al("PB", 512) for _ in range(3)], al("PB", 128)
-    fill(KRP, 0.0)
-    for x in KBZ: fill(x, 0.0)
+    KRP, KBZ, ZERO, ZW, B8F = al("PB", 400), al("PB", 384), al("PB", 128), al("PB", 240), al("PF", 8)
+    fill(sub(KRP, 0, 16), 1.0)
+    fill(KBZ, 0.0)
     fill(ZERO, 0.0)
+    fill(ZW, 0.0)
+    move(sub(ZW, 112, 128), M16)
+    move(B8F, BO8)
 
     SQ, SI, C16, Y1, HB = two("PF", 64), two("PI", 64), two("PU", 64), two("PB", 512), two("PB", 512)
     ZH, ZF, GE = al("PB", 1536), al("PB", 512), al("PB", 512)
-    CN, TM = two("PI", 256), two("PF", 256)
-    tda, NF, NBIG = al("PF", 256), al("PB", 32), scaled(ID, -16384.0)
+    CN, TM = two("PI", 256) + (al("PI", 256),), two("PF", 256)
+    tda, NF, NBIG = al("PF", 256), two("PB", 32), scaled(ID, -16384.0)
     OFF, CR, crk = al("PU", 256), [al("PF", 64 * t + 64) for t in range(TS)], al("PF", 256)
     ZG, SQS, VSE, SIS, CS = al("PB", 512), al("PF", 64), al("PF", 64), al("PI", 64), al("PI", 64)
-    AQ, KKC, NC, SGN = al("PB", 128), al("PF", 1), al("PF", 4), al("PB", 512)
-    fill(KKC, KK)
+    AQ, SGN, SGP = al("PB", 128), al("PB", 512), al("PB", 512)
     LRF, lr1, lr2, lr3, LRU = two("PF", 32), al("PF", 32), al("PF", 32), al("PF", 32), two("PU", 32)
-    LG, WO = al("PB", 512), two("PF", 32)
-    HAL, HTT, GO, FRA, FR = al("PB", 48), al("PF", 48), al("PB", 32), al("PB", 32), two("PB", 32)
+    LG, WS = al("PB", 512), two("PF", 64)
+    WO = [sub(x, 32, 64) for x in WS]
+    HAL, HTT, GO, FRA, FR, FQ = al("PB", 48), al("PF", 48), al("PB", 32), al("PB", 32), two("PB", 32), two("PB", 32)
     fill(HAL, 0.0)
     fill(HTT, 8192.0)
     HALT, HT = sub(HAL, 16, 48), sub(HTT, 16, 48)
-    dht, SOFF = al("PF", 32), al("PU", 32)
+    dht, SOFF = al("PF", 64), al("PU", 32)
+    fill(sub(dht, 0, 32), 0.0)
     vm, vw, vq, vr = (al("PI", 32) for _ in range(4))
     VB = al("PF", 32)
     SV0, SIN = al("PF", 64), al("PI", 64)
@@ -390,7 +408,7 @@ def build(g, core, rank, T, topo, choice):
     KW = sub(KM, 15, 128, 16)
     AB = al("PF", 8 * 144)
     EXT = sub(AB, 0, 8 * 144, 144)
-    OK, MOF, TP, TOFF, NDX = al("PB", 8), al("PF", 16), al("PF", 16), two("PU", 8), al("PB", 128)
+    OK, MOF, TP, TOFF = al("PB", 8), al("PF", 16), al("PF", 16), two("PU", 8)
     fill(MOF, 0.0)
     c8, c9, g9, dl0, DL = al("PF", 1), al("PF", 1), al("PF", 1), al("PF", 1), al("PU", 1)
     ts(c8, IC, 7.5, ALU.is_ge, -8.0, ALU.mult)
@@ -399,11 +417,8 @@ def build(g, core, rank, T, topo, choice):
     tt(dl0, g9, c9, ALU.add)
     copy(DL, dl0)
     ZI, ZJ, ZO = al("PI", 8), al("PI", 8), al("PU", 8)
-    YQ, MK, LV, VL, FRB = al("PB", 256), al("PB", 512), al("PB", 512), al("PU", 32), al("PF", 32)
-    w1, w2, w3, w4 = al("PI", 32), al("PI", 32), al("PI", 32), al("PB", 32)
-    SG, ACC, A16, DMS, DMC, sw = al("PB", 65), al("PF", 1), al("PF", 1), al("PB", 8), al("PF", 1), al("PF", 65)
-    fill(sub(SG, 64, 65), 1.0)
-    SG = sub(SG, 0, 64)
+    YQ, LV, VL, RM = al("PB", 256), al("PB", 512), al("PU", 32), al("PB", 256)
+    SG, ACC, A16, DMS = al("PB", 64), al("PF", 1), al("PF", 1), al("PB", 8)
     hb1, hb2 = al("PI", 256), al("PI", 256)
 
     def vbase(v):
@@ -419,69 +434,83 @@ def build(g, core, rank, T, topo, choice):
         ts(sub(VD, 0, 32), v, 8064, ALU.bitwise_and)
         ts(sub(VD, 32, 64), v, 127, ALU.bitwise_and)
         copy(VDB, VD)
-        if CFG["keys"] == "pe":
-            mm([(("BD", 0, 512), BO, LR, True, False)])
-            mms([(("BD", i, 512, 16), EI[i], sub(VDB, d * 32, d * 32 + 32), False, i == 15 and d == 1) for i in range(16) for d in range(2)], 4)
-        else:
-            for i in range(16): times(("KX", i, 1024, 16), VDB, m16(i))
-        for h in range(2 * (CFG["keys"] != "pe")):
-            o = ("BD", h * 256, h * 256 + 256)
-            mms([(o, BO, sub(LR, h * 256, h * 256 + 256), True, False), (o, BO, ("KX", h * 256, h * 256 + 256), False, False),
-                 (o, BO, ("KX", 512 + h * 256, 768 + h * 256), False, True)], 1)
-        for h in range(2): aff(("KEYR", h * 256, h * 256 + 256), ("BD", h * 256, h * 256 + 256), 1024.0 * KB, -(MID + 256.0) * KB)
+        mm([(("BD", 0, 512), LW, LR, True, False)])
+        mms([(("BD", 32 * i, 32 * i + 32), EI[i], sub(VDB, d * 32, d * 32 + 32), False, i == 15 and d == 1) for i in range(16) for d in range(2)], 4)
+        n = 512 // CFG["kcut"]
+        for h in range(0, 512, n): aff(("KEYR", h, h + n), ("BD", h % 256 * 2 + h // 256, h % 256 * 2 + 2 * n, 2), 1024.0 * KB, -(MID + 256.0) * KB)
 
     turns = [0]
-    RHX = al("PB", 136)
+    RHX = al("PB", 280)
     fill(RHX, 0.0)
-    for k in range(8): move(sub(RHX, 8 + 16 * k, 16 + 16 * k), sub(RHE, 0, 8))
+    move(sub(RHX, 24, 32), sub(RHE, 0, 8))
+    for k in (32, 64, 128): move(sub(RHX, 24 + k, 24 + 2 * k), sub(RHX, 24, 24 + k))
+    MD, DF, dl8, DL8, IDF = al("PB", 128), al("PB", 144), al("PF", 8), al("PU", 8), scaled(ID, 1.0, "PF")
+    move(sub(MD, 0, 16), M16)
+    for k in (16, 32, 64): move(sub(MD, k, 2 * k), sub(MD, 0, k))
+    fill(sub(DF, 128, 144), 0.0)
+    ts(dl8, sub(i16, 0, 8), g9, ALU.add)
+    copy(DL8, dl8)
 
     def tile(u):
         return ("G", u * 128, u * 128 + 128)
     NB8, FRC, RND = scaled(BO8, -1.0), al("PB", 64), al("PF", 1)
     fill(FRC, -0.3125)
-    ts(RND, g8, 0.25, ALU.mult, 12582914.0, ALU.add)
+    ts(RND, g8, 0.25, ALU.mult, RM0 + 2, ALU.add)
+    NB64, RH64, CR4, cr4 = scaled(sub(BO, 0, 128, 2), -1.0), al("PB", 64), al("PB", 256), al("PB", 256)
+    times(RH64, sub(BO, 0, 128, 2), m16(0))
+    iota(cr4, [[0, 32], [-16, 8]], -1, 0)
+    move(CR4, cr4, scale=0.25)
 
-    def join(win, off, cr, gb, u0, batches, hp, start, stop):
-        for k, nt in enumerate(batches):
-            new, nt = nt < 0, abs(nt)
-            xs = ("Q%d" % (k % 2), 0, nt * 8)
-            if new: mm([(xs, ID, FRC, True, False), (xs, AQ, RHE, False, False)])
-            j1 = (u0 + nt) // 2
-            for j0 in range(u0 // 2, j1, CFG["turn"]):
+    def join(win, gb, u0, off, cr, batches, hp, start, stop, last):
+        def tile(u):
+            return (gb, u * 128, u * 128 + 128)
+        for k, (nt, how, gs) in enumerate(batches):
+            n = 64 if how == "r" else 8
+            xs = ("Q%d" % (k % 2), 0, nt * n)
+            if how == "n": mm([(xs, ID, sub(FRC, 0, nt * n), True, False), (xs, AQ, sub(RHE, 0, nt * n), False, False)])
+            if how == "r":
+                mm([(xs, ID, sub(CR4, 0, nt * n), True, False)])
+                for u in range(u0, u0 + nt):
+                    b = u % 4
+                    mm([(sub(xs, (u - u0) * n, (u - u0) * n + n), sub(LG, b * 128, b * 128 + 128) if last else AQ, RH64, False, False)])
+            for j0 in range(u0, u0 + nt, 2 * CFG["turn"]):
                 bank = CFG["banks"][turns[0] % len(CFG["banks"])]
                 turns[0] += 1
-                je = min(j1, j0 + CFG["turn"])
-                for j in range(j0, je):
-                    if u0 + nt + sum(map(abs, batches[k + 1:])) - 2 * j0 <= CFG["fine"]: gather(None, (gb, j * 256, j * 256 + 256), win, sub(off, j * 16, j * 16 + 16))
-                    elif j == j0: gather(None, (gb, j0 * 256, je * 256), win, sub(off, j0 * 16, je * 16))
-                    tiles, c0 = [(gb, u * 128, u * 128 + 128) for u in (2 * j, 2 * j + 1)], (j - j0) * 256
+                je = min(u0 + nt, j0 + 2 * CFG["turn"])
+                for u in range(j0, je):
+                    if (u - u0) % gs == 0: gather(None, (gb, u * 128, min(u + gs, u0 + nt) * 128), win, sub(off, u * 8, min(u + gs, u0 + nt) * 8))
+                    if gs > 1 and u % 2 == 0: continue
+                    us = range(u - (gs > 1), u + 1)
 
-                    def turn(tiles=tiles, bank=bank, c0=c0):
-                        g.tensor.transpose(T[bank][:, c0:c0 + 128], ap(tiles[0]), ap(ID))
-                        return g.tensor.transpose(T[bank][:, c0 + 128:c0 + 256], ap(tiles[1]), ap(ID))
-                    if bank[0] == "T": op("pe", turn, tiles + [ID], [(bank, c0, c0 + 256)], 256 * PEC)
-                    else: mm([((bank, c0 + w * 128, c0 + w * 128 + 128), tiles[w], ID, True, True) for w in range(2)])
-                    mm([(sub(xs, (2 * j + w - u0) * 8, (2 * j + w - u0) * 8 + 8), tiles[w], NB8 if new else BO8, not new, not new or j == j1 - 1 and w == 1) for w in range(2)])
-                move(("LO", j0 * 256, je * 256), (bank, 0, (je - j0) * 256), relu=True)
-            if new:
-                for d in range(8): ts(("HI", u0 * 64 + d, (u0 + nt) * 64, 8), xs, RND, ALU.add, 12582914.0 + 4 * d, ALU.is_equal)
+                    def turn(us=us, bank=bank, j0=j0):
+                        for w in us: x = g.tensor.transpose(T[bank][:, (w - j0) * 128:(w - j0) * 128 + 128], ap(tile(w)), ap(ID))
+                        return x
+                    op("pe", turn, [tile(w) for w in us] + [ID], [(bank, (us[0] - j0) * 128, (u + 1 - j0) * 128)], 128 * len(us) * PEC)
+                    mm([(sub(xs, (w - u0) * n, (w - u0) * n + n), tile(w), {"o": BO8, "n": NB8, "r": NB64}[how], how == "o", how == "o" or w == u0 + nt - 1) for w in us])
+                move(("LO", j0 * 128, je * 128), (bank, 0, (je - j0) * 128), relu=True)
+            if how == "r": ts(("HI", u0 * 64, (u0 + nt) * 64), xs, RM0 - 50 if last else RND, ALU.add, RM0 + 2, ALU.is_equal)
+            elif how == "n":
+                for d in range(8): ts(("HI", u0 * 64 + d, (u0 + nt) * 64, 8), xs, RND, ALU.add, RM0 + 2 + 4 * d, ALU.is_equal)
             else:
                 yq = sub(YQ, u0 * 8, (u0 + nt) * 8)
                 tt(yq, sub(cr, u0 * 8, (u0 + nt) * 8), xs, ALU.subtract)
                 for d in range(8): ts(("HI", u0 * 64 + d, (u0 + nt) * 64, 8), yq, 130.0 + 4 * d, ALU.is_equal)
             mms([(hp, ("LO", u * 128, u * 128 + 128), ("HI", u * 64, u * 64 + 64), start and not k and u == u0, stop and k == len(batches) - 1 and u == u0 + nt - 1)
-                 for u in range(u0, u0 + nt)], 8)
+                 for u in range(u0, u0 + nt)], 4)
             u0 += nt
 
-    MAP2 = ("MAP2", 0, NMAP)
     keys(V0)
     vbase(V0)
 
     for t in range(TS):
         pr, nx, last = t % 2, (t + 1) % 2, t == TS - 1
         partner = T.cores[rank ^ (1 + t % 7)]
-        cn, fr, vc = CN[pr], FR[pr], VC[pr] if t else V0
+        cn, fr, fq, vc = CN[t % 3], FR[pr], FQ[pr], VC[pr] if t else V0
         ksd = "KSD"
+        if last: OFF = al("PU", 256)
+        if t - 1 in CFG["zall"]: ZF = al("PB", 512)
+        far = sum(x[0] for x in CFG["far"][t])
+        ofl, crl = ("OFL", 128 * t - 128, 128 * t - 128 + 8 * far), ("CRL", 128 * t - 128, 128 * t - 128 + 8 * far)
         for b in range(4):
             p = b % 2
             zc = SD if b == 0 else sub(ZH, b * 512 - 512, b * 512)
@@ -493,58 +522,62 @@ def build(g, core, rank, T, topo, choice):
                     sums(o, sub(zc, z0, 16 * q1))
                     for m in (1, 0): act(sub(SQ[p], k0 + m * nq, k0 + m * nq + nq), o, AF.Square, BIAS[m])
                 c16 = sub(C16[p], k0, k0 + 2 * nq)
-                for m0, m1 in (((nq, 2 * nq), (0, nq)) if CFG["perm"] and b else ((0, 2 * nq),)):
+                for m0, m1 in ((nq, 2 * nq), (0, nq)):
                     si = sub(SIN if t and not b else SI[p], k0 + m0, k0 + m1)
                     if b or not t: tt(si, sub(SQ[p] if b else SQ0, k0 + m0, k0 + m1), sub(V16, k0 + m0, k0 + m1), ALU.add)
-                    cc = sub(cn, 8 * q0 + b * 2 * nq + m0, 8 * q0 + b * 2 * nq + m1)
+                    cc = sub(cn, 64 * b + 2 * m0 + q0, 64 * b + 2 * m0 + q1)
                     ts(cc, si, 4, ALU.arith_shift_right, 8191, ALU.bitwise_and)
                     copy(sub(c16, m0, m1), cc)
                 for c0, c1 in gcut:
                     r0, r1 = z0 + c0 * 16, z0 + c1 * 16
-                    yy, hu, o16 = sub(Y1[p], r0, r1), sub(HB[p], r0, r1), sub(c16, c0, c1)
-                    gather("act", yy, XW, sub(c16, nq + c0, nq + c1))
-                    op("dve", lambda o16=o16, yy=yy, hu=hu: g.vector.tensor_tensor(out=ap(hu), in0=ind(XW, o16), in1=ap(yy), op=ALU.max),
-                       [XW, o16, yy], [hu], gat(r1 - r0))
+                    gather("act", sub(Y1[p], r0, r1), XW, sub(c16, nq + c0, nq + c1))
+                    gtt(sub(HB[p], r0, r1), XW, sub(c16, c0, c1), sub(Y1[p], r0, r1), ALU.max)
                 for c0, c1, bank in dcut:
                     r0, r1 = z0 + c0 * 16, z0 + c1 * 16
                     dps = (bank, 0, r1 - r0)
-                    mm([(dps, NID, sub(zc, r0, r1), True, False)])
-                    mm([(dps, ID, sub(HB[p], r0, r1), False, True)])
-                    act(sub(zn, r0, r1), dps, AF.Abs)
-                    if b == 3: ts(sub(GE, r0, r1), sub(zn, r0, r1), sub(TH, t, t + 1), ALU.is_ge, 1024.0, ALU.mult)
+                    if b < 3:
+                        mm([(dps, NID, sub(zc, r0, r1), True, False)])
+                        mm([(dps, ID, sub(HB[p], r0, r1), False, True)])
+                        act(sub(zn, r0, r1), dps, AF.Abs)
+                    else:
+                        mm([(dps, FD[2], sub(zc, r0, r1), True, False), (dps, FD[3], sub(zc, r0, r1), False, False)])
+                        mm([(dps, FD[0], sub(HB[p], r0, r1), False, False), (dps, FD[1], sub(HB[p], r0, r1), False, True)])
+                        ts(sub(GE, r0, r1), dps, RM0, ALU.add, sub(TM0, t, t + 1), ALU.not_equal)
+                        act(sub(zn, r0, r1), dps, AF.Abs, scale=sub(TH, t, t + 1))
+                if b == 3 and t in CFG["zall"]: send(partner, ("ZL", 384 + z0, 384 + 16 * q1), sub(ZF, z0, 16 * q1), "rz%d" % t if q0 else "ry%d" % t)
+            if b == 0:
+                for k in range(4): times(FD[k], (ID, NID)[k // 2], sub(F12, 4 * (k % 2) + t, 4 * (k % 2) + t + 1))
         aff((ksd, 0, 128), SROW, KB, -(MID + 256.0) * KB)
-        for q0, q1, b0, b1 in CFG["post"]:
-            nq = q1 - q0
-            o, dl = (b0, 320, 320 + nq), (b1, 352, 352 + nq)
-            sums(o, sub(GE, 16 * q0, 16 * q1), sub(fr, q0, q1) if t else None)
-            ts(sub(HALT, q0, q1), o, 8704.0, ALU.is_ge)
-            tt(sub(HT, q0, q1), o, sub(TL, q0, q1), ALU.min)
-            mm([(dl, ID, sub(C16B, 0, nq), True, False)])
-            mm([(dl, UT, sub(HALT, q0 - 1, q1 - 1), False, False), (dl, LT, sub(HALT, q0, q1), False, True)])
-            tt(sub(dht, q0, q1), sub(HT, q0 - 1, q1 - 1), sub(HT, q0, q1), ALU.subtract)
-            ini, wo, da = sub(WO[pr], q0 - 1, q0) if q0 else INI, sub(WO[pr], q0, q1), sub(dht, q0, q1)
-            op("dve", lambda ini=ini, wo=wo, da=da, dl=dl: g.vector.tensor_tensor_scan(out=ap(wo), data0=ap(da), data1=ap(dl), initial=ap(ini), op0=ALU.add, op1=ALU.add),
-               [da, dl, ini], [wo], dv(16))
-            copy(sub(SOFF, q0, q1), wo)
-            scatter((ksd, 0, NK), sub(SOFF, q0, q1), ("KEYR", 16 * q0, 16 * q1))
+        o, dl = (CFG["cnt"][0], 320, 352), (CFG["cnt"][1], 352, 416)
+        if t: mm([(o, NID16, fq, True, False)])
+        mms([(o, sub(YK, 15 - i, 143 - i), sub(GE, 32 * i, 32 * i + 32), not t and i == 0, i == 15) for i in range(16)], 4)
+        ts(HALT, o, 8704.0, ALU.is_ge)
+        tt(HT, o, TL, ALU.min)
+        mm([(dl, ID, C64, True, False)])
+        mm([(sub(dl, 0, 32), LT, HALT, False, False), (sub(dl, 32, 64), ID, sub(HALT, -1, 31), False, True)])
+        tt(sub(dht, 32, 64), sub(HT, -1, 31), HT, ALU.subtract)
+        scan(WS[pr], dht, dl, INI, ALU.add, ALU.add)
+        copy(SOFF, WO[pr])
+        scatter((ksd, 0, NK), SOFF, ("KEYR", 0, 512))
         ks = (ksd, 0, 128)
-        aq = ("P0", 0, 128)
-        ends = CFG["mv"] == "ends"
-        mq = ("Q0", 0, 128)
-        if ends: mm([(aq, ID, CQ, True, False), (mq, ID, C2, True, False)])
-        for c in range(1 * ends):
-            mm([(("BD", 0, 32), BO, HALT, True, True)])
-            for k in range(4):
-                act(sub(KJ, 32 * k, 40 * k + 8), ("BD", 0, 8 * k + 8), AF.Copy, scale=-1.0, acc_o=sub(NC, k, k + 1))
-                act(sub(SGN, k * 128, k * 128 + 128), SLH, AF.Sign, sub(NC, k, k + 1))
-                mm([(sub(mq, w, 128, 2), ROW[w][k == 3], sub(SGN, k * 128 + w, k * 128 + 128, 2), False, k == 3 and w == 1) for w in range(2)])
-                mm([(aq, ID2 if k == 3 else IDH, sub(SGN, k * 128, k * 128 + 128), False, k == 3)])
+        aq, mq, early = ("P1", 0, 128), ("Q1", 0, 128), t in CFG["early"]
+        ncs, ncl = ("NCS", 4 * t, 4 * t + 4), ("NCL", 4 * t, 4 * t + 4)
         mvs, mvl = ("MVS", t * 128, t * 128 + 128), ("MVL", t * 128, t * 128 + 128)
-        if ends:
-            act(mvs, mq, AF.Copy)
-            send(partner, mvl, mvs, "rm%d" % t)
-            if not last: move(AQ, aq)
-        op("dve", lambda ks=ks: g.vector.tensor_tensor_scan(out=ap(KM), data0=ap(D0), data1=ap(ks), initial=0.0, op0=ALU.add, op1=ALU.max), [D0, ks], [KM], dv(128))
+        mm([(("P0", 128 + 32 * k, 160 + 32 * k), CM[k], HALT, True, True) for k in range(4)])
+        for k in range(4): act(sub(KJ, 32 * k, 32 * k + 32), ("P0", 128 + 32 * k, 160 + 32 * k), AF.Copy, scale=-1.0, acc_o=sub(ncs, k, k + 1))
+        if early: send(partner, ncl, ncs, "rm%d" % t)
+        if not last: mm([(aq, ID, CQ, True, False)])
+        mm([(mq, ID, C2, True, False)])
+        for k in range(4):
+            own, sg = sub(SGN, k * 128, k * 128 + 128), sub(SGP if early else SGN, k * 128, k * 128 + 128)
+            if not (last and early): act(own, SLH, AF.Sign, sub(ncs, k, k + 1))
+            if not last: mm([(aq, ID2 if k == 3 else IDH, own, False, k == 3)])
+            if early: act(sg, SLH, AF.Sign, sub(ncl, k, k + 1))
+            mm([(sub(mq, w, 128, 2), ROW[w][k == 3], sub(sg, w, 128, 2), False, k == 3 and w == 1) for w in range(2)])
+        act(mvl if early else mvs, mq, AF.Copy)
+        if not early: send(partner, mvl, mvs, "rm%d" % t)
+        if not last: move(AQ, aq)
+        scan(KM, D0, ks, 0.0, ALU.add, ALU.max)
         act(KS2, ks, AF.Identity, OFC)
         aff(EXT, KW, -1.0 / (1024.0 * KB), EXC)
         for q in range(7, -1, -1):
@@ -553,24 +586,22 @@ def build(g, core, rank, T, topo, choice):
             else: ts(ab, sub(ks, 0, 16 * q + 16), kw, ALU.subtract, OFC, ALU.add)
             red(sub(MN, q, q + 1), sub(AB, q * 144, q * 144 + 16 * q + 17), ALU.min, True)
         tt(MO, MN, TRW, ALU.min)
-        mos, mol = ("MOS", t * 8, t * 8 + 8), ("MOL", t * 8, t * 8 + 8)
+        a = 32 if t in CFG["zall"] else 8 * t
+        mos, mol = ("MOS", a, a + 8), ("MOL", a, a + 8)
         ts(mos, MO, KK, ALU.add)
-        send(partner, mol, mos, "ro%d" % t)
+        if t not in CFG["zall"]: send(partner, mol, mos, "ro%d" % t)
         ts(GO, WO[pr], 127.5, ALU.is_lt)
-        if t:
-            tt(FRA, fr, GO, ALU.add)
-            if not last:
-                aff(lr2, WO[pr], 1.0, 128.0 * t)
-                tt(lr3, lr2, GO, ALU.mult)
-                tt(LRF[pr], LRF[nx], lr3, ALU.max)
-        else:
-            copy(FRA, GO)
-            tt(LRF[pr], WO[pr], GO, ALU.mult)
         if not last:
+            aff(lr2, WO[pr], 1.0, 16.0 + 128.0 * t)
+            tt(lr3 if t else LRF[pr], lr2, GO, ALU.mult)
+            if t: tt(LRF[pr], LRF[nx], lr3, ALU.max)
             copy(LRU[pr], LRF[pr])
             ts(ZI, KW, 1.0 / KB, ALU.mult, 256.0, ALU.add)
             ts(ZJ, ZI, 511, ALU.bitwise_and)
             copy(ZO, ZJ)
+            if t in CFG["zall"]:
+                copy(("MOS", 40, 48), ZJ)
+                send(partner, ("MOL", 32, 48), ("MOS", 32, 48), "ro%d" % t)
             for b in range(4): gather(None, sub(ZG, b * 128, b * 128 + 128), SD if b == 0 else sub(ZH, b * 512 - 512, b * 512), ZO)
             us = ("BD", 0, 32)
             sums(us, ZG)
@@ -584,58 +615,52 @@ def build(g, core, rank, T, topo, choice):
             copy(sub(OFF, t * 64, t * 64 + 64), CS)
             mm([(("BD", 64, 128), AQ, RHE, True, True)])
             aff(sub(CR[t], t * 64, t * 64 + 64), ("BD", 64, 128), 1.0, CQ4)
-            gather(None, ("ZS", t * 128, t * 128 + 128), ZF, ZO)
-            send(partner, ("ZL", t * 128, t * 128 + 128), ("ZS", t * 128, t * 128 + 128), "rz%d" % t)
+            if t in CFG["zall"]: gather(None, ("ZL", t * 128, t * 128 + 128), ("ZL", 384, 896), ("MOL", 40, 48))
+            else:
+                gather(None, ("ZS", t * 128, t * 128 + 128), ZF, ZO)
+                send(partner, ("ZL", t * 128, t * 128 + 128), ("ZS", t * 128, t * 128 + 128), "rz%d" % t)
         else:
-            mms([(("BD", i, 512, 16), EI[i], FRA, True, True) for i in range(16)], 4)
-            for k in range(4): move(sub(LG, k * 128, k * 128 + 128), ("BD", k * 128, k * 128 + 128), scale=200.0 - k)
-            mm([(("P0", 128 + k // 2 * 128, 256 + k // 2 * 128), sub(LG, k * 128, k * 128 + 128), sub(RHX, 8 - k % 2 * 8, 136 - k % 2 * 8), k % 2 == 0, k % 2 == 1) for k in range(4)])
-            aff(CR[t], ("P0", 128, 384), 0.25, 77.6875)
-            copy(w1, WO[pr])
-            ts(w2, w1, 4, ALU.arith_shift_right, 7, ALU.bitwise_and)
-            ts(VL, w2, g9, ALU.add)
-            ts(w3, w1, 15, ALU.bitwise_and)
-            ts(lr1, GO, -16.0, ALU.mult, 16.0, ALU.add)
-            tt(w4, w3, lr1, ALU.add)
-            mms([(("BD", i, 512, 16), EI[i], w4, True, True) for i in range(16)], 4)
-            for h in range(2): ts(sub(MK, h * 256, h * 256 + 256), ("BD", h * 256, h * 256 + 256), IC, ALU.is_equal)
-            ts(lr2, fr, 5.5, ALU.mult, -5.0, ALU.add)
-            ts(lr3, GO, 4.5, ALU.mult)
-            tt(FRB, lr2, lr3, ALU.add)
-        if t:
-            for h, (x, sg) in enumerate(((fr, fr), (NF, NF))):
-                mms([(("HP", h * 256 + 8 * q0 + e * (q1 - q0), h * 256 + 8 * q0 + (e + 1) * (q1 - q0)), NBIG, sub(x, q0, q1), True, True)
-                     for q0, q1, _g, _d in CH for e in range(8)], 4)
-            tt(tda, ("HP", 256, 512), TM[nx] if t > 1 else CN[0], ALU.add)
-            tt(("HP", 0, 256), ("HP", 0, 256), cn, ALU.add)
-            tt(TM[pr], ("HP", 0, 256), tda, ALU.max)
+            tt(FRA, fq, GO, ALU.add)
+            mms([(("BD", 32 * i, 32 * i + 32), EI[i], FRA, True, True) for i in range(16)], 4)
+            for k in range(4): move(sub(LG, k * 128, k * 128 + 128), ("BD", k * 128, k * 128 + 128), scale=50.0 - k / 4)
+            mms([(("P0", 128, 384), sub(LG, k * 128, k * 128 + 128), sub(RHX, 24 - 8 * k, 280 - 8 * k), k == 0, k == 3) for k in range(4)], 1)
+            aff(CR[t], ("P0", 128, 384), 1.0, 77.6875)
+            if far: send(partner, crl, sub(CR[t], 0, 8 * far), "rc%d" % t)
+            ts(VL, WO[pr], 128.0, ALU.min)
+        def trails():
+            tb, tm = CFG["tbank"], ("YT", 0, 256) if last else TM[pr]
+            mms([((tb, 32 * e, 32 * e + 32), NBIG, fr, True, True) for e in range(8)], 4)
+            mm([((tb, 256, 512), IDF, TM[nx], True, False)], f32=True)
+            mms([((tb, 256 + 32 * e, 288 + 32 * e), NBIG, NF[pr], False, e == 7) for e in range(8)], 4)
+            for c0, c1 in CFG["tcut"]:
+                tt(sub(tda, c0, c1), (tb, c0, c1), sub(cn, c0, c1), ALU.add)
+                tt(sub(tm, c0, c1), (tb, 256 + c0, 256 + c1), sub(tda, c0, c1), ALU.max)
+                if last: copy(sub(OFF, c0, c1), sub(tm, c0, c1))
             if last:
-                for h in range(2): copy(sub(OFF, h * 128, h * 128 + 128), sub(TM[pr], h * 128, h * 128 + 128))
-                for q0, q1, _g, _d in CH:
-                    for e in range(8): move(("YT", e * 32 + q0, e * 32 + q1), sub(TM[pr], 8 * q0 + e * (q1 - q0), 8 * q0 + (e + 1) * (q1 - q0)))
-                dma(T.yt[:], T.YT[:], [("YT", 0, 256)], [], "st_t", 2.4)
-        far = sum(CFG["far"][t])
+                if far: send(partner, ofl, sub(OFF, 0, 8 * far), "rf%d" % t)
+                dma(T.yt[:], T.YT[:], [tm], [], "st_t", 2.4)
+        if last or t and not CFG["late"]: trails()
+        if not t: copy(TM[0], cn)
         if far:
-            ps, pl = ("PS", t * 64, t * 64 + 64), ("PL", t * 64, t * 64 + 64)
+            ps, pl = ("PS", t * 64 - 64, t * 64), ("PL", t * 64 - 64, t * 64)
             scatter(MAP2, mos, mvs)
-            join(("MAP2", 0, W), ("OFL", t * 128, t * 128 + 128), ("CRL", t * 128, t * 128 + 128), "GW", 0, CFG["far"][t], ("P1", 0, 64), True, True)
+            join(MAP2W, "GW%d" % t, 0, ofl, crl, CFG["far"][t], ("P1", 0, 64), True, True, last)
             move(ps, ("P1", 0, 64))
             send(partner, pl, ps, "rp%d" % t)
+            send(partner, ("G", 0, 128 * far), ("GW%d" % t, 0, 128 * far), "rg%d" % t)
             if not last: scatter(MAP2, mos, ZERO)
         scatter(MAP, mol, mvl)
         ts(OK, mol, W - 0.5, ALU.is_lt)
-        ts(sub(MOF, 0, 8), mol, 1.0 / 4096, ALU.mult, 1.0, ALU.add)
+        if not last: ts(sub(MOF, 0, 8), mol, 1.0 / 4096, ALU.mult, 1.0, ALU.add)
         hp, ap16 = ("HP", 0, 64), ("P0", 0, 1)
         mm([(hp, ID, BASE, True, False)] + [(sub(hp, k * 8, k * 8 + 8), IDG[k], OK, False, False) for k in range(8)])
-        join(MAPW, OFF, CR[t], "G", far, CFG["batch"][t], hp, False, not far)
-        if far:
-            mm([(hp, ID, pl, False, True)])
-            for j in range(far // 2): gather(None, ("G", j * 256, j * 256 + 256), MAPW, sub(OFF, j * 16, j * 16 + 16))
+        join(MAPW, "G", far, OFF, CR[t], CFG["batch"][t], hp, False, not far, last)
+        if far: mm([(hp, ID, pl, False, True)])
         act(SG, hp, AF.Sign, acc_o=ACC)
         mm([(ap16, N8F, ACC, True, True)], f32=True)
         if last: send(partner, ("SGL", 0, 64), SG, "rb%d" % t)
         else:
-            op("dve", lambda: g.vector.tensor_tensor(out=ap(TP), in0=ind(SG, DL), in1=ap(MOF), op=ALU.add), [SG, DL, MOF], [TP], gat(16))
+            gtt(TP, SG, DL, MOF, ALU.add)
             tp = sub(TP, 0, 8)
             for q0, q1, _g, _d in CH: ts(sub(SIN, 2 * q0, 2 * q1), sub(SV0, 2 * q0, 2 * q1), ap16, ALU.add)
             ts(TOFF[pr], tp, 4096.0, ALU.mult)
@@ -653,65 +678,64 @@ def build(g, core, rank, T, topo, choice):
             keys(vn)
             scatter(MAP, mol, ZERO)
         w = 8 * t + 8
-        if CFG["dm"] == "pe" or last and CFG["dm"] == "end":
-            mm([(("HP", 256, 264), IDQ[q], sub(SG, q, 64, 8), q == 0, q == 7) for q in range(8)])
-            ts(DMS, ("HP", 256, 264), 1020.0, ALU.add)
-        else:
-            tt(sw, sub(SG, 0, 65), W64, ALU.mult)
-            red(DMC, sw, ALU.add)
-            times(DMS, BO8, DMC)
+        mm([(("HP", 256, 264), IDQ[q], sub(SG, q, 64, 8), q == 0, q == 7) for q in range(8)])
+        ts(DMS, ("HP", 256, 264), 1020.0, ALU.add)
         ecut, run = CFG["ecut"][t], None
         for k, (e0, e1) in enumerate(ecut):
-            hq = (("HP", "Q1", "Q0")[k % 3] if last else "HP", e0 * w, e1 * w)
-            mms([(sub(hq, (e - e0) * w + b * 8, (e - e0) * w + b * 8 + 8), tile(b // 2 * 16 + 2 * e + b % 2 if last else b * 8 + e), DMS, True, True)
-                 for e in range(e0, e1) for b in range(t + 1)], 4)
+            hq = (("HP", "Q1", "Q0", "BD")[k % 4] if last else "HP", 0, (e1 - e0) * w)
+            if last: mms([(sub(hq, (e - e0) * w + b, (e - e0) * w + w, 4), tile(4 * e + b), DMS, True, True) for e in range(e0, e1) for b in range(4)], 4)
+            else: mms([(sub(hq, (e - e0) * w + b * 8, (e - e0) * w + b * 8 + 8), tile(b * 8 + e), DMS, True, True) for e in range(e0, e1) for b in range(t + 1)], 4)
             ts(sub(hb1, e0 * w, e1 * w), hq, -0.5 + 2.0 ** -8, ALU.add)
             x, n = sub(hb2, e0 * w, e1 * w), e1 - e0
             ts(x, sub(hb1, e0 * w, e1 * w), 1, ALU.bitwise_and)
             while n > 1:
                 n //= 2
-                y = sub(KBZ[k], 0, 16 * w, 16) if n == 1 else al("PI", n * w)
+                y = al("PI", n * w) if n > 1 or last else sub(KBZ, 0, 16 * w, 16)
                 tt(y, sub(x, 0, n * w), sub(x, n * w, 2 * n * w), ALU.max)
                 x = y
+            if run:
+                y = al("PB" if k == len(ecut) - 1 else "PI", w)
+                tt(y, x, run, ALU.max)
+                x = y
+            run = x
         if last:
-            for bank, c0 in (("BD", 0), ("P0", 256)): mm([((bank, c0, c0 + 256), ZERO, sub(LR, 0, 256), True, False)])
-            for k in range(len(ecut)):
-                for b in range(4): mm([((("BD", "P0")[b // 2], b * 128, b * 128 + 128), sub(KBZ[k], b * 128, b * 128 + 128), ID, False, k == len(ecut) - 1 and b % 2 == 1)])
-        for b in range((t + 1) * (not last)):
-            kp = ("BD", b * 128, b * 128 + 128)
-            mm([(kp, sub(KBZ[0], b * 128, b * 128 + 128), ID, True, b < t)])
-        if not last: mms([(sub(kp, i, 128, 16), EI[i], ndl, False, i == 15) for i in range(16)], 4)
-        e = 128 * t + 128
-        if last:
-            move(sub(KRP, 0, 256), ("BD", 0, 256))
-            move(sub(KRP, 256, 512), ("P0", 256, 512))
+            fp, frn = ("P1", 0, 32), ("YS", 32, 64)
+            mm([(fp, NID, fr, True, False)])
+
+            def hurt(stop):
+                for j in range(8): times(sub(RM, j, 256, 8), run, sub(B8F, j, j + 1))
+                mm([(fp, sub(ZW, 112 - 16 * j, 240 - 16 * j), sub(RM, 32 * j, 32 * j + 32), False, stop and j == 7) for j in range(8)])
+            gtt(sub(DF, 0, 128), ("SGL", 0, 64), DL8, MD, ALU.mult)
+            for c0, c1 in CFG["vcut"]:
+                if c0 == CFG["hat"]: hurt(False)
+                gather(None, sub(LV, c0 * 16, c1 * 16), DF, sub(VL, c0, c1))
+                lanes(fp, LV, c0, c1, False, CFG["hat"] < 32 and c1 == 32)
+            if CFG["hat"] == 32: hurt(True)
+            ts(frn, fp, -0.5, ALU.is_lt)
         else:
-            move(sub(KRP, 0, e), ("BD", 0, e))
+            for b in range(t + 1):
+                kp = ("HP", b * 128, b * 128 + 128)
+                mm([(kp, sub(KBZ, b * 128, b * 128 + 128), ID, True, False)] + [(kp, ID, sub(KRP, 16 + b * 128, 144 + b * 128), False, True)] * (b < t))
+            mms([(sub(kp, i, 128, 16), EI[i], ndl, False, i == 15) for i in range(16)], 4)
+            e = 128 * t + 128
+            move(sub(KRP, 16, 16 + e), ("HP", 0, e))
             if t < TS - 2:
-                mm([(("HP", 256 + b * 64, 320 + b * 64), sub(KRP, b * 128, b * 128 + 128), RHE, True, True) for b in range(t + 1)])
+                mm([(("HP", 256 + b * 64, 320 + b * 64), sub(KRP, 16 + b * 128, 144 + b * 128), RHE, True, True) for b in range(t + 1)])
                 aff(sub(crk, 0, e // 2), ("HP", 256, 256 + e // 2), -200.0, 200.0)
                 tt(sub(CR[t + 1], 0, e // 2), sub(CR[t], 0, e // 2), sub(crk, 0, e // 2), ALU.min)
-            n8 = 8 * sum(CFG["far"][t + 1])
-            if n8:
-                nxt, a = T.cores[rank ^ (1 + (t + 1) % 7)], t * 128 + 128
-                send(nxt, ("OFL", a, a + n8), sub(OFF, 0, n8), "rf%d" % (t + 1))
-                send(nxt, ("CRL", a, a + n8), sub(CR[t + 1], 0, n8), "rc%d" % (t + 1))
-        for h in range(2 * (not last)): gather(None, sub(LG, h * 256, h * 256 + 256), KRP, sub(LRU[pr], h * 16, h * 16 + 16))
-        bw = ("P1" if last else "HP", 0, 32)
-        frn = ("YS", 32, 64) if last else FR[nx]
-        if last:
-            for c0, c1 in CFG["vcut"]:
-                lv, mk, li = sub(LV, c0 * 16, c1 * 16), sub(MK, c0 * 16, c1 * 16), sub(VL, c0, c1)
-                op("dve", lambda lv=lv, mk=mk, li=li: g.vector.tensor_tensor(out=ap(lv), in0=ind(("SGL", 0, 64), li), in1=ap(mk), op=ALU.mult),
-                   [("SGL", 0, 64), li, mk], [lv], gat(wd(lv)))
-            sums(bw, LV)
-            sums(("HP", 0, 32), KRP)
-            tt(lr1, FRB, bw, ALU.subtract)
-            tt(frn, lr1, ("HP", 0, 32), ALU.is_gt)
-        else:
-            sums(bw, LG)
-            tt(frn, FRA, bw, ALU.is_gt)
-            aff(NF, frn, -1.0, 1.0)
+                n8, nxt = 8 * sum(x[0] for x in CFG["far"][t + 1]), T.cores[rank ^ (1 + (t + 1) % 7)]
+                if n8:
+                    send(nxt, ("OFL", 128 * t, 128 * t + n8), sub(OFF, 0, n8), "rf%d" % (t + 1))
+                    send(nxt, ("CRL", 128 * t, 128 * t + n8), sub(CR[t + 1], 0, n8), "rc%d" % (t + 1))
+            n = 32 // CFG["lcut"]
+            for h in range(0, 32, n): gather(None, sub(LG, h * 16, h * 16 + n * 16), sub(KRP, 0, 16 + e), sub(LRU[pr], h, h + n))
+            frn = FR[nx]
+            sums(("HP", 32, 64), LG)
+            lanes(("HP", 0, 32), LG, 0, 32, True, True)
+            ts(FQ[nx], ("HP", 32, 64), 0.5, ALU.is_lt)
+            ts(frn, ("HP", 0, 32), 0.5, ALU.is_lt)
+            aff(NF[nx], frn, -1.0, 1.0)
+            if t and CFG["late"]: trails()
         vcn = ("YS", 0, 32) if last else VC[nx]
         tt(vd, vc, vn, ALU.subtract)
         tt(vd2, vd, frn, ALU.mult)
@@ -720,9 +744,6 @@ def build(g, core, rank, T, topo, choice):
 
     dma(T.ys[:], T.YS[:], [("YS", 0, 64)], [], "st_s", 2.4)
     return ops, used[0]
-
-
-setup()
 
 
 def place(ops, links, first, order):
@@ -807,13 +828,109 @@ def schedule(ops, rounds, key=None):
     return sorted(range(n), key=lambda i: (start[i], i)), best[2], best[3]
 
 
+def polish(ops, order, at, tries):
+    n, models = len(ops), ((1.0, 1.0, 1.0, HOP, 0.0, 1.0),) + CFG["other"]
+    order, at = list(order), list(at)
+    rng = np.random.RandomState(2)
+    links = [[[(d, ops[d]["lat"] + hop + (late if ops[d]["eng"] == "net" else load * (ops[d]["eng"] == "sp" and ops[d]["lat"] > 4)) if w else 0.0)
+               for d, w in o["deps"].items()] for o in ops] for (slow, ga, sc, hop, late, norm), load in zip(models, CFG["load"])]
+    cost = [[{q: du * (slow * (1.0, ga, sc)[o["kind"]] if q in ("pe", "dve", "act") else 1.0) for q, du in (o["alts"] or {o["eng"]: o["dur"]}).items()} for o in ops]
+            for slow, ga, sc, hop, late, norm in models]
+    succ = [[] for _ in range(n)]
+    for i, o in enumerate(ops):
+        for d in o["deps"]: succ[d].append(i)
+    tail = [i for i in range(n) if ops[i]["lat"] and not succ[i]]
+
+    def run(m, p0, old, p1):
+        fin, free, lk, co = list(old), {}, links[m], cost[m]
+        p = p0 - 1
+        while p >= 0 and len(free) < 4 and p > p0 - 400:
+            if at[order[p]] not in free and at[order[p]] != "net": free[at[order[p]]] = old[order[p]]
+            p -= 1
+        same, last = 0, None
+        for p in range(p0, n):
+            i = order[p]
+            q = at[i]
+            t = free.get(q, 0.0)
+            for d, lag in lk[i]:
+                if fin[d] + lag > t: t = fin[d] + lag
+            t += co[i][q]
+            fin[i] = t
+            if q != "net": free[q] = t
+            if p > p1:
+                if last is not None and abs(t - old[i] - last) < 1e-9: same += 1
+                else: same, last = 0, t - old[i]
+                if same > CFG["calm"]: return None, last
+        return fin, None
+
+    def span(fin):
+        return max(fin[i] + ops[i]["lat"] for i in tail)
+    fins = [run(m, 0, [0.0] * n, n)[0] for m in range(len(models))]
+    arcs = {}
+    for r in range(tries):
+        m = rng.randint(len(models))
+        if m not in arcs:
+            fin, pos, prev, free = fins[m], {i: p for p, i in enumerate(order)}, {}, {}
+            for i in order:
+                prev[i] = free.get(at[i])
+                if at[i] != "net": free[at[i]] = i
+            i, arcs[m] = max(tail, key=lambda i: fin[i] + ops[i]["lat"]), []
+            while i is not None:
+                t, a = fin[i] - cost[m][i][at[i]], prev[i]
+                by = [d for d, lag in links[m][i] if fin[d] + lag > t - 1e-9]
+                if by: i = by[0]
+                elif a is not None and fin[a] > t - 1e-9:
+                    arcs[m].append((pos[a], pos[i]))
+                    i = a
+                else: i = None
+        if not arcs[m]: continue
+        pa, pb = arcs[m][rng.randint(len(arcs[m]))]
+        a, b, how = order[pa], order[pb], rng.randint(5)
+        keep, was = order[:], None
+        if how == 0 or how == 1:
+            x = (a, b)[how]
+            if not ops[x]["alts"]: continue
+            was = (x, at[x])
+            at[x] = "act" if at[x] == "dve" else "dve"
+            p0, p1 = (pa, pb)[how], pb
+        elif how == 2:
+            lo = max([0] + [order.index(d, 0, pb) + 1 for d in ops[b]["deps"]])
+            p0 = max(lo, pa - rng.randint(2) * rng.randint(12))
+            if p0 > pa: continue
+            order.insert(p0, order.pop(pb))
+            p1 = pb
+        else:
+            hi = min([n] + [order.index(u, pa) for u in succ[a]])
+            p1 = min(hi - 1, pb + rng.randint(2) * rng.randint(25))
+            if p1 < pb: continue
+            order.insert(p1, order.pop(pa))
+            p0 = pa
+        gain, outs = 0.0, []
+        for k in range(len(models)):
+            fin, shift = run(k, p0, fins[k], p1)
+            gain += (shift if fin is None else span(fin) - span(fins[k])) * models[k][5]
+            if k == 1 and gain > 0.3: break
+        if gain < 1e-9 and (gain < -1e-9 or rng.rand() < CFG["side"]):
+            fins = [run(k, p0, fins[k], n)[0] for k in range(len(models))]
+            arcs = {}
+        else:
+            order = keep
+            if was: at[was[0]] = was[1]
+    CFG["span"].append(round(sum(span(f) * x[5] for f, x in zip(fins, models)) / len(models), 2))
+    return order, at
+
+
 def rank_program(g, core, T, topo):
     rank = T.rank_of(core)
     if rank is None:
         return
-    if "choice" not in PLAN: PLAN["choice"], PLAN["key"] = schedule(build(g, core, rank, T, topo, {})[0], CFG["r1"])[1:]
+    if "choice" not in PLAN:
+        ops = build(g, core, rank, T, topo, {})[0]
+        order, choice = schedule(ops, CFG["r1"])[:2]
+        order, at = polish(ops, order, [choice.get(i, o["eng"]) for i, o in enumerate(ops)], CFG["p1"])
+        PLAN["choice"], PLAN["first"] = {i: at[i] for i in choice}, order
     ops, used = build(g, core, rank, T, topo, PLAN["choice"])
-    if "order" not in PLAN: PLAN["order"] = schedule(ops, CFG["r2"], PLAN["key"])[0]
+    if "order" not in PLAN: PLAN["order"] = polish(ops, PLAN["first"], [o["eng"] for o in ops], CFG["p2"])[0]
     order = PLAN["order"]
 
     pos, cnt = {}, {}

import numpy as np
from concourse.mybir import AluOpType as ALU, AxisListType, ActivationFunctionType as AF

W, L, TS = 8192, 512, 4
KS = (3, 29)
NMAP = 8464
NX = W + NMAP
MID, UP = 4224.0 * 1024, 8448.0 * 1024
KB, KK = 65536.0, 16777216.0
RM0 = 12582912.0

SCRATCH = {
    "X": ("sbuf", [128, NX], "bfloat16"), "MAP": ("sbuf", [128, NMAP], "bfloat16"),
    "SD": ("sbuf", [128, 512], "bfloat16"), "V0": ("sbuf", [128, 32], "int32"), "THI": ("sbuf", [128, 4], "int32"),
    "ZS": ("sbuf", [128, 384], "bfloat16"), "ZL": ("sbuf", [128, 896], "bfloat16"),
    "NDS": ("sbuf", [128, 32], "bfloat16"), "NDL": ("sbuf", [128, 32], "bfloat16"),
    "MVS": ("sbuf", [128, 512], "bfloat16"), "MVL": ("sbuf", [128, 512], "bfloat16"),
    "NCS": ("sbuf", [128, 16], "float32"), "NCL": ("sbuf", [128, 16], "float32"),
    "MOS": ("sbuf", [128, 48], "uint16"), "MOL": ("sbuf", [128, 48], "uint16"),
    "G": ("sbuf", [128, 4096], "bfloat16"), "LO": ("sbuf", [128, 4096], "bfloat16"), "HI": ("sbuf", [128, 2048], "bfloat16"),
    "SGL": ("sbuf", [128, 64], "bfloat16"), "KEYR": ("sbuf", [128, 512], "float32"),
    "YT": ("sbuf", [128, 256], "float32"), "YS": ("sbuf", [128, 64], "float32"),
    "PF": ("sbuf", [128, 6300], "float32"), "PI": ("sbuf", [128, 2700], "int32"),
    "PU": ("sbuf", [128, 900], "uint16"), "PB": ("sbuf", [128, 20200], "bfloat16"),
    "GW1": ("sbuf", [128, 1024], "bfloat16"), "GW2": ("sbuf", [128, 1536], "bfloat16"), "GW3": ("sbuf", [128, 2048], "bfloat16"), "OFL": ("sbuf", [128, 384], "uint16"), "CRL": ("sbuf", [128, 384], "float32"),
    "PS": ("sbuf", [128, 192], "bfloat16"), "PL": ("sbuf", [128, 192], "bfloat16"),
}
NK = 17920
SCRATCH["KSD"] = ("sbuf", [128, NK], "float32")
PSUM = ("P0", "Q0", "P1", "Q1", "HP", "BD", "TA", "TB")
for _b in PSUM[:6]: SCRATCH[_b] = ("psum", [128, 512], "float32")
for _b in PSUM[6:]: SCRATCH[_b] = ("psum", [128, 1024], "bfloat16")
QUEUES = ("pe", "dve", "act", "gp")
SEMAPHORES = (["c_" + q for q in QUEUES] + ["ld_x", "ld_sd", "ld_v", "ld_th", "st_t", "st_s", "lsem"]
              + ["%s%d" % (k, t) for k in ("ro", "rm", "rz", "rb", "rf", "rc", "rp", "rg", "rx", "ry") for t in range(TS)])

CYC, PEC, HOP = 0.00088, 0.00045, 0.16
PLAN = {}
CFG = {"chains": ((0, 16, ((0, 8), (8, 16)), ((0, 8, "P0"), (8, 16, "Q0"))), (16, 32, ((0, 8), (8, 16)), ((0, 8, "P1"), (8, 16, "Q1")))),
       "uq": (0, 1, 2, 3, 4), "early": (), "zall": (0,), "cnt": ("HP", "BD"), "kcut": 4, "lcut": 4, "hat": 32, "tbank": "Q0", "tcut": ((0, 256),), "late": False, "far": ((), (), (), ()), "glat": 2.0,
       "batch": (((4, "n", 2), (4, "r", 1)), ((12, "o", 2), (4, "r", 1)), ((16, "o", 4), (8, "n", 2)), ((16, "o", 4), (16, "o", 2))),
       "ldx": 5.0, "net": 0.95, "iss": 0.45, "first": 2.5, "vcut": ((0, 16), (16, 32)),
       "ecut": (((0, 8),), ((0, 8),), ((0, 8),), ((0, 4), (4, 6), (6, 8))), "span": [],
       "banks": ("TA", "TB"), "turn": 2, "passes": 2, "r1": 40, "p1": 36000, "p2": 6000, "load": (0.0, -2.0, 1.0, -1.5, -1.0, 0.5), "calm": 120, "side": 0.5, "shake": 0.8, "near": 1.5, "lean": 0.05,
       "other": ((0.95, 1.0, 1.0, 0.18, -0.3, 1.0), (1.18, 0.77, 0.66, 0.12, 0.2, 1.0), (1.32, 1.2, 1.3, 0.15, -0.2, 0.8),
                 (1.32, 0.77, 0.47, 0.10, 0.3, 1.0), (1.09, 1.28, 0.6, 0.2, 0.8, 0.9))}


def dv(n, c=1.0):
    return max(64, n * c) * CYC


def ac(n):
    return 0.068 + n * CYC


def gat(n, eng="dve"):
    return (0.05 if eng == "dve" else 0.065) + 1.56 * n * CYC


def sca(n):
    return 0.05 + 3.8 * n * CYC


def build(g, core, rank, T, topo, choice):
    ops = []
    acc = {}
    pool = {"PF": [0], "PI": [0], "PU": [0], "PB": [0]}

    def op(eng, fn, reads, writes, dur, event=None, after=(), lat=0.0, alts=None):
        n = len(ops)
        deps = {}

        def need(m, wait):
            deps[m] = deps.get(m, False) or wait
        reads, writes = [rg(r) for r in reads], [rg(r) for r in writes]
        for r in reads:
            ex = r[0] in PSUM
            for (r2, m, wr) in acc.get(r[0], []):
                if ex: need(m, ops[m]["eng"] != eng or wr and meet(r, r2))
                elif wr and meet(r, r2): need(m, True)
        for r in writes:
            ex = r[0] in PSUM
            for (r2, m, wr) in acc.get(r[0], []):
                if ex: need(m, ops[m]["eng"] != eng)
                elif meet(r, r2): need(m, True)
        for m in after: need(m, False)
        ops.append({"eng": eng, "fn": fn, "deps": deps, "dur": dur, "event": event, "lat": lat, "alts": alts,
                    "kind": 0 if not any(r[0] in ("PU", "MOS", "MOL") for r in reads) or len(reads) < 2 else 2 if writes[0][2] - writes[0][1] > 1024 else 1})
        for r in reads:
            acc.setdefault(r[0], []).append((r, n, False))
        for r in writes:
            if r[0] in PSUM: keep = []
            else: keep = [a for a in acc.get(r[0], []) if not (a[0] == r or r[3] == 1 and r[1] <= a[0][1] and a[0][2] <= r[2])]
            acc[r[0]] = keep + [(r, n, True)]
        return n

    def meet(a, b):
        if a[1] >= b[2] or b[1] >= a[2]: return False
        if a[3] == b[3]: return (a[1] - b[1]) % a[3] == 0
        if a[3] < b[3]: a, b = b, a
        return any(b[1] <= x < b[2] and (x - b[1]) % b[3] == 0 for x in range(a[1], a[2], a[3]))

    def either(alts, reads, writes):
        n = len(ops)
        if n in choice: return op(choice[n], alts[choice[n]][0], reads, writes, alts[choice[n]][1])
        return op("open%d" % n, None, reads, writes, min(a[1] for a in alts.values()), alts={e: alts[e][1] for e in alts})

    def al(p, n):
        a = pool[p][0]
        pool[p][0] = a + (n + 15) // 16 * 16
        assert pool[p][0] <= SCRATCH[p][1][1], p
        return (p, a, a + n)

    def two(p, n):
        return (al(p, n), al(p, n))

    def ap(r):
        return T[r[0]][:, r[1]:r[2]] if len(r) == 3 else T[r[0]][:, r[1]:r[2]:r[3]]

    def rg(r):
        return r if len(r) == 4 else (r[0], r[1], r[2], 1)

    def sub(r, lo, hi, st=None):
        return (r[0], r[1] + lo, r[1] + hi) if st is None else (r[0], r[1] + lo, r[1] + hi, st)

    def wd(r):
        return r[2] - r[1] if len(r) == 3 else (r[2] - r[1] + r[3] - 1) // r[3]

    def fastc(*rs):
        return 0.5 if all(SCRATCH[r[0]][2] in ("bfloat16", "uint16") for r in rs) else 1.0

    def copy(o, i):
        op("dve", lambda: g.vector.tensor_copy(out=ap(o), in_=ap(i)), [rg(i)], [rg(o)], dv(wd(o), fastc(o, i)))

    def tt(o, a, b, f):
        c = 1.0 if (a[0] in PSUM or b[0] in PSUM) else 2.0
        op("dve", lambda: g.vector.tensor_tensor(out=ap(o), in0=ap(a), in1=ap(b), op=f), [rg(a), rg(b)], [rg(o)], dv(wd(o), c))

    def ts_call(o, a, s1, f1, s2=None, f2=None):
        def fn():
            x1 = ap(s1) if isinstance(s1, tuple) else s1
            x2 = ap(s2) if isinstance(s2, tuple) else s2
            if f2 is None:
                return g.vector.tensor_scalar(out=ap(o), in0=ap(a), scalar1=x1, scalar2=None, op0=f1)
            return g.vector.tensor_scalar(out=ap(o), in0=ap(a), scalar1=x1, scalar2=x2, op0=f1, op1=f2)
        return fn

    def ts(o, a, s1, f1, s2=None, f2=None):
        rd = [rg(a)] + [rg(s) for s in (s1, s2) if isinstance(s, tuple)]
        op("dve", ts_call(o, a, s1, f1, s2, f2), rd, [rg(o)], dv(wd(o), fastc(o, a)))

    def fill(o, v):
        op("dve", lambda: g.vector.memset(ap(o), v), [], [rg(o)], dv(wd(o), fastc(o)))

    def red(o, a, f, neg=False):
        op("dve", lambda: g.vector.tensor_reduce(out=ap(o), in_=ap(a), axis=AxisListType.X, op=f, negate=neg, apply_absolute_value=neg), [rg(a)], [rg(o)], dv(wd(a)))

    def scan(o, a, b, ini, f0, f1):
        op("dve", lambda: g.vector.tensor_tensor_scan(out=ap(o), data0=ap(a), data1=ap(b), initial=ap(ini) if isinstance(ini, tuple) else ini, op0=f0, op1=f1),
           [a, b] + [ini] * isinstance(ini, tuple), [o], dv(wd(o)))

    def ind(win, off):
        return T[win[0]][:, win[1]:win[2]].indirect(ap(off))

    def scatter(win, off, src):
        op("dve", lambda: g.vector.tensor_copy(out=ind(win, off), in_=ap(src)), [rg(off), rg(src)], [rg(win)], sca(wd(src)))

    def gather(eng, o, win, off):
        alts = {"act": (lambda: g.scalar.activation(out=ap(o), in_=ind(win, off), func=AF.Copy), gat(wd(o), "act")),
                "dve": (lambda: g.vector.tensor_copy(out=ap(o), in_=ind(win, off)), gat(wd(o)))}
        if eng: op(eng, alts[eng][0], [rg(win), rg(off)], [rg(o)], alts[eng][1])
        else: either(alts, [rg(win), rg(off)], [rg(o)])

    def gtt(o, win, off, b, f):
        op("dve", lambda: g.vector.tensor_tensor(out=ap(o), in0=ind(win, off), in1=ap(b), op=f), [win, off, b], [o], gat(wd(o)))

    def act_call(o, a, f, bias=None, scale=None, acc_o=None):
        def fn():
            kw = {}
            if bias is not None: kw["bias"] = ap(bias)
            if scale is not None: kw["scale"] = ap(scale) if isinstance(scale, tuple) else scale
            if acc_o is not None: kw["accum_out"] = ap(acc_o)
            return g.scalar.activation(out=ap(o), in_=ap(a), func=f, **kw)
        return fn

    def act(o, a, f, bias=None, scale=None, acc_o=None):
        rd = [rg(a)] + [rg(r) for r in (bias, scale) if isinstance(r, tuple)]
        op("act", act_call(o, a, f, bias, scale, acc_o), rd, [rg(o)] + ([rg(acc_o)] if acc_o is not None else []),
           ac(wd(o)) + (0.02 if acc_o is not None else 0.0))

    def move(o, a, relu=False, scale=None):
        if relu: d, s = ts_call(o, a, 0.0, ALU.max), act_call(o, a, AF.Relu)
        elif scale: d, s = ts_call(o, a, scale, ALU.mult), act_call(o, a, AF.Copy, scale=scale)
        else: d, s = (lambda: g.vector.tensor_copy(out=ap(o), in_=ap(a))), act_call(o, a, AF.Copy)
        either({"dve": (d, dv(wd(o), fastc(o, a))), "act": (s, ac(wd(o)))}, [rg(a)], [rg(o)])

    def times(o, a, col):
        either({"dve": (ts_call(o, a, col, ALU.mult), dv(wd(o), fastc(o, a))), "act": (act_call(o, a, AF.Copy, scale=col), ac(wd(o)))}, [a, col], [o])

    cols = {}

    def aff(o, a, s, b):
        if not isinstance(b, tuple) and b not in cols:
            cols[b] = al("PF", 1)
            fill(cols[b], b)
        col = b if isinstance(b, tuple) else cols[b]
        either({"dve": (ts_call(o, a, s, ALU.mult, b, ALU.add), dv(wd(o), fastc(o, a))), "act": (act_call(o, a, AF.Identity, col, s), ac(wd(o)))}, [a, col], [o])

    def mm(lst, f32=False):
        rd, wr = [], []
        d = 0.0
        for (o, a, b, s0, s1) in lst:
            for r in (a, b):
                if rg(r) not in rd: rd.append(rg(r))
            if rg(o) not in wr: wr.append(rg(o))
            d += max(min(64, wd(a)), wd(b)) * PEC * (4 if f32 else 1)

        def fn():
            x = None
            for (o, a, b, s0, s1) in lst: x = g.tensor.matmul(ap(o), ap(a), ap(b), s0, s1)
            return x
        op("pe", fn, rd, wr, d)

    def mms(lst, k):
        for j in range(0, len(lst), k): mm(lst[j:j + k])

    def iota(o, pat, base, cm):
        op("gp", lambda: g.iota(ap(o), pat, base, cm, allow_small_or_imprecise_dtypes=True), [], [rg(o)], 0.15 + 2 * wd(o) * CYC)

    def asel(o, a, pat, cmp, base, cm):
        op("gp", lambda: g.affine_select(ap(o), ap(a), pat, cmp, 0.0, base, cm), [rg(a)], [rg(o)], 0.2 + 2 * wd(o) * CYC)

    used = [0]

    def send(dst, o, i, sem):
        rid, pid, _ = topo.addr(dst)
        en = topo.engines(core, dst)
        if not CFG["zall"]: en = {"rm0": en[0::2], "ro0": en[0::2], "rz0": en[1::2]}.get(sem, en)
        m = sum(1 << e for e in en)
        used[0] += len(en)

        def fn():
            g.remote_dma(ap(o), ap(i), T.sem[sem], T.sem.lsem, pid, rid, m)
        s = op("gp", fn, [rg(i)], [], CFG["iss"] + ({"ry0": CFG["first"] + 1.5} if CFG["zall"] else {"rm0": CFG["first"], "rz0": 1.5}).get(sem, 0.0))
        op("net", None, [], [rg(o)], 0.0, event=(sem, len(en)), after=(s,), lat=CFG["net"] + CFG["glat"] * (sem[:2] == "rg"))

    def dma(o_ap, i_ap, rd, wr, sem, lat, eng="sp", after=()):
        return op(eng, lambda: (g.sync if eng == "sp" else g.scalar).dma_start(o_ap, i_ap).then_inc(T.sem[sem], 16), rd, wr, 0.1,
                  event=(sem, 16), lat=lat, after=after)

    V0, THI, SD, XW = ("V0", 0, 32), ("THI", 0, 4), ("SD", 0, 512), ("X", 0, W)
    dma(T.V0[:], T.v0[:], [], [V0], "ld_v", 2.0, "act")
    d0 = dma(T.SD[:, 0:512], T.sd[:], [], [SD], "ld_sd", 2.0)
    d1 = dma(T.X[:, 0:W], T.x[:], [], [XW], "ld_x", CFG["ldx"], after=(d0,))
    dma(T.THI[:], T.th[:], [], [THI], "ld_th", CFG["ldx"] + 0.5, after=(d1,))

    ONE, BO, t0, t8, ID, BO8, YW = al("PB", 128), al("PB", 128), al("PB", 128), al("PB", 8), al("PB", 128), al("PB", 8), al("PB", 144)
    fill(ONE, 1.0)
    fill(YW, 0.0)
    asel(t8, sub(ONE, 0, 8), [[-16, 8]], ALU.is_ge, 0, 1)
    asel(BO8, t8, [[16, 8]], ALU.is_ge, 15, -1)
    copy(sub(YW, 15, 143, 16), BO8)
    asel(ID, ONE, [[-1, 128]], ALU.is_equal, 0, 1)
    asel(t0, ONE, [[-16, 8], [0, 16]], ALU.is_ge, 0, 1)
    asel(BO, t0, [[16, 8], [0, 16]], ALU.is_ge, 15, -1)

    def sel(i):
        return sub(YW, 15 - i, 143 - i)

    def scaled(src, c, p="PB"):
        r = al(p, wd(src))
        move(r, src, scale=c)
        return r
    NID, NID16, IDH, ID2, N8F = scaled(ID, -1.0), scaled(ID, -8192.0), scaled(ID, -0.125), scaled(ID, -0.5), scaled(ONE, -8.0, "PF")
    IDG = [al("PB", 128) for _ in range(8)]
    for k in range(8): ts(IDG[k], ID, sub(BO8, k, k + 1), ALU.mult, -2.0 ** -10, ALU.mult)
    BIAS = (al("PF", 1), al("PF", 1))
    for m in range(2): fill(BIAS[m], 8.0 * KS[m])
    h1, h2, M16 = al("PF", 64), al("PF", 32), al("PF", 16)
    tt(h1, sub(ID, 0, 64), sub(ID, 64, 128), ALU.add)
    tt(h2, sub(h1, 0, 32), sub(h1, 32, 64), ALU.add)
    tt(M16, sub(h2, 0, 16), sub(h2, 16, 32), ALU.add)

    def m16(i):
        return sub(M16, i, i + 1)
    i16, x16, IC = al("PF", 16), al("PF", 16), al("PF", 1)
    iota(i16, [[1, 16]], 0, 0)
    tt(x16, M16, i16, ALU.mult)
    red(IC, x16, ALU.add)
    INI, iq, TL, C64, BASE, c32 = al("PF", 1), al("PF", 32), al("PF", 32), al("PB", 64), al("PB", 64), al("PF", 1)
    ts(INI, IC, 32.0, ALU.mult, 511.0, ALU.add)
    ts(c32, IC, 32.0, ALU.mult)
    iota(iq, [[1, 32]], 512 + 8192, 0)
    ts(TL, iq, c32, ALU.add)
    fill(sub(C64, 0, 32), 0.0)
    fill(sub(C64, 32, 64), 1.0)
    fill(BASE, 2.0 ** -11)
    V16 = al("PF", 64)

    def v16ops(dst, src):
        for q0, q1, _g, _d in CH:
            for m in range(2):
                o = sub(dst, 2 * q0 + m * (q1 - q0), q0 + q1 + m * (q1 - q0))
                if src[0] == "V0": ts(o, sub(src, q0, q1), 16.0, ALU.mult, -64.0 * KS[m] ** 2, ALU.add)
                else: aff(o, sub(src, q0, q1), 16.0, -64.0 * KS[m] ** 2)
    CH = CFG["chains"]
    v16ops(V16, V0)

    def sums(o, zr):
        mms([(o, sel(i), sub(zr, i, wd(zr), 16), i == 0, i == 15) for i in range(16)], 4)

    def lanes(o, zr, c0, c1, own, stop):
        mms([(sub(o, c // 16, 32, 2), sel(c % 16), sub(zr, 16 * c, 16 * c + 16), own and c % 16 == 0, own and c % 16 == 15 or stop and c == c1 - 1)
             for c in range(c0, c1)], 4)
    SQ0, SQ1 = al("PF", 64), al("PF", 64)
    sums(("P0", 0, 32), SD)
    for q0, q1, _g, _d in CH:
        for m in range(2): act(sub(SQ0, 2 * q0 + m * (q1 - q0), q0 + q1 + m * (q1 - q0)), ("P0", q0, q1), AF.Square, BIAS[m])
    ts(SQ1, SQ0, 65536.0, ALU.add)

    MAP, MAPW, MAP2, MAP2W = ("X", W, NX), ("X", W, 2 * W), ("MAP", 0, NMAP), ("MAP", 0, W)
    for k in range(16): fill(sub(MAP, k * 512, k * 512 + 512), 0.0)
    for k in range(16 * any(CFG["far"])): fill(sub(MAP2, k * 512, k * 512 + 512), 0.0)
    TH, TM0, fr0, f1, F12, FD = al("PF", 4), al("PF", 4), al("PF", 4), al("PB", 4), al("PF", 8), [al("PB", 128) for _ in range(4)]
    ts(TH, THI, 2.0, ALU.mult, -1.0, ALU.add)
    ts(TM0, THI, 0.5, ALU.is_gt, RM0, ALU.mult)
    op("dve", lambda: g.vector.reciprocal(out=ap(fr0), in_=ap(TH)), [TH], [fr0], 0.22)
    copy(f1, fr0)
    copy(sub(F12, 0, 4), f1)
    tt(sub(F12, 4, 8), fr0, f1, ALU.subtract)
    YK = scaled(YW, 1024.0)
    LT = al("PB", 128)
    asel(LT, BO, [[1, 128]], ALU.is_gt, 0, -1)
    LR, LW = al("PB", 512), al("PB", 128)
    ll = al("PB", 512)
    iota(LR, [[0, 16], [1, 32]], 0, 0)
    iota(ll, [[1, 16], [0, 32]], 0, 0)
    op("dve", lambda: g.vector.tensor_copy(out=T.PB[64:128, LR[1]:LR[2]], in_=T.PB[64:128, ll[1]:ll[2]]), [ll], [LR], dv(256))
    for p0, c in ((0, 2.0 ** -12), (64, 2.0 ** -16)):
        op("dve", lambda p0=p0, c=c: g.vector.memset(T.PB[p0:p0 + 64, LW[1]:LW[2]], c), [], [LW], dv(64))
    EI = [al("PB", 128) for _ in range(16)]
    for i in range(16): times(EI[i], BO, m16(i))
    IDQ = [scaled(ID, -2.0 ** (q + 2)) for q in range(8)]
    CM, cmc = [al("PB", 128) for _ in range(3)] + [BO], al("PF", 3)
    for k in range(3):
        ts(sub(cmc, k, k + 1), IC, 4.0 * k + 3.5, ALU.is_lt)
        times(CM[k], BO, sub(cmc, k, k + 1))
    RHE = al("PB", 64)
    times(sub(RHE, 0, 8), BO8, m16(0))
    for k in (8, 16, 32): move(sub(RHE, k, 2 * k), sub(RHE, 0, k))
    D0, dm2, OFC, EXC = al("PF", 128), al("PF", 16), al("PF", 1), al("PF", 1)
    ts(sub(D0, 0, 16), M16, -2.0 * UP * KB, ALU.mult)
    ts(sub(dm2, 0, 15), sub(M16, 0, 15), UP * KB, ALU.mult)
    tt(sub(D0, 1, 16), sub(D0, 1, 16), sub(dm2, 0, 15), ALU.add)
    for k in (16, 32, 64): move(sub(D0, k, 2 * k), sub(D0, 0, k))
    ts(OFC, m16(15), -UP * KB, ALU.mult, (UP + 256.0) * KB, ALU.add)
    ts(EXC, m16(15), -UP / 1024, ALU.mult, KK + (UP - MID) / 1024, ALU.add)
    pc, g8, CQ4 = al("PF", 1), al("PF", 1), al("PF", 1)
    iota(pc, [[0, 1]], 0, 1)
    tt(g8, pc, IC, ALU.subtract)
    ts(CQ4, g8, 0.25, ALU.mult, 129.6875, ALU.add)
    i8, TRW, SROW = al("PF", 8), al("PF", 8), al("PF", 128)
    iota(i8, [[16, 8]], W + 129, 0)
    ts(TRW, i8, IC, ALU.add, -KK, ALU.add)
    iota(SROW, [[1024, 128]], W * 1024 + 896, 0)
    CQ, C2, cq, SLH = al("PB", 128), al("PB", 128), al("PF", 128), al("PF", 128)
    iota(cq, [[-32, 8], [0, 16]], -23, 0)
    move(CQ, cq, scale=0.125)
    ts(SLH, SROW, 1.0 / 1024, ALU.mult, -W - 0.375, ALU.add)
    hot, neg = al("PF", 128), al("PF", 128)
    for q in range(8): move(sub(hot, q * 16, q * 16 + 16), M16, scale=2.0 ** (-q - 3))
    for w in range(2): times(sub(neg, w, 128, 2), sub(CQ, w, 128, 2), m16(1 - w))
    tt(C2, hot, neg, ALU.add)
    ROW = [[al("PB", 128), al("PB", 128)] for w in range(2)]
    for w in range(2):
        for k in range(2): times(ROW[w][k], (IDH, ID2)[k], m16(1 - w))
    KRP, KBZ, ZERO, ZW, B8F = al("PB", 400), al("PB", 384), al("PB", 128), al("PB", 240), al("PF", 8)
    fill(sub(KRP, 0, 16), 1.0)
    fill(KBZ, 0.0)
    fill(ZERO, 0.0)
    fill(ZW, 0.0)
    move(sub(ZW, 112, 128), M16)
    move(B8F, BO8)

    SQ, SI, C16, Y1, HB = two("PF", 64), two("PI", 64), two("PU", 64), two("PB", 512), two("PB", 512)
    ZH, ZF, GE = al("PB", 1536), al("PB", 512), al("PB", 512)
    CN, TM = two("PI", 256) + (al("PI", 256),), two("PF", 256)
    tda, NF, NBIG = al("PF", 256), two("PB", 32), scaled(ID, -16384.0)
    OFF, CR, crk = al("PU", 256), [al("PF", 64 * t + 64) for t in range(TS)], al("PF", 256)
    ZG, SQS, VSE, SIS, CS = al("PB", 512), al("PF", 64), al("PF", 64), al("PI", 64), al("PI", 64)
    AQ, SGN, SGP = al("PB", 128), al("PB", 512), al("PB", 512)
    LRF, lr1, lr2, lr3, LRU = two("PF", 32), al("PF", 32), al("PF", 32), al("PF", 32), two("PU", 32)
    LG, WS = al("PB", 512), two("PF", 64)
    WO = [sub(x, 32, 64) for x in WS]
    HAL, HTT, GO, FRA, FR, FQ = al("PB", 48), al("PF", 48), al("PB", 32), al("PB", 32), two("PB", 32), two("PB", 32)
    fill(HAL, 0.0)
    fill(HTT, 8192.0)
    HALT, HT = sub(HAL, 16, 48), sub(HTT, 16, 48)
    dht, SOFF = al("PF", 64), al("PU", 32)
    fill(sub(dht, 0, 32), 0.0)
    vm, vw, vq, vr = (al("PI", 32) for _ in range(4))
    VB = al("PF", 32)
    SV0, SIN = al("PF", 64), al("PI", 64)
    VB16, VN, VNs, VC = al("PF", 64), two("PI", 32), al("PI", 32), two("PI", 32)
    vd, vd2, VD, VDB = al("PF", 32), al("PF", 32), al("PI", 64), al("PB", 64)
    KJ, KM, KS2, MN, MO = al("PF", 128), al("PF", 128), al("PF", 128), al("PF", 8), al("PF", 8)
    KW = sub(KM, 15, 128, 16)
    AB = al("PF", 8 * 144)
    EXT = sub(AB, 0, 8 * 144, 144)
    OK, MOF, TP, TOFF = al("PB", 8), al("PF", 16), al("PF", 16), two("PU", 8)
    fill(MOF, 0.0)
    c8, c9, g9, dl0, DL = al("PF", 1), al("PF", 1), al("PF", 1), al("PF", 1), al("PU", 1)
    ts(c8, IC, 7.5, ALU.is_ge, -8.0, ALU.mult)
    tt(c9, c8, IC, ALU.add)
    ts(g9, g8, 0.5, ALU.mult)
    tt(dl0, g9, c9, ALU.add)
    copy(DL, dl0)
    ZI, ZJ, ZO = al("PI", 8), al("PI", 8), al("PU", 8)
    YQ, LV, VL, RM = al("PB", 256), al("PB", 512), al("PU", 32), al("PB", 256)
    SG, ACC, A16, DMS = al("PB", 64), al("PF", 1), al("PF", 1), al("PB", 8)
    hb1, hb2 = al("PI", 256), al("PI", 256)

    def vbase(v):
        ts(vm, v, 4095, ALU.bitwise_and)
        ts(vw, vm, 288.0, ALU.add)
        tt(vq, vm, vw, ALU.mult)
        ts(vr, vq, 3, ALU.arith_shift_right, 8191, ALU.bitwise_and)
        tt(VB, vr, v, ALU.add)
        v16ops(VB16, VB)
        tt(SV0, SQ1, VB16, ALU.add)

    def keys(v):
        ts(sub(VD, 0, 32), v, 8064, ALU.bitwise_and)
        ts(sub(VD, 32, 64), v, 127, ALU.bitwise_and)
        copy(VDB, VD)
        mm([(("BD", 0, 512), LW, LR, True, False)])
        mms([(("BD", 32 * i, 32 * i + 32), EI[i], sub(VDB, d * 32, d * 32 + 32), False, i == 15 and d == 1) for i in range(16) for d in range(2)], 4)
        n = 512 // CFG["kcut"]
        for h in range(0, 512, n): aff(("KEYR", h, h + n), ("BD", h % 256 * 2 + h // 256, h % 256 * 2 + 2 * n, 2), 1024.0 * KB, -(MID + 256.0) * KB)

    turns = [0]
    RHX = al("PB", 280)
    fill(RHX, 0.0)
    move(sub(RHX, 24, 32), sub(RHE, 0, 8))
    for k in (32, 64, 128): move(sub(RHX, 24 + k, 24 + 2 * k), sub(RHX, 24, 24 + k))
    MD, DF, dl8, DL8, IDF = al("PB", 128), al("PB", 144), al("PF", 8), al("PU", 8), scaled(ID, 1.0, "PF")
    move(sub(MD, 0, 16), M16)
    for k in (16, 32, 64): move(sub(MD, k, 2 * k), sub(MD, 0, k))
    fill(sub(DF, 128, 144), 0.0)
    ts(dl8, sub(i16, 0, 8), g9, ALU.add)
    copy(DL8, dl8)

    def tile(u):
        return ("G", u * 128, u * 128 + 128)
    NB8, FRC, RND = scaled(BO8, -1.0), al("PB", 64), al("PF", 1)
    fill(FRC, -0.3125)
    ts(RND, g8, 0.25, ALU.mult, RM0 + 2, ALU.add)
    NB64, RH64, CR4, cr4 = scaled(sub(BO, 0, 128, 2), -1.0), al("PB", 64), al("PB", 256), al("PB", 256)
    times(RH64, sub(BO, 0, 128, 2), m16(0))
    iota(cr4, [[0, 32], [-16, 8]], -1, 0)
    move(CR4, cr4, scale=0.25)

    def join(win, gb, u0, off, cr, batches, hp, start, stop, last):
        def tile(u):
            return (gb, u * 128, u * 128 + 128)
        for k, (nt, how, gs) in enumerate(batches):
            n = 64 if how == "r" else 8
            xs = ("Q%d" % (k % 2), 0, nt * n)
            if how == "n": mm([(xs, ID, sub(FRC, 0, nt * n), True, False), (xs, AQ, sub(RHE, 0, nt * n), False, False)])
            if how == "r":
                mm([(xs, ID, sub(CR4, 0, nt * n), True, False)])
                for u in range(u0, u0 + nt):
                    b = u % 4
                    mm([(sub(xs, (u - u0) * n, (u - u0) * n + n), sub(LG, b * 128, b * 128 + 128) if last else AQ, RH64, False, False)])
            for j0 in range(u0, u0 + nt, 2 * CFG["turn"]):
                bank = CFG["banks"][turns[0] % len(CFG["banks"])]
                turns[0] += 1
                je = min(u0 + nt, j0 + 2 * CFG["turn"])
                for u in range(j0, je):
                    if (u - u0) % gs == 0: gather(None, (gb, u * 128, min(u + gs, u0 + nt) * 128), win, sub(off, u * 8, min(u + gs, u0 + nt) * 8))
                    if gs > 1 and u % 2 == 0: continue
                    us = range(u - (gs > 1), u + 1)

                    def turn(us=us, bank=bank, j0=j0):
                        for w in us: x = g.tensor.transpose(T[bank][:, (w - j0) * 128:(w - j0) * 128 + 128], ap(tile(w)), ap(ID))
                        return x
                    op("pe", turn, [tile(w) for w in us] + [ID], [(bank, (us[0] - j0) * 128, (u + 1 - j0) * 128)], 128 * len(us) * PEC)
                    mm([(sub(xs, (w - u0) * n, (w - u0) * n + n), tile(w), {"o": BO8, "n": NB8, "r": NB64}[how], how == "o", how == "o" or w == u0 + nt - 1) for w in us])
                move(("LO", j0 * 128, je * 128), (bank, 0, (je - j0) * 128), relu=True)
            if how == "r": ts(("HI", u0 * 64, (u0 + nt) * 64), xs, RM0 - 50 if last else RND, ALU.add, RM0 + 2, ALU.is_equal)
            elif how == "n":
                for d in range(8): ts(("HI", u0 * 64 + d, (u0 + nt) * 64, 8), xs, RND, ALU.add, RM0 + 2 + 4 * d, ALU.is_equal)
            else:
                yq = sub(YQ, u0 * 8, (u0 + nt) * 8)
                tt(yq, sub(cr, u0 * 8, (u0 + nt) * 8), xs, ALU.subtract)
                for d in range(8): ts(("HI", u0 * 64 + d, (u0 + nt) * 64, 8), yq, 130.0 + 4 * d, ALU.is_equal)
            mms([(hp, ("LO", u * 128, u * 128 + 128), ("HI", u * 64, u * 64 + 64), start and not k and u == u0, stop and k == len(batches) - 1 and u == u0 + nt - 1)
                 for u in range(u0, u0 + nt)], 4)
            u0 += nt

    keys(V0)
    vbase(V0)

    for t in range(TS):
        pr, nx, last = t % 2, (t + 1) % 2, t == TS - 1
        partner = T.cores[rank ^ (1 + t % 7)]
        cn, fr, fq, vc = CN[t % 3], FR[pr], FQ[pr], VC[pr] if t else V0
        ksd = "KSD"
        if last: OFF = al("PU", 256)
        if t - 1 in CFG["zall"]: ZF = al("PB", 512)
        far = sum(x[0] for x in CFG["far"][t])
        ofl, crl = ("OFL", 128 * t - 128, 128 * t - 128 + 8 * far), ("CRL", 128 * t - 128, 128 * t - 128 + 8 * far)
        for b in range(4):
            p = b % 2
            zc = SD if b == 0 else sub(ZH, b * 512 - 512, b * 512)
            zn = sub(ZH, b * 512, b * 512 + 512) if b < 3 else ZF
            for q0, q1, gcut, dcut in CH:
                nq, k0, z0 = q1 - q0, 2 * q0, 16 * q0
                o = (dcut[0][2], 320, 320 + nq)
                if b:
                    sums(o, sub(zc, z0, 16 * q1))
                    for m in (1, 0): act(sub(SQ[p], k0 + m * nq, k0 + m * nq + nq), o, AF.Square, BIAS[m])
                c16 = sub(C16[p], k0, k0 + 2 * nq)
                for m0, m1 in ((nq, 2 * nq), (0, nq)):
                    si = sub(SIN if t and not b else SI[p], k0 + m0, k0 + m1)
                    if b or not t: tt(si, sub(SQ[p] if b else SQ0, k0 + m0, k0 + m1), sub(V16, k0 + m0, k0 + m1), ALU.add)
                    cc = sub(cn, 64 * b + 2 * m0 + q0, 64 * b + 2 * m0 + q1)
                    ts(cc, si, 4, ALU.arith_shift_right, 8191, ALU.bitwise_and)
                    copy(sub(c16, m0, m1), cc)
                for c0, c1 in gcut:
                    r0, r1 = z0 + c0 * 16, z0 + c1 * 16
                    gather("act", sub(Y1[p], r0, r1), XW, sub(c16, nq + c0, nq + c1))
                    gtt(sub(HB[p], r0, r1), XW, sub(c16, c0, c1), sub(Y1[p], r0, r1), ALU.max)
                for c0, c1, bank in dcut:
                    r0, r1 = z0 + c0 * 16, z0 + c1 * 16
                    dps = (bank, 0, r1 - r0)
                    if b < 3:
                        mm([(dps, NID, sub(zc, r0, r1), True, False)])
                        mm([(dps, ID, sub(HB[p], r0, r1), False, True)])
                        act(sub(zn, r0, r1), dps, AF.Abs)
                    else:
                        mm([(dps, FD[2], sub(zc, r0, r1), True, False), (dps, FD[3], sub(zc, r0, r1), False, False)])
                        mm([(dps, FD[0], sub(HB[p], r0, r1), False, False), (dps, FD[1], sub(HB[p], r0, r1), False, True)])
                        ts(sub(GE, r0, r1), dps, RM0, ALU.add, sub(TM0, t, t + 1), ALU.not_equal)
                        act(sub(zn, r0, r1), dps, AF.Abs, scale=sub(TH, t, t + 1))
                if b == 3 and t in CFG["zall"]: send(partner, ("ZL", 384 + z0, 384 + 16 * q1), sub(ZF, z0, 16 * q1), "rz%d" % t if q0 else "ry%d" % t)
            if b == 0:
                for k in range(4): times(FD[k], (ID, NID)[k // 2], sub(F12, 4 * (k % 2) + t, 4 * (k % 2) + t + 1))
        aff((ksd, 0, 128), SROW, KB, -(MID + 256.0) * KB)
        o, dl = (CFG["cnt"][0], 320, 352), (CFG["cnt"][1], 352, 416)
        if t: mm([(o, NID16, fq, True, False)])
        mms([(o, sub(YK, 15 - i, 143 - i), sub(GE, 32 * i, 32 * i + 32), not t and i == 0, i == 15) for i in range(16)], 4)
        ts(HALT, o, 8704.0, ALU.is_ge)
        tt(HT, o, TL, ALU.min)
        mm([(dl, ID, C64, True, False)])
        mm([(sub(dl, 0, 32), LT, HALT, False, False), (sub(dl, 32, 64), ID, sub(HALT, -1, 31), False, True)])
        tt(sub(dht, 32, 64), sub(HT, -1, 31), HT, ALU.subtract)
        scan(WS[pr], dht, dl, INI, ALU.add, ALU.add)
        copy(SOFF, WO[pr])
        scatter((ksd, 0, NK), SOFF, ("KEYR", 0, 512))
        ks = (ksd, 0, 128)
        aq, mq, early = ("P1", 0, 128), ("Q1", 0, 128), t in CFG["early"]
        ncs, ncl = ("NCS", 4 * t, 4 * t + 4), ("NCL", 4 * t, 4 * t + 4)
        mvs, mvl = ("MVS", t * 128, t * 128 + 128), ("MVL", t * 128, t * 128 + 128)
        mm([(("P0", 128 + 32 * k, 160 + 32 * k), CM[k], HALT, True, True) for k in range(4)])
        for k in range(4): act(sub(KJ, 32 * k, 32 * k + 32), ("P0", 128 + 32 * k, 160 + 32 * k), AF.Copy, scale=-1.0, acc_o=sub(ncs, k, k + 1))
        if early: send(partner, ncl, ncs, "rm%d" % t)
        if not last: mm([(aq, ID, CQ, True, False)])
        mm([(mq, ID, C2, True, False)])
        for k in range(4):
            own, sg = sub(SGN, k * 128, k * 128 + 128), sub(SGP if early else SGN, k * 128, k * 128 + 128)
            if not (last and early): act(own, SLH, AF.Sign, sub(ncs, k, k + 1))
            if not last: mm([(aq, ID2 if k == 3 else IDH, own, False, k == 3)])
            if early: act(sg, SLH, AF.Sign, sub(ncl, k, k + 1))
            mm([(sub(mq, w, 128, 2), ROW[w][k == 3], sub(sg, w, 128, 2), False, k == 3 and w == 1) for w in range(2)])
        act(mvl if early else mvs, mq, AF.Copy)
        if not early: send(partner, mvl, mvs, "rm%d" % t)
        if not last: move(AQ, aq)
        scan(KM, D0, ks, 0.0, ALU.add, ALU.max)
        act(KS2, ks, AF.Identity, OFC)
        aff(EXT, KW, -1.0 / (1024.0 * KB), EXC)
        for q in range(7, -1, -1):
            ab, kw = sub(AB, q * 144 + 1, q * 144 + 16 * q + 17), sub(KM, q * 16 + 15, q * 16 + 16)
            if q in CFG["uq"]: act(ab, sub(KS2, 0, 16 * q + 16), AF.Abs, kw, -1.0)
            else: ts(ab, sub(ks, 0, 16 * q + 16), kw, ALU.subtract, OFC, ALU.add)
            red(sub(MN, q, q + 1), sub(AB, q * 144, q * 144 + 16 * q + 17), ALU.min, True)
        tt(MO, MN, TRW, ALU.min)
        a = 32 if t in CFG["zall"] else 8 * t
        mos, mol = ("MOS", a, a + 8), ("MOL", a, a + 8)
        ts(mos, MO, KK, ALU.add)
        if t not in CFG["zall"]: send(partner, mol, mos, "ro%d" % t)
        ts(GO, WO[pr], 127.5, ALU.is_lt)
        if not last:
            aff(lr2, WO[pr], 1.0, 16.0 + 128.0 * t)
            tt(lr3 if t else LRF[pr], lr2, GO, ALU.mult)
            if t: tt(LRF[pr], LRF[nx], lr3, ALU.max)
            copy(LRU[pr], LRF[pr])
            ts(ZI, KW, 1.0 / KB, ALU.mult, 256.0, ALU.add)
            ts(ZJ, ZI, 511, ALU.bitwise_and)
            copy(ZO, ZJ)
            if t in CFG["zall"]:
                copy(("MOS", 40, 48), ZJ)
                send(partner, ("MOL", 32, 48), ("MOS", 32, 48), "ro%d" % t)
            for b in range(4): gather(None, sub(ZG, b * 128, b * 128 + 128), SD if b == 0 else sub(ZH, b * 512 - 512, b * 512), ZO)
            us = ("BD", 0, 32)
            sums(us, ZG)
            for m in range(2): act(sub(SQS, m * 32, m * 32 + 32), us, AF.Square, BIAS[m])
            aff(sub(VSE, 0, 8), EXT, -16.0, 16.0 * KK - 64.0 * KS[0] ** 2)
            move(sub(VSE, 8, 16), sub(VSE, 0, 8))
            move(sub(VSE, 16, 32), sub(VSE, 0, 16))
            aff(sub(VSE, 32, 64), sub(VSE, 0, 32), 1.0, 64.0 * (KS[0] ** 2 - KS[1] ** 2))
            tt(SIS, SQS, VSE, ALU.add)
            ts(CS, SIS, 4, ALU.arith_shift_right, 8191, ALU.bitwise_and)
            copy(sub(OFF, t * 64, t * 64 + 64), CS)
            mm([(("BD", 64, 128), AQ, RHE, True, True)])
            aff(sub(CR[t], t * 64, t * 64 + 64), ("BD", 64, 128), 1.0, CQ4)
            if t in CFG["zall"]: gather(None, ("ZL", t * 128, t * 128 + 128), ("ZL", 384, 896), ("MOL", 40, 48))
            else:
                gather(None, ("ZS", t * 128, t * 128 + 128), ZF, ZO)
                send(partner, ("ZL", t * 128, t * 128 + 128), ("ZS", t * 128, t * 128 + 128), "rz%d" % t)
        else:
            tt(FRA, fq, GO, ALU.add)
            mms([(("BD", 32 * i, 32 * i + 32), EI[i], FRA, True, True) for i in range(16)], 4)
            for k in range(4): move(sub(LG, k * 128, k * 128 + 128), ("BD", k * 128, k * 128 + 128), scale=50.0 - k / 4)
            mms([(("P0", 128, 384), sub(LG, k * 128, k * 128 + 128), sub(RHX, 24 - 8 * k, 280 - 8 * k), k == 0, k == 3) for k in range(4)], 1)
            aff(CR[t], ("P0", 128, 384), 1.0, 77.6875)
            if far: send(partner, crl, sub(CR[t], 0, 8 * far), "rc%d" % t)
            ts(VL, WO[pr], 128.0, ALU.min)
        def trails():
            tb, tm = CFG["tbank"], ("YT", 0, 256) if last else TM[pr]
            mms([((tb, 32 * e, 32 * e + 32), NBIG, fr, True, True) for e in range(8)], 4)
            mm([((tb, 256, 512), IDF, TM[nx], True, False)], f32=True)
            mms([((tb, 256 + 32 * e, 288 + 32 * e), NBIG, NF[pr], False, e == 7) for e in range(8)], 4)
            for c0, c1 in CFG["tcut"]:
                tt(sub(tda, c0, c1), (tb, c0, c1), sub(cn, c0, c1), ALU.add)
                tt(sub(tm, c0, c1), (tb, 256 + c0, 256 + c1), sub(tda, c0, c1), ALU.max)
                if last: copy(sub(OFF, c0, c1), sub(tm, c0, c1))
            if last:
                if far: send(partner, ofl, sub(OFF, 0, 8 * far), "rf%d" % t)
                dma(T.yt[:], T.YT[:], [tm], [], "st_t", 2.4)
        if last or t and not CFG["late"]: trails()
        if not t: copy(TM[0], cn)
        if far:
            ps, pl = ("PS", t * 64 - 64, t * 64), ("PL", t * 64 - 64, t * 64)
            scatter(MAP2, mos, mvs)
            join(MAP2W, "GW%d" % t, 0, ofl, crl, CFG["far"][t], ("P1", 0, 64), True, True, last)
            move(ps, ("P1", 0, 64))
            send(partner, pl, ps, "rp%d" % t)
            send(partner, ("G", 0, 128 * far), ("GW%d" % t, 0, 128 * far), "rg%d" % t)
            if not last: scatter(MAP2, mos, ZERO)
        scatter(MAP, mol, mvl)
        ts(OK, mol, W - 0.5, ALU.is_lt)
        if not last: ts(sub(MOF, 0, 8), mol, 1.0 / 4096, ALU.mult, 1.0, ALU.add)
        hp, ap16 = ("HP", 0, 64), ("P0", 0, 1)
        mm([(hp, ID, BASE, True, False)] + [(sub(hp, k * 8, k * 8 + 8), IDG[k], OK, False, False) for k in range(8)])
        join(MAPW, "G", far, OFF, CR[t], CFG["batch"][t], hp, False, not far, last)
        if far: mm([(hp, ID, pl, False, True)])
        act(SG, hp, AF.Sign, acc_o=ACC)
        mm([(ap16, N8F, ACC, True, True)], f32=True)
        if last: send(partner, ("SGL", 0, 64), SG, "rb%d" % t)
        else:
            gtt(TP, SG, DL, MOF, ALU.add)
            tp = sub(TP, 0, 8)
            for q0, q1, _g, _d in CH: ts(sub(SIN, 2 * q0, 2 * q1), sub(SV0, 2 * q0, 2 * q1), ap16, ALU.add)
            ts(TOFF[pr], tp, 4096.0, ALU.mult)
            scatter(("X", 0, NX), TOFF[pr], ("ZL", t * 128, t * 128 + 128))
        ts(A16, ap16, 65536.0, ALU.add)
        if not last:
            nds, ndl = ("NDS", t * 8, t * 8 + 8), ("NDL", t * 8, t * 8 + 8)
            ts(nds, tp, 2.0, ALU.is_ge)
            send(partner, ndl, nds, "rb%d" % t)
            aff(V16, VB16, 1.0, A16)
        vn = VN[pr]
        ts(VNs, VB, 16.0, ALU.mult, A16, ALU.add)
        ts(vn, VNs, 4, ALU.arith_shift_right, 8191, ALU.bitwise_and)
        if not last:
            keys(vn)
            scatter(MAP, mol, ZERO)
        w = 8 * t + 8
        mm([(("HP", 256, 264), IDQ[q], sub(SG, q, 64, 8), q == 0, q == 7) for q in range(8)])
        ts(DMS, ("HP", 256, 264), 1020.0, ALU.add)
        ecut, run = CFG["ecut"][t], None
        for k, (e0, e1) in enumerate(ecut):
            hq = (("HP", "Q1", "Q0", "BD")[k % 4] if last else "HP", 0, (e1 - e0) * w)
            if last: mms([(sub(hq, (e - e0) * w + b, (e - e0) * w + w, 4), tile(4 * e + b), DMS, True, True) for e in range(e0, e1) for b in range(4)], 4)
            else: mms([(sub(hq, (e - e0) * w + b * 8, (e - e0) * w + b * 8 + 8), tile(b * 8 + e), DMS, True, True) for e in range(e0, e1) for b in range(t + 1)], 4)
            ts(sub(hb1, e0 * w, e1 * w), hq, -0.5 + 2.0 ** -8, ALU.add)
            x, n = sub(hb2, e0 * w, e1 * w), e1 - e0
            ts(x, sub(hb1, e0 * w, e1 * w), 1, ALU.bitwise_and)
            while n > 1:
                n //= 2
                y = al("PI", n * w) if n > 1 or last else sub(KBZ, 0, 16 * w, 16)
                tt(y, sub(x, 0, n * w), sub(x, n * w, 2 * n * w), ALU.max)
                x = y
            if run:
                y = al("PB" if k == len(ecut) - 1 else "PI", w)
                tt(y, x, run, ALU.max)
                x = y
            run = x
        if last:
            fp, frn = ("P1", 0, 32), ("YS", 32, 64)
            mm([(fp, NID, fr, True, False)])

            def hurt(stop):
                for j in range(8): times(sub(RM, j, 256, 8), run, sub(B8F, j, j + 1))
                mm([(fp, sub(ZW, 112 - 16 * j, 240 - 16 * j), sub(RM, 32 * j, 32 * j + 32), False, stop and j == 7) for j in range(8)])
            gtt(sub(DF, 0, 128), ("SGL", 0, 64), DL8, MD, ALU.mult)
            for c0, c1 in CFG["vcut"]:
                if c0 == CFG["hat"]: hurt(False)
                gather(None, sub(LV, c0 * 16, c1 * 16), DF, sub(VL, c0, c1))
                lanes(fp, LV, c0, c1, False, CFG["hat"] < 32 and c1 == 32)
            if CFG["hat"] == 32: hurt(True)
            ts(frn, fp, -0.5, ALU.is_lt)
        else:
            for b in range(t + 1):
                kp = ("HP", b * 128, b * 128 + 128)
                mm([(kp, sub(KBZ, b * 128, b * 128 + 128), ID, True, False)] + [(kp, ID, sub(KRP, 16 + b * 128, 144 + b * 128), False, True)] * (b < t))
            mms([(sub(kp, i, 128, 16), EI[i], ndl, False, i == 15) for i in range(16)], 4)
            e = 128 * t + 128
            move(sub(KRP, 16, 16 + e), ("HP", 0, e))
            if t < TS - 2:
                mm([(("HP", 256 + b * 64, 320 + b * 64), sub(KRP, 16 + b * 128, 144 + b * 128), RHE, True, True) for b in range(t + 1)])
                aff(sub(crk, 0, e // 2), ("HP", 256, 256 + e // 2), -200.0, 200.0)
                tt(sub(CR[t + 1], 0, e // 2), sub(CR[t], 0, e // 2), sub(crk, 0, e // 2), ALU.min)
                n8, nxt = 8 * sum(x[0] for x in CFG["far"][t + 1]), T.cores[rank ^ (1 + (t + 1) % 7)]
                if n8:
                    send(nxt, ("OFL", 128 * t, 128 * t + n8), sub(OFF, 0, n8), "rf%d" % (t + 1))
                    send(nxt, ("CRL", 128 * t, 128 * t + n8), sub(CR[t + 1], 0, n8), "rc%d" % (t + 1))
            n = 32 // CFG["lcut"]
            for h in range(0, 32, n): gather(None, sub(LG, h * 16, h * 16 + n * 16), sub(KRP, 0, 16 + e), sub(LRU[pr], h, h + n))
            frn = FR[nx]
            sums(("HP", 32, 64), LG)
            lanes(("HP", 0, 32), LG, 0, 32, True, True)
            ts(FQ[nx], ("HP", 32, 64), 0.5, ALU.is_lt)
            ts(frn, ("HP", 0, 32), 0.5, ALU.is_lt)
            aff(NF[nx], frn, -1.0, 1.0)
            if t and CFG["late"]: trails()
        vcn = ("YS", 0, 32) if last else VC[nx]
        tt(vd, vc, vn, ALU.subtract)
        tt(vd2, vd, frn, ALU.mult)
        tt(vcn, vd2, vn, ALU.add)
        if not last: vbase(vcn)

    dma(T.ys[:], T.YS[:], [("YS", 0, 64)], [], "st_s", 2.4)
    return ops, used[0]


def place(ops, links, first, order):
    n = len(ops)
    busy, choice = {}, {}
    start, end = [0.0] * n, [0.0] * n
    for i in order:
        o = ops[i]
        at0 = first[i]
        for j, lag in links[i]:
            if end[j] + lag > at0: at0 = end[j] + lag
        best = None
        for q, du in o["ways"]:
            at, k = at0, 0
            if q != "net":
                sl = busy.setdefault(q, [])
                k, hi = 0, len(sl)
                while k < hi:
                    mid = (k + hi) // 2
                    if sl[mid][1] > at: hi = mid
                    else: k = mid + 1
                while k < len(sl) and sl[k][0] < at + du - 1e-9:
                    at = max(at, sl[k][1])
                    k += 1
            if best is None or at + du < best[0] + best[1] - CFG["lean"]: best = (at, du, q, k)
        at, du, q, k = best
        o["at"] = q
        if q != "net": busy[q].insert(k, (at, at + du))
        if o["alts"]: choice[i] = q
        start[i], end[i] = at, at + du
    return start, end, choice


def replay(ops, order, start, end, slow, ga, sc, hop, late, norm):
    free, fin = {}, [0.0] * len(ops)
    for i in order:
        o = ops[i]
        q = o["at"]
        at = free.get(q, 0.0)
        for d, w in o["deps"].items():
            e = fin[d] + (ops[d]["lat"] + hop + (late if ops[d]["at"] == "net" else 0.0) if w else 0.0)
            if e > at: at = e
        fin[i] = at + (end[i] - start[i]) * (slow * (1.0, ga, sc)[o["kind"]] if q in ("pe", "dve", "act") else 1.0)
        if q != "net": free[q] = fin[i]
    return max(fin[i] + ops[i]["lat"] for i in order) * norm


def schedule(ops, rounds, key=None):
    n = len(ops)
    for o in ops: o["ways"] = sorted((o["alts"] or {o["eng"]: o["dur"]}).items())
    fwd = [[(d, ops[d]["lat"] + HOP if w else 0.0) for d, w in o["deps"].items()] for o in ops]
    bwd = [[] for _ in range(n)]
    for i in range(n):
        for d, lag in fwd[i]: bwd[d].append((i, lag))
    if key is None:
        key = [0.0] * n
        for i in range(n - 1, -1, -1):
            key[i] = min([key[u] - lag for u, lag in bwd[i]] + [-ops[i]["lat"]]) - ops[i]["dur"]
    zero, lat = [0.0] * n, [o["lat"] for o in ops]
    rng = np.random.RandomState(1)
    best = None
    for r in range(rounds):
        if r:
            near = np.abs(np.array(best[1]) - rng.uniform(10.0, best[0])) < CFG["near"]
            key = [float(x) for x in np.array(best[3]) + rng.uniform(-CFG["shake"], CFG["shake"], n) * near]
        key = list(key)
        for i in range(n):
            for d, lag in fwd[i]:
                if key[d] > key[i]: key[i] = key[d]
        for _ in range(CFG["passes"] if r else 6):
            start, end, choice = place(ops, fwd, zero, sorted(range(n), key=lambda i: (key[i], i)))
            span = max(end[i] + lat[i] for i in range(n))
            if best is None or span < best[0] + 1.0:
                order = sorted(range(n), key=lambda i: (start[i], i))
                span = (span + sum(replay(ops, order, start, end, *m) for m in CFG["other"])) / (1 + len(CFG["other"]))
                if best is None or span <= best[0] + 1e-6: best = (span, start, choice, key)
            if _ == CFG["passes"] - 1 and r: break
            back, bend, _c = place(ops, bwd, lat, sorted(range(n), key=lambda i: (-end[i], -i)))
            key = [-x for x in bend]
    CFG["span"].append(round(best[0], 1))
    start = best[1]
    return sorted(range(n), key=lambda i: (start[i], i)), best[2], best[3]


def polish(ops, order, at, tries):
    n, models = len(ops), ((1.0, 1.0, 1.0, HOP, 0.0, 1.0),) + CFG["other"]
    order, at = list(order), list(at)
    rng = np.random.RandomState(2)
    links = [[[(d, ops[d]["lat"] + hop + (late if ops[d]["eng"] == "net" else load * (ops[d]["eng"] == "sp" and ops[d]["lat"] > 4)) if w else 0.0)
               for d, w in o["deps"].items()] for o in ops] for (slow, ga, sc, hop, late, norm), load in zip(models, CFG["load"])]
    cost = [[{q: du * (slow * (1.0, ga, sc)[o["kind"]] if q in ("pe", "dve", "act") else 1.0) for q, du in (o["alts"] or {o["eng"]: o["dur"]}).items()} for o in ops]
            for slow, ga, sc, hop, late, norm in models]
    succ = [[] for _ in range(n)]
    for i, o in enumerate(ops):
        for d in o["deps"]: succ[d].append(i)
    tail = [i for i in range(n) if ops[i]["lat"] and not succ[i]]

    def run(m, p0, old, p1):
        fin, free, lk, co = list(old), {}, links[m], cost[m]
        p = p0 - 1
        while p >= 0 and len(free) < 4 and p > p0 - 400:
            if at[order[p]] not in free and at[order[p]] != "net": free[at[order[p]]] = old[order[p]]
            p -= 1
        same, last = 0, None
        for p in range(p0, n):
            i = order[p]
            q = at[i]
            t = free.get(q, 0.0)
            for d, lag in lk[i]:
                if fin[d] + lag > t: t = fin[d] + lag
            t += co[i][q]
            fin[i] = t
            if q != "net": free[q] = t
            if p > p1:
                if last is not None and abs(t - old[i] - last) < 1e-9: same += 1
                else: same, last = 0, t - old[i]
                if same > CFG["calm"]: return None, last
        return fin, None

    def span(fin):
        return max(fin[i] + ops[i]["lat"] for i in tail)
    fins = [run(m, 0, [0.0] * n, n)[0] for m in range(len(models))]
    arcs = {}
    for r in range(tries):
        m = rng.randint(len(models))
        if m not in arcs:
            fin, pos, prev, free = fins[m], {i: p for p, i in enumerate(order)}, {}, {}
            for i in order:
                prev[i] = free.get(at[i])
                if at[i] != "net": free[at[i]] = i
            i, arcs[m] = max(tail, key=lambda i: fin[i] + ops[i]["lat"]), []
            while i is not None:
                t, a = fin[i] - cost[m][i][at[i]], prev[i]
                by = [d for d, lag in links[m][i] if fin[d] + lag > t - 1e-9]
                if by: i = by[0]
                elif a is not None and fin[a] > t - 1e-9:
                    arcs[m].append((pos[a], pos[i]))
                    i = a
                else: i = None
        if not arcs[m]: continue
        pa, pb = arcs[m][rng.randint(len(arcs[m]))]
        a, b, how = order[pa], order[pb], rng.randint(5)
        keep, was = order[:], None
        if how == 0 or how == 1:
            x = (a, b)[how]
            if not ops[x]["alts"]: continue
            was = (x, at[x])
            at[x] = "act" if at[x] == "dve" else "dve"
            p0, p1 = (pa, pb)[how], pb
        elif how == 2:
            lo = max([0] + [order.index(d, 0, pb) + 1 for d in ops[b]["deps"]])
            p0 = max(lo, pa - rng.randint(2) * rng.randint(12))
            if p0 > pa: continue
            order.insert(p0, order.pop(pb))
            p1 = pb
        else:
            hi = min([n] + [order.index(u, pa) for u in succ[a]])
            p1 = min(hi - 1, pb + rng.randint(2) * rng.randint(25))
            if p1 < pb: continue
            order.insert(p1, order.pop(pa))
            p0 = pa
        gain, outs = 0.0, []
        for k in range(len(models)):
            fin, shift = run(k, p0, fins[k], p1)
            gain += (shift if fin is None else span(fin) - span(fins[k])) * models[k][5]
            if k == 1 and gain > 0.3: break
        if gain < 1e-9 and (gain < -1e-9 or rng.rand() < CFG["side"]):
            fins = [run(k, p0, fins[k], n)[0] for k in range(len(models))]
            arcs = {}
        else:
            order = keep
            if was: at[was[0]] = was[1]
    CFG["span"].append(round(sum(span(f) * x[5] for f, x in zip(fins, models)) / len(models), 2))
    return order, at


def rank_program(g, core, T, topo):
    rank = T.rank_of(core)
    if rank is None:
        return
    if "choice" not in PLAN:
        ops = build(g, core, rank, T, topo, {})[0]
        order, choice = schedule(ops, CFG["r1"])[:2]
        order, at = polish(ops, order, [choice.get(i, o["eng"]) for i, o in enumerate(ops)], CFG["p1"])
        PLAN["choice"], PLAN["first"] = {i: at[i] for i in choice}, order
    ops, used = build(g, core, rank, T, topo, PLAN["choice"])
    if "order" not in PLAN: PLAN["order"] = polish(ops, PLAN["first"], [o["eng"] for o in ops], CFG["p2"])[0]
    order = PLAN["order"]

    pos, cnt = {}, {}
    for i in order:
        q = ops[i]["eng"]
        cnt[q] = cnt.get(q, 0) + 1
        pos[i] = cnt[q]
    known, vcs, waits, needed, final = {}, {}, {}, set(), {}
    for i in order:
        o = ops[i]
        q = o["eng"]
        final[q] = i
        if q == "net":
            vcs[i] = {("ev", i): 1}
            continue
        kn = known.setdefault(q, {})
        mine = []
        for d in sorted((d for d, w in o["deps"].items() if w), key=lambda d: -pos[d]):
            key, val = (("ev", d), 1) if ops[d]["event"] else (ops[d]["eng"], pos[d])
            if kn.get(key, 0) >= val: continue
            mine.append(d)
            needed.add(d)
            for k2, x2 in vcs[d].items():
                if kn.get(k2, 0) < x2: kn[k2] = x2
        waits[i] = mine
        v = dict(kn)
        v[("ev", i) if o["event"] else q] = 1 if o["event"] else pos[i]
        vcs[i] = v
    for q in ("pe", "dve", "act"): needed.add(final[q])

    eng = {"pe": g.tensor, "dve": g.vector, "act": g.scalar, "gp": g, "sp": g.sync}
    num, tot = {}, {}
    for i in order:
        q = ops[i]["eng"]
        if i in needed and not ops[i]["event"]:
            tot[q] = tot.get(q, 0) + 1
            num[i] = tot[q]
    for i in order:
        o = ops[i]
        q = o["eng"]
        if q == "net": continue
        best = {}
        for d in waits[i]:
            s, v = ops[d]["event"] if ops[d]["event"] else ("c_" + ops[d]["eng"], num[d])
            best[s] = max(best.get(s, 0), v)
        for s in best: eng[q].wait_ge(T.sem[s], best[s])
        x = o["fn"]()
        if i in num: x.then_inc(T.sem["c_" + q], 1)
    for q in tot: g.sync.wait_ge(T.sem["c_" + q], tot[q])
    g.sync.wait_ge(T.sem.lsem, used)
    for s in ("st_t", "st_s"): g.sync.wait_ge(T.sem[s], 16)
